import numpy as np
import ml_dtypes


def mxq(x, axis, fmt="e4m3"):
    dtype, down = {"e4m3": (ml_dtypes.float8_e4m3fn, 7), "e5m2": (ml_dtypes.float8_e5m2, 14)}[fmt]
    v = np.moveaxis(np.asarray(x, np.float32).astype(ml_dtypes.bfloat16).astype(np.float64), axis, -1)
    blocks = v.reshape(v.shape[:-1] + (-1, 32))
    amax = np.abs(blocks).max(-1, keepdims=True)
    byte = np.maximum(np.where(amax > 0, np.frexp(amax)[1] - 1 + 127, 0) - down, 1)
    scale = np.exp2(byte - 127.0)
    codes = (blocks / scale).astype(np.float32).astype(dtype).astype(np.float64)
    return np.moveaxis((codes * scale).reshape(v.shape), -1, axis)


WIDE = False


def mx_kscale(k, group=512):
    if not WIDE:
        return np.ones(k)
    levels = np.array([10, -10, 5, -5, 0])
    if group != 512:
        return np.exp2(np.random.permutation(np.resize(levels, k // group))).repeat(group)
    if k % 512:
        return np.exp2(np.random.permutation(np.resize(levels, k // 32))).repeat(32)
    a = np.empty((k // 512, 16))
    for p in range(k // 512):
        a[p, :8] = np.random.permutation(np.resize(levels, 8))
        for g in range(8):
            far = levels[np.abs(levels - a[p, g]) >= 10]
            a[p, g + 8] = far[np.random.randint(len(far))]
    return np.exp2(a.ravel()).repeat(32)


def f64(x):
    return np.asarray(x).astype(np.float64)


def striped(idx):
    return np.tile(np.asarray(idx).reshape(-1, 16).T, (8, 1)).astype(np.uint16)


def unstriped(offs):
    return offs[:16].T.reshape(-1).astype(np.int64)


H, KV, D, NQ, N = 2, 2, 256, 512, 512


def setup_inputs():
    n = np.random.standard_normal
    s = mx_kscale(D, 0)[:, None]
    u = mx_kscale(N)
    t = np.random.uniform(0.5, 2.0, N) * u
    v = n((KV, N, 128))
    return {
        "qT": (n((H, D, NQ)) * s * (0.70 / np.sqrt(D))).astype(np.float32),
        "kT": (n((KV, D, N)) / s).astype(np.float32),
        "t": t.reshape(N, 1).astype(np.float32),
        "v": (v / t[:, None]).astype(np.float32),
        "mask": (np.arange(N)[:, None] <= np.sort(np.random.randint(N // 4, N, NQ))[None, :]).astype(np.float32),
        "gn": np.tile(np.random.uniform(0.5, 2.0, 128), (128, 1)).astype(np.float32),
        "og": n((H, NQ, 128)).astype(np.float32),
    }


def reference(qT, kT, t, v, mask, gn, og):
    a = mxq(f64(kT), 1, "e4m3").transpose(0, 2, 1) @ mxq(f64(qT), 1, "e4m3")
    p = np.tanh(a)
    p = p * f64(mask)
    w = p * f64(t)
    y = mxq(w, 1, "e4m3").transpose(0, 2, 1) @ mxq(f64(v), 1, "e4m3")
    y = y / 16.0
    y = y / np.sqrt(np.mean(np.square(y), -1, keepdims=True) + 1e-5) * f64(gn)[:1]
    y = y / (1.0 + np.exp(-f64(og)))
    return y

@@ -1,0 +1,302 @@
+from contextlib import ExitStack
+
+import concourse.mybir as mybir
+
+F32 = mybir.dt.float32
+BF16 = mybir.dt.bfloat16
+U32 = mybir.dt.uint32
+U8 = mybir.dt.uint8
+FP8X4 = mybir.dt.float8_e4m3fn_x4
+ACT = mybir.ActivationFunctionType
+ALU = mybir.AluOpType
+
+H, D, NQ, N, E = 2, 256, 512, 512, 128
+P = 128
+PACK = 4
+ROWS = D // PACK
+QT = 128
+TILES = NQ // QT
+UNITS = TILES * H
+FLOPS = 2 * H * N * NQ * D + 2 * H * NQ * N * E
+
+
+def tile_rows_a_tanh_mask_onorm_gate_kernel(tc, qT, kT, t, v, mask, gn, og, out):
+    nc = tc.nc
+    with ExitStack() as ctx:
+        sb = ctx.enter_context(tc.tile_pool(name="sb", bufs=1))
+        ps = ctx.enter_context(tc.psum_pool(name="ps", bufs=1))
+        ctx.enter_context(tc.manual_schedule())
+
+        def tiles(name, count, shape, dtype, pool=sb, **kw):
+            return [pool.tile(shape, dtype, name=name + str(i), **kw) for i in range(count)]
+
+        qv = qT.rearrange("h (p j) c -> (h p) j c", j=PACK)
+        kv = kT.rearrange("h (p j) c -> (h p) j c", j=PACK)
+        mv = mask.rearrange("(s r) c -> s r c", r=PACK)
+        vv = v.rearrange("h (s r) e -> s h (r e)", r=PACK)
+        ogv = og.rearrange("h (n p) e -> n p h e", p=QT)
+        outv = out.rearrange("h (n p) e -> n p h e", p=QT)
+
+        QCH = [[0,1],[1,2],[2,4]]
+        MCH = [[0,1],[1,2],[2,4]]
+        k_raw = tiles("k_raw", 2, [P, PACK, N // 2], F32)
+        k_bf = tiles("k_bf", 2, [P, PACK, N // 2], BF16, align_bytes=64)
+        k_codes = sb.tile([P, N], U32, name="k_codes", align_bytes=64)
+        k_scales = sb.tile([P, N], U8, name="k_scales", align_bytes=64)
+        q_raw = [sb.tile([P, PACK, (b - a) * QT], F32, name="q_raw" + str(a)) for a, b in QCH]
+        q_bf = tiles("q_bf", TILES, [P, QT * PACK], BF16, align_bytes=64)
+        q_codes = tiles("q_codes", TILES, [P, QT], U32, align_bytes=64)
+        q_scales = tiles("q_scales", TILES, [P, QT], U8, align_bytes=64)
+        m_raw = [sb.tile([P, PACK, (b - a) * QT], F32, name="m_raw" + str(a)) for a, b in MCH]
+        mt = [sb.tile([P, PACK, (b - a) * QT], F32, name="mt" + str(a)) for a, b in MCH]
+        v_raw = sb.tile([P, H, PACK * E], F32, name="v_raw")
+        v_bf = sb.tile([P, H, PACK * E], BF16, name="v_bf", align_bytes=64)
+        v_codes = sb.tile([P, H * E], U32, name="v_codes", align_bytes=64)
+        v_scales = sb.tile([P, H * E], U8, name="v_scales", align_bytes=64)
+        t_sb = sb.tile([P, PACK], F32, name="t_sb")
+        gn_sb = sb.tile([P, E], F32, name="gn_sb")
+        og_sb = tiles("og_sb", TILES, [P, H, E], F32)
+        th = tiles("th", TILES, [P, H, E], F32)
+        gate = tiles("gate", TILES, [P, H, E], F32)
+        p = tiles("p", UNITS, [P, PACK * QT], F32)
+        w_bf = tiles("w_bf", UNITS, [P, QT * PACK], BF16, align_bytes=64)
+        w_codes = tiles("w_codes", UNITS, [P, QT], U32, align_bytes=64)
+        w_scales = tiles("w_scales", UNITS, [P, QT], U8, align_bytes=64)
+        sq_junk = tiles("sq_junk", UNITS, [P, E], BF16)
+        ss = sb.tile([P, UNITS], F32, name="ss")
+        rms = sb.tile([P, UNITS], F32, name="rms")
+        rstd = sb.tile([P, UNITS], F32, name="rstd")
+        warm2 = sb.tile([P, 1], F32, name="warm2")
+        res = tiles("res", TILES, [P, H, E], F32)
+        one = sb.tile([P, 1], F32, name="one")
+        warm = sb.tile([P, 1], F32, name="warm")
+        sc = tiles("sc", 2 * H, [P, PACK * QT], F32, pool=ps)
+        ybank = tiles("ybank", 4, [P, 512], F32, pool=ps)
+
+        def chunk(chs, n):
+            for i, (a, b) in enumerate(chs):
+                if a <= n < b:
+                    return i, (n - a) * QT
+            raise ValueError(n)
+
+        def cast(eng, dst, src):
+            if eng == "v":
+                nc.vector.tensor_copy(out=dst, in_=src)
+            else:
+                nc.scalar.copy(out=dst, in_=src)
+
+        def ld_k(a):
+            nc.sync.dma_start(out=k_raw[a][:], in_=kv[:, :, a * 256:(a + 1) * 256])
+
+        def ld_q(i):
+            a, b = QCH[i]
+            nc.sync.dma_start(out=q_raw[i][:], in_=qv[:, :, a * QT:b * QT])
+
+        def ld_m(i):
+            a, b = MCH[i]
+            nc.sync.dma_start(out=m_raw[i][:], in_=mv[:, :, a * QT:b * QT])
+
+        def ld_v():
+            nc.sync.dma_start(out=v_raw[:], in_=vv)
+
+        def ld_og(n):
+            nc.sync.dma_start(out=og_sb[n][:], in_=ogv[n])
+
+        def ld_small():
+            nc.sync.dma_start(out=t_sb[:], in_=t.rearrange("(s r) o -> s (r o)", r=PACK))
+            nc.sync.dma_start(out=gn_sb[:], in_=gn)
+
+        def init():
+            nc.vector.memset(one[:], 1.0)
+            nc.scalar.activation(out=warm[:], in_=one[:], func=ACT.Tanh)
+
+        def cast_k(a, eng, s0=0, s1=64):
+            cast(eng, k_bf[a][:].rearrange("p r (s j) -> p s j r", j=PACK)[:, s0:s1],
+                 k_raw[a][:].rearrange("p j (s r) -> p s j r", r=PACK)[:, s0:s1])
+
+        def quant_k(a, r):
+            cols = slice(r * QT + a * 64, r * QT + (a + 1) * 64)
+            nc.vector.quantize_mx(out=k_codes[:, cols].bitcast(FP8X4), scales=k_scales[:, cols], in_=k_bf[a][:, r, :])
+
+        def cast_q(n, eng):
+            i, c0 = chunk(QCH, n)
+            cast(eng, q_bf[n][:].rearrange("p (c i j) -> p c j i", i=2, j=PACK),
+                 q_raw[i][:, :, c0:c0 + QT].rearrange("p j (c i) -> p c j i", i=2))
+
+        def quant_q(n):
+            nc.vector.quantize_mx(out=q_codes[n][:].bitcast(FP8X4), scales=q_scales[n][:], in_=q_bf[n][:])
+
+        def cast_v(h, eng):
+            cast(eng, v_bf[:, h, :].rearrange("p (c i j) -> p c j i", i=2, j=PACK),
+                 v_raw[:, h, :].rearrange("p (j c i) -> p c j i", i=2, j=PACK))
+
+        def quant_v(h):
+            cols = slice(h * E, (h + 1) * E)
+            nc.vector.quantize_mx(out=v_codes[:, cols].bitcast(FP8X4), scales=v_scales[:, cols], in_=v_bf[:, h, :])
+
+        def make_mt(i, eng):
+            for r in range(PACK):
+                if eng == "v":
+                    nc.vector.tensor_scalar(out=mt[i][:, r, :], in0=m_raw[i][:, r, :], scalar1=t_sb[:, r:r + 1], scalar2=None, op0=ALU.mult)
+                else:
+                    nc.scalar.activation(out=mt[i][:, r, :], in_=m_raw[i][:, r, :], func=ACT.Copy, scale=t_sb[:, r:r + 1])
+
+        def scores(u):
+            n, h = divmod(u, H)
+            rows = slice(h * ROWS, (h + 1) * ROWS)
+            for r in range(PACK):
+                cols = slice(r * QT, (r + 1) * QT)
+                nc.tensor.matmul_mx(
+                    out=sc[2 * h + n % 2][:, cols],
+                    lhsT=k_codes[rows, cols].bitcast(FP8X4), lhsT_scale=k_scales[rows, cols],
+                    rhs=q_codes[n][rows, :].bitcast(FP8X4), rhs_scale=q_scales[n][rows, :],
+                    start=True, stop=True)
+
+        def tanh(u):
+            n, h = divmod(u, H)
+            nc.scalar.activation(out=p[u][:], in_=sc[2 * h + n % 2][:], func=ACT.Tanh)
+
+        def weigh(u):
+            i, c0 = chunk(MCH, u // H)
+            nc.vector.tensor_tensor(
+                out=w_bf[u][:].rearrange("p (c i r) -> p c r i", i=2, r=PACK),
+                in0=p[u][:].rearrange("p (r c i) -> p c r i", i=2, r=PACK),
+                in1=mt[i][:, :, c0:c0 + QT].rearrange("p r (c i) -> p c r i", i=2),
+                op=ALU.mult)
+
+        def quant_w(u):
+            nc.vector.quantize_mx(out=w_codes[u][:].bitcast(FP8X4), scales=w_scales[u][:], in_=w_bf[u][:])
+
+        def y_of(u):
+            return ybank[u % 4][:, (u // 4) * E:(u // 4 + 1) * E]
+
+        def pv(u):
+            cols = slice((u % H) * E, (u % H + 1) * E)
+            nc.tensor.matmul_mx(out=y_of(u), lhsT=w_codes[u][:].bitcast(FP8X4), lhsT_scale=w_scales[u][:],
+                                rhs=v_codes[:, cols].bitcast(FP8X4), rhs_scale=v_scales[:, cols], start=True, stop=True)
+
+        def square(u):
+            nc.scalar.activation(out=sq_junk[u][:], in_=y_of(u), func=ACT.Square, accum_out=ss[:, u:u + 1])
+
+        def switch():
+            nc.scalar.activation(out=warm2[:], in_=one[:], func=ACT.Sqrt)
+
+        def root(a, b):
+            nc.scalar.activation(out=rms[:, a:b], in_=ss[:, a:b], func=ACT.Sqrt, scale=4.0 / E, bias=4.0 * 256.0 * 1e-5)
+
+        def recip(a, b):
+            nc.vector.reciprocal(out=rstd[:, a:b], in_=rms[:, a:b])
+
+        def gate_tanh(n):
+            nc.scalar.activation(out=th[n][:], in_=og_sb[n][:], func=ACT.Tanh, scale=0.5)
+
+        def gate_gain(n):
+            nc.vector.scalar_tensor_tensor(out=gate[n][:], in0=th[n][:], scalar=1.0, in1=gn_sb[:].unsqueeze(1).broadcast_to([P, H, E]), op0=ALU.add, op1=ALU.mult)
+
+        def finish(u):
+            n, h = divmod(u, H)
+            nc.vector.scalar_tensor_tensor(out=res[n][:, h, :], in0=y_of(u), scalar=rstd[:, u:u + 1], in1=gate[n][:, h, :], op0=ALU.mult, op1=ALU.mult)
+
+        def store(n):
+            nc.sync.dma_start(out=outv[n], in_=res[n][:])
+
+        def store1(u):
+            n, h = divmod(u, H)
+            nc.sync.dma_start(out=outv[n][:, h, :], in_=res[n][:, h, :])
+
+        init()
+        ld_k(1); ld_k(0); ld_q(0); ld_q(1); ld_q(2); ld_m(0); ld_small(); ld_m(1); ld_v(); ld_og(3); ld_m(2); ld_og(2); ld_og(0); ld_og(1)
+        cast_k(1, "v")
+        [quant_k(1, r) for r in range(4)]
+        cast_k(0, "v")
+        [quant_k(0, r) for r in range(4)]
+        cast_q(0, "s")
+        quant_q(0)
+        cast_q(1, "s")
+        scores(1)
+        tanh(1)
+        quant_q(1)
+        cast_q(2, "v")
+        cast_q(3, "v")
+        scores(0)
+        quant_q(2)
+        make_mt(0, "v")
+        scores(2)
+        tanh(0)
+        scores(3)
+        quant_q(3)
+        tanh(2)
+        weigh(1)
+        weigh(0)
+        tanh(3)
+        make_mt(1, "v")
+        scores(5)
+        scores(6)
+        scores(4)
+        cast_v(1, "s")
+        cast_v(0, "v")
+        weigh(3)
+        quant_w(1)
+        quant_v(0)
+        scores(7)
+        tanh(6)
+        quant_w(0)
+        tanh(4)
+        weigh(2)
+        gate_tanh(3)
+        pv(0)
+        quant_v(1)
+        make_mt(2, "v")
+        quant_w(3)
+        tanh(5)
+        gate_tanh(0)
+        gate_tanh(2)
+        gate_tanh(1)
+        quant_w(2)
+        weigh(6)
+        tanh(7)
+        pv(3)
+        pv(2)
+        weigh(4)
+        quant_w(6)
+        weigh(7)
+        weigh(5)
+        quant_w(4)
+        quant_w(7)
+        pv(1)
+        square(0)
+        quant_w(5)
+        square(2)
+        square(1)
+        square(3)
+        gate_gain(3)
+        gate_gain(1)
+        pv(6)
+        switch()
+        gate_gain(0)
+        root(0, 4)
+        pv(4)
+        square(6)
+        pv(7)
+        recip(0, 4)
+        square(7)
+        gate_gain(2)
+        finish(2)
+        finish(3)
+        store(1)
+        finish(1)
+        square(4)
+        pv(5)
+        square(5)
+        root(6, 8)
+        recip(6, 8)
+        finish(0)
+        store(0)
+        root(4, 6)
+        recip(4, 6)
+        finish(6)
+        finish(7)
+        store(3)
+        finish(4)
+        finish(5)
+        store(2)

@@ -39,14 +39,17 @@ def tile_rows_a_tanh_mask_onorm_gate_kernel(tc, qT, kT, t, v, mask, gn, og, out)
 
         QCH = [[0,1],[1,2],[2,4]]
         MCH = [[0,1],[1,2],[2,4]]
-        k_raw = tiles("k_raw", 2, [P, PACK, N // 2], F32)
+        KCH = [[0,256],[256,384],[384,512]]
+        WG = [[0,2],[2,4],[4,6],[6,7],[7,8]]
+        NG = 2
+        k_raw = [sb.tile([P, PACK, b - a], F32, name="k_raw" + str(a)) for a, b in KCH]
         k_bf = tiles("k_bf", 2, [P, PACK, N // 2], BF16, align_bytes=64)
         k_codes = sb.tile([P, N], U32, name="k_codes", align_bytes=64)
         k_scales = sb.tile([P, N], U8, name="k_scales", align_bytes=64)
         q_raw = [sb.tile([P, PACK, (b - a) * QT], F32, name="q_raw" + str(a)) for a, b in QCH]
-        q_bf = tiles("q_bf", TILES, [P, QT * PACK], BF16, align_bytes=64)
-        q_codes = tiles("q_codes", TILES, [P, QT], U32, align_bytes=64)
-        q_scales = tiles("q_scales", TILES, [P, QT], U8, align_bytes=64)
+        q_bf = [sb.tile([P, (b - a) * QT * PACK], BF16, name="q_bf" + str(a), align_bytes=64) for a, b in QCH]
+        q_codes = [sb.tile([P, (b - a) * QT], U32, name="q_codes" + str(a), align_bytes=64) for a, b in QCH]
+        q_scales = [sb.tile([P, (b - a) * QT], U8, name="q_scales" + str(a), align_bytes=64) for a, b in QCH]
         m_raw = [sb.tile([P, PACK, (b - a) * QT], F32, name="m_raw" + str(a)) for a, b in MCH]
         mt = [sb.tile([P, PACK, (b - a) * QT], F32, name="mt" + str(a)) for a, b in MCH]
         v_raw = sb.tile([P, H, PACK * E], F32, name="v_raw")
@@ -55,13 +58,13 @@ def tile_rows_a_tanh_mask_onorm_gate_kernel(tc, qT, kT, t, v, mask, gn, og, out)
         v_scales = sb.tile([P, H * E], U8, name="v_scales", align_bytes=64)
         t_sb = sb.tile([P, PACK], F32, name="t_sb")
         gn_sb = sb.tile([P, E], F32, name="gn_sb")
-        og_sb = tiles("og_sb", TILES, [P, H, E], F32)
-        th = tiles("th", TILES, [P, H, E], F32)
-        gate = tiles("gate", TILES, [P, H, E], F32)
+        og_sb = tiles("og_sb", NG, [P, UNITS // NG, E], F32)
+        th = tiles("th", NG, [P, UNITS // NG, E], F32)
+        gate = tiles("gate", NG, [P, UNITS // NG, E], F32)
         p = tiles("p", UNITS, [P, PACK * QT], F32)
-        w_bf = tiles("w_bf", UNITS, [P, QT * PACK], BF16, align_bytes=64)
-        w_codes = tiles("w_codes", UNITS, [P, QT], U32, align_bytes=64)
-        w_scales = tiles("w_scales", UNITS, [P, QT], U8, align_bytes=64)
+        w_bf = [sb.tile([P, b - a, QT * PACK], BF16, name="w_bf" + str(a), align_bytes=64) for a, b in WG]
+        w_codes = [sb.tile([P, b - a, QT], U32, name="w_codes" + str(a), align_bytes=64) for a, b in WG]
+        w_scales = [sb.tile([P, b - a, QT], U8, name="w_scales" + str(a), align_bytes=64) for a, b in WG]
         sq_junk = tiles("sq_junk", UNITS, [P, E], BF16)
         ss = sb.tile([P, UNITS], F32, name="ss")
         rms = sb.tile([P, UNITS], F32, name="rms")
@@ -76,7 +79,7 @@ def tile_rows_a_tanh_mask_onorm_gate_kernel(tc, qT, kT, t, v, mask, gn, og, out)
         def chunk(chs, n):
             for i, (a, b) in enumerate(chs):
                 if a <= n < b:
-                    return i, (n - a) * QT
+                    return i, n - a
             raise ValueError(n)
 
         def cast(eng, dst, src):
@@ -86,7 +89,7 @@ def tile_rows_a_tanh_mask_onorm_gate_kernel(tc, qT, kT, t, v, mask, gn, og, out)
                 nc.scalar.copy(out=dst, in_=src)
 
         def ld_k(a):
-            nc.sync.dma_start(out=k_raw[a][:], in_=kv[:, :, a * 256:(a + 1) * 256])
+            nc.sync.dma_start(out=k_raw[a][:], in_=kv[:, :, KCH[a][0]:KCH[a][1]])
 
         def ld_q(i):
             a, b = QCH[i]
@@ -100,28 +103,30 @@ def tile_rows_a_tanh_mask_onorm_gate_kernel(tc, qT, kT, t, v, mask, gn, og, out)
             nc.sync.dma_start(out=v_raw[:], in_=vv)
 
         def ld_og(n):
-            nc.sync.dma_start(out=og_sb[n][:], in_=ogv[n])
+            nc.sync.dma_start(out=og_sb[n][:], in_=og[n].rearrange("(n p) e -> p n e", p=QT))
 
-        def ld_small():
+        def ld_t():
             nc.sync.dma_start(out=t_sb[:], in_=t.rearrange("(s r) o -> s (r o)", r=PACK))
+
+        def ld_gn():
             nc.sync.dma_start(out=gn_sb[:], in_=gn)
 
         def init():
             nc.vector.memset(one[:], 1.0)
             nc.scalar.activation(out=warm[:], in_=one[:], func=ACT.Tanh)
 
-        def cast_k(a, eng, s0=0, s1=64):
+        def cast_k(a, eng, s0, s1):
+            i, c0 = chunk(KCH, PACK * (64 * a + s0))
             cast(eng, k_bf[a][:].rearrange("p r (s j) -> p s j r", j=PACK)[:, s0:s1],
-                 k_raw[a][:].rearrange("p j (s r) -> p s j r", r=PACK)[:, s0:s1])
+                 k_raw[i][:, :, c0:c0 + PACK * (s1 - s0)].rearrange("p j (s r) -> p s j r", r=PACK))
 
         def quant_k(a, r):
             cols = slice(r * QT + a * 64, r * QT + (a + 1) * 64)
             nc.vector.quantize_mx(out=k_codes[:, cols].bitcast(FP8X4), scales=k_scales[:, cols], in_=k_bf[a][:, r, :])
 
-        def cast_q(n, eng):
-            i, c0 = chunk(QCH, n)
-            cast(eng, q_bf[n][:].rearrange("p (c i j) -> p c j i", i=2, j=PACK),
-                 q_raw[i][:, :, c0:c0 + QT].rearrange("p j (c i) -> p c j i", i=2))
+        def cast_q(i, eng):
+            cast(eng, q_bf[i][:].rearrange("p (c i j) -> p c j i", i=2, j=PACK),
+                 q_raw[i][:].rearrange("p j (c i) -> p c j i", i=2))
 
         def quant_q(n):
             nc.vector.quantize_mx(out=q_codes[n][:].bitcast(FP8X4), scales=q_scales[n][:], in_=q_bf[n][:])
@@ -130,9 +135,8 @@ def tile_rows_a_tanh_mask_onorm_gate_kernel(tc, qT, kT, t, v, mask, gn, og, out)
             cast(eng, v_bf[:, h, :].rearrange("p (c i j) -> p c j i", i=2, j=PACK),
                  v_raw[:, h, :].rearrange("p (j c i) -> p c j i", i=2, j=PACK))
 
-        def quant_v(h):
-            cols = slice(h * E, (h + 1) * E)
-            nc.vector.quantize_mx(out=v_codes[:, cols].bitcast(FP8X4), scales=v_scales[:, cols], in_=v_bf[:, h, :])
+        def quant_v():
+            nc.vector.quantize_mx(out=v_codes[:].bitcast(FP8X4), scales=v_scales[:], in_=v_bf[:].rearrange("p h c -> p (h c)"))
 
         def make_mt(i, eng):
             for r in range(PACK):
@@ -144,12 +148,14 @@ def tile_rows_a_tanh_mask_onorm_gate_kernel(tc, qT, kT, t, v, mask, gn, og, out)
         def scores(u):
             n, h = divmod(u, H)
             rows = slice(h * ROWS, (h + 1) * ROWS)
+            i, c0 = chunk(QCH, n)
+            qcols = slice(c0 * QT, (c0 + 1) * QT)
             for r in range(PACK):
                 cols = slice(r * QT, (r + 1) * QT)
                 nc.tensor.matmul_mx(
                     out=sc[2 * h + n % 2][:, cols],
                     lhsT=k_codes[rows, cols].bitcast(FP8X4), lhsT_scale=k_scales[rows, cols],
-                    rhs=q_codes[n][rows, :].bitcast(FP8X4), rhs_scale=q_scales[n][rows, :],
+                    rhs=q_codes[i][rows, qcols].bitcast(FP8X4), rhs_scale=q_scales[i][rows, qcols],
                     start=True, stop=True)
 
         def tanh(u):
@@ -158,31 +164,33 @@ def tile_rows_a_tanh_mask_onorm_gate_kernel(tc, qT, kT, t, v, mask, gn, og, out)
 
         def weigh(u):
             i, c0 = chunk(MCH, u // H)
+            g, x = chunk(WG, u)
             nc.vector.tensor_tensor(
-                out=w_bf[u][:].rearrange("p (c i r) -> p c r i", i=2, r=PACK),
+                out=w_bf[g][:, x, :].rearrange("p (c i r) -> p c r i", i=2, r=PACK),
                 in0=p[u][:].rearrange("p (r c i) -> p c r i", i=2, r=PACK),
-                in1=mt[i][:, :, c0:c0 + QT].rearrange("p r (c i) -> p c r i", i=2),
+                in1=mt[i][:, :, c0 * QT:(c0 + 1) * QT].rearrange("p r (c i) -> p c r i", i=2),
                 op=ALU.mult)
 
-        def quant_w(u):
-            nc.vector.quantize_mx(out=w_codes[u][:].bitcast(FP8X4), scales=w_scales[u][:], in_=w_bf[u][:])
+        def quant_w(g):
+            nc.vector.quantize_mx(out=w_codes[g][:].rearrange("p u c -> p (u c)").bitcast(FP8X4), scales=w_scales[g][:].rearrange("p u c -> p (u c)"), in_=w_bf[g][:].rearrange("p u c -> p (u c)"))
 
         def y_of(u):
             return ybank[u % 4][:, (u // 4) * E:(u // 4 + 1) * E]
 
         def pv(u):
+            g, x = chunk(WG, u)
             cols = slice((u % H) * E, (u % H + 1) * E)
-            nc.tensor.matmul_mx(out=y_of(u), lhsT=w_codes[u][:].bitcast(FP8X4), lhsT_scale=w_scales[u][:],
+            nc.tensor.matmul_mx(out=y_of(u), lhsT=w_codes[g][:, x, :].bitcast(FP8X4), lhsT_scale=w_scales[g][:, x, :],
                                 rhs=v_codes[:, cols].bitcast(FP8X4), rhs_scale=v_scales[:, cols], start=True, stop=True)
 
         def square(u):
             nc.scalar.activation(out=sq_junk[u][:], in_=y_of(u), func=ACT.Square, accum_out=ss[:, u:u + 1])
 
         def switch():
-            nc.scalar.activation(out=warm2[:], in_=one[:], func=ACT.Sqrt)
+            nc.scalar.activation(out=warm2[:], in_=one[:], func=ACT.Abs_reciprocal_sqrt)
 
         def root(a, b):
-            nc.scalar.activation(out=rms[:, a:b], in_=ss[:, a:b], func=ACT.Sqrt, scale=4.0 / E, bias=4.0 * 256.0 * 1e-5)
+            nc.scalar.activation(out=rstd[:, a:b], in_=ss[:, a:b], func=ACT.Abs_reciprocal_sqrt, scale=4.0 / E, bias=4.0 * 256.0 * 1e-5)
 
         def recip(a, b):
             nc.vector.reciprocal(out=rstd[:, a:b], in_=rms[:, a:b])
@@ -191,11 +199,11 @@ def tile_rows_a_tanh_mask_onorm_gate_kernel(tc, qT, kT, t, v, mask, gn, og, out)
             nc.scalar.activation(out=th[n][:], in_=og_sb[n][:], func=ACT.Tanh, scale=0.5)
 
         def gate_gain(n):
-            nc.vector.scalar_tensor_tensor(out=gate[n][:], in0=th[n][:], scalar=1.0, in1=gn_sb[:].unsqueeze(1).broadcast_to([P, H, E]), op0=ALU.add, op1=ALU.mult)
+            nc.vector.scalar_tensor_tensor(out=gate[n][:], in0=th[n][:], scalar=1.0, in1=gn_sb[:].unsqueeze(1).broadcast_to([P, UNITS // NG, E]), op0=ALU.add, op1=ALU.mult)
 
         def finish(u):
             n, h = divmod(u, H)
-            nc.vector.scalar_tensor_tensor(out=res[n][:, h, :], in0=y_of(u), scalar=rstd[:, u:u + 1], in1=gate[n][:, h, :], op0=ALU.mult, op1=ALU.mult)
+            nc.vector.scalar_tensor_tensor(out=res[n][:, h, :], in0=y_of(u), scalar=rstd[:, u:u + 1], in1=gate[h][:, n, :], op0=ALU.mult, op1=ALU.mult)
 
         def store(n):
             nc.sync.dma_start(out=outv[n], in_=res[n][:])
@@ -205,98 +213,89 @@ def tile_rows_a_tanh_mask_onorm_gate_kernel(tc, qT, kT, t, v, mask, gn, og, out)
             nc.sync.dma_start(out=outv[n][:, h, :], in_=res[n][:, h, :])
 
         init()
-        ld_k(1); ld_k(0); ld_q(0); ld_q(1); ld_q(2); ld_m(0); ld_small(); ld_m(1); ld_v(); ld_og(3); ld_m(2); ld_og(2); ld_og(0); ld_og(1)
-        cast_k(1, "v")
-        [quant_k(1, r) for r in range(4)]
-        cast_k(0, "v")
-        [quant_k(0, r) for r in range(4)]
+        ld_k(0); ld_q(0); ld_k(1); ld_k(2); ld_q(2); ld_q(1); ld_m(0); ld_t(); ld_m(1); ld_m(2); ld_gn(); ld_v(); ld_og(0); ld_og(1)
         cast_q(0, "s")
+        cast_k(0, "v", 0, 64)
+        [quant_k(0, r) for r in range(4)]
+        cast_k(1, "s", 52, 64)
+        cast_k(1, "v", 0, 32)
         quant_q(0)
-        cast_q(1, "s")
+        cast_k(1, "v", 32, 52)
+        [quant_k(1, r) for r in range(4)]
         scores(1)
-        tanh(1)
-        quant_q(1)
         cast_q(2, "v")
-        cast_q(3, "v")
+        cast_q(1, "v")
+        tanh(1)
         scores(0)
         quant_q(2)
         make_mt(0, "v")
-        scores(2)
         tanh(0)
-        scores(3)
-        quant_q(3)
-        tanh(2)
+        make_mt(1, "s")
+        quant_q(1)
         weigh(1)
-        weigh(0)
-        tanh(3)
-        make_mt(1, "v")
-        scores(5)
-        scores(6)
+        scores(2)
+        tanh(2)
         scores(4)
-        cast_v(1, "s")
+        weigh(0)
+        make_mt(2, "v")
+        tanh(4)
+        quant_w(0)
+        scores(3)
+        tanh(3)
+        scores(5)
+        weigh(2)
+        cast_v(1, "v")
+        tanh(5)
+        scores(6)
         cast_v(0, "v")
         weigh(3)
+        quant_v()
         quant_w(1)
-        quant_v(0)
-        scores(7)
         tanh(6)
-        quant_w(0)
-        tanh(4)
-        weigh(2)
-        gate_tanh(3)
-        pv(0)
-        quant_v(1)
-        make_mt(2, "v")
-        quant_w(3)
-        tanh(5)
+        scores(7)
         gate_tanh(0)
-        gate_tanh(2)
         gate_tanh(1)
-        quant_w(2)
-        weigh(6)
-        tanh(7)
-        pv(3)
         pv(2)
-        weigh(4)
-        quant_w(6)
-        weigh(7)
-        weigh(5)
-        quant_w(4)
-        quant_w(7)
+        tanh(7)
         pv(1)
-        square(0)
-        quant_w(5)
+        weigh(6)
+        pv(0)
         square(2)
-        square(1)
+        pv(3)
+        weigh(5)
         square(3)
-        gate_gain(3)
+        weigh(4)
+        square(0)
+        square(1)
+        weigh(7)
+        quant_w(2)
         gate_gain(1)
-        pv(6)
         switch()
-        gate_gain(0)
-        root(0, 4)
-        pv(4)
-        square(6)
-        pv(7)
-        recip(0, 4)
-        square(7)
-        gate_gain(2)
-        finish(2)
-        finish(3)
-        store(1)
-        finish(1)
-        square(4)
+        root(2, 4)
+        quant_w(3)
+        quant_w(4)
         pv(5)
         square(5)
-        root(6, 8)
-        recip(6, 8)
+        gate_gain(0)
+        pv(4)
+        pv(6)
+        finish(3)
+        square(4)
+        root(0, 2)
+        square(6)
+        pv(7)
+        finish(2)
+        store(1)
+        finish(1)
+        root(4, 6)
+        square(7)
         finish(0)
         store(0)
-        root(4, 6)
-        recip(4, 6)
+        root(6, 7)
+        finish(5)
+        root(7, 8)
+        finish(4)
+        store(2)
         finish(6)
         finish(7)
         store(3)
-        finish(4)
-        finish(5)
-        store(2)

@@ -39,9 +39,9 @@ def tile_rows_a_tanh_mask_onorm_gate_kernel(tc, qT, kT, t, v, mask, gn, og, out)
 
         QCH = [[0,1],[1,2],[2,4]]
         MCH = [[0,1],[1,2],[2,4]]
-        KCH = [[0,256],[256,384],[384,512]]
+        KCH = [[0,256],[256,512]]
         WG = [[0,2],[2,4],[4,6],[6,7],[7,8]]
-        NG = 2
+        NG = 4
         k_raw = [sb.tile([P, PACK, b - a], F32, name="k_raw" + str(a)) for a, b in KCH]
         k_bf = tiles("k_bf", 2, [P, PACK, N // 2], BF16, align_bytes=64)
         k_codes = sb.tile([P, N], U32, name="k_codes", align_bytes=64)
@@ -103,10 +103,10 @@ def tile_rows_a_tanh_mask_onorm_gate_kernel(tc, qT, kT, t, v, mask, gn, og, out)
             nc.sync.dma_start(out=v_raw[:], in_=vv)
 
         def ld_og(n):
-            nc.sync.dma_start(out=og_sb[n][:], in_=og[n].rearrange("(n p) e -> p n e", p=QT))
+            nc.sync.dma_start(out=og_sb[n][:], in_=ogv[n])
 
         def ld_t():
-            nc.sync.dma_start(out=t_sb[:], in_=t.rearrange("(s r) o -> s (r o)", r=PACK))
+            nc.scalar.dma_start(out=t_sb[:], in_=t.rearrange("(s r) o -> s (r o)", r=PACK))
 
         def ld_gn():
             nc.sync.dma_start(out=gn_sb[:], in_=gn)
@@ -115,10 +115,9 @@ def tile_rows_a_tanh_mask_onorm_gate_kernel(tc, qT, kT, t, v, mask, gn, og, out)
             nc.vector.memset(one[:], 1.0)
             nc.scalar.activation(out=warm[:], in_=one[:], func=ACT.Tanh)
 
-        def cast_k(a, eng, s0, s1):
-            i, c0 = chunk(KCH, PACK * (64 * a + s0))
-            cast(eng, k_bf[a][:].rearrange("p r (s j) -> p s j r", j=PACK)[:, s0:s1],
-                 k_raw[i][:, :, c0:c0 + PACK * (s1 - s0)].rearrange("p j (s r) -> p s j r", r=PACK))
+        def cast_k(a, b, eng):
+            cast(eng, k_bf[a][:, 2 * b:2 * b + 2, :].rearrange("p r (s j) -> p s j r", j=PACK),
+                 k_raw[a][:].rearrange("p j (s r) -> p s j r", r=PACK)[:, :, :, 2 * b:2 * b + 2])
 
         def quant_k(a, r):
             cols = slice(r * QT + a * 64, r * QT + (a + 1) * 64)
@@ -157,6 +156,19 @@ def tile_rows_a_tanh_mask_onorm_gate_kernel(tc, qT, kT, t, v, mask, gn, og, out)
                     lhsT=k_codes[rows, cols].bitcast(FP8X4), lhsT_scale=k_scales[rows, cols],
                     rhs=q_codes[i][rows, qcols].bitcast(FP8X4), rhs_scale=q_scales[i][rows, qcols],
                     start=True, stop=True)
+
+        def scores2(n):
+            i, c0 = chunk(QCH, n)
+            qcols = slice(c0 * QT, (c0 + 1) * QT)
+            for r in range(PACK):
+                cols = slice(r * QT, (r + 1) * QT)
+                for h in range(H):
+                    rows = slice(h * ROWS, (h + 1) * ROWS)
+                    nc.tensor.matmul_mx(
+                        out=sc[2 * h + n % 2][:, cols],
+                        lhsT=k_codes[rows, cols].bitcast(FP8X4), lhsT_scale=k_scales[rows, cols],
+                        rhs=q_codes[i][rows, qcols].bitcast(FP8X4), rhs_scale=q_scales[i][rows, qcols],
+                        start=True, stop=True)
 
         def tanh(u):
             n, h = divmod(u, H)
@@ -203,7 +215,7 @@ def tile_rows_a_tanh_mask_onorm_gate_kernel(tc, qT, kT, t, v, mask, gn, og, out)
 
         def finish(u):
             n, h = divmod(u, H)
-            nc.vector.scalar_tensor_tensor(out=res[n][:, h, :], in0=y_of(u), scalar=rstd[:, u:u + 1], in1=gate[h][:, n, :], op0=ALU.mult, op1=ALU.mult)
+            nc.vector.scalar_tensor_tensor(out=res[n][:, h, :], in0=y_of(u), scalar=rstd[:, u:u + 1], in1=gate[n][:, h, :], op0=ALU.mult, op1=ALU.mult)
 
         def store(n):
             nc.sync.dma_start(out=outv[n], in_=res[n][:])
@@ -212,90 +224,94 @@ def tile_rows_a_tanh_mask_onorm_gate_kernel(tc, qT, kT, t, v, mask, gn, og, out)
             n, h = divmod(u, H)
             nc.sync.dma_start(out=outv[n][:, h, :], in_=res[n][:, h, :])
 
+        ld_t()
         init()
-        ld_k(0); ld_q(0); ld_k(1); ld_k(2); ld_q(2); ld_q(1); ld_m(0); ld_t(); ld_m(1); ld_m(2); ld_gn(); ld_v(); ld_og(0); ld_og(1)
-        cast_q(0, "s")
-        cast_k(0, "v", 0, 64)
-        [quant_k(0, r) for r in range(4)]
-        cast_k(1, "s", 52, 64)
-        cast_k(1, "v", 0, 32)
+        ld_k(1); ld_k(0); ld_q(0); ld_q(1); ld_q(2); ld_m(0); ld_og(2); ld_m(1); ld_og(0); ld_v(); ld_m(2); ld_og(3); ld_og(1); ld_gn()
+        cast_k(1, 1, "s")
+        cast_k(1, 0, "v")
+        quant_k(1, 0); quant_k(1, 1)
+        quant_k(1, 2); quant_k(1, 3)
+        cast_k(0, 1, "v")
+        cast_q(0, "v")
+        cast_k(0, 0, "s")
+        quant_k(0, 2); quant_k(0, 3)
+        quant_k(0, 0); quant_k(0, 1)
         quant_q(0)
-        cast_k(1, "v", 32, 52)
-        [quant_k(1, r) for r in range(4)]
+        cast_q(1, "v")
+        quant_q(1)
         scores(1)
         cast_q(2, "v")
-        cast_q(1, "v")
-        tanh(1)
         scores(0)
-        quant_q(2)
+        scores2(1)
         make_mt(0, "v")
+        tanh(1)
+        quant_q(2)
         tanh(0)
-        make_mt(1, "s")
-        quant_q(1)
+        gate_tanh(2)
         weigh(1)
-        scores(2)
-        tanh(2)
-        scores(4)
-        weigh(0)
-        make_mt(2, "v")
-        tanh(4)
-        quant_w(0)
-        scores(3)
         tanh(3)
-        scores(5)
-        weigh(2)
-        cast_v(1, "v")
-        tanh(5)
-        scores(6)
-        cast_v(0, "v")
+        tanh(2)
+        scores2(2)
+        make_mt(1, "v")
+        weigh(0)
         weigh(3)
-        quant_v()
-        quant_w(1)
-        tanh(6)
-        scores(7)
+        weigh(2)
+        cast_v(0, "v")
+        scores2(3)
+        quant_w(0)
         gate_tanh(0)
-        gate_tanh(1)
-        pv(2)
-        tanh(7)
-        pv(1)
-        weigh(6)
+        tanh(5)
+        cast_v(1, "s")
+        tanh(4)
+        quant_v()
+        tanh(6)
+        make_mt(2, "v")
         pv(0)
-        square(2)
-        pv(3)
+        quant_w(1)
+        pv(1)
         weigh(5)
-        square(3)
         weigh(4)
-        square(0)
-        square(1)
-        weigh(7)
+        gate_tanh(1)
+        gate_tanh(3)
+        weigh(6)
         quant_w(2)
-        gate_gain(1)
-        switch()
-        root(2, 4)
+        tanh(7)
+        weigh(7)
         quant_w(3)
-        quant_w(4)
-        pv(5)
-        square(5)
-        gate_gain(0)
+        gate_gain(1)
+        square(1)
+        pv(3)
+        square(0)
+        pv(2)
+        square(3)
         pv(4)
-        pv(6)
-        finish(3)
+        quant_w(4)
+        square(2)
+        gate_gain(0)
+        switch()
+        pv(5)
+        root(0, 4)
+        gate_gain(2)
         square(4)
-        root(0, 2)
+        square(5)
+        pv(6)
+        finish(0)
         square(6)
+        root(4, 6)
         pv(7)
+        finish(1)
+        store(0)
+        finish(3)
+        square(7)
+        root(6, 7)
         finish(2)
         store(1)
-        finish(1)
-        root(4, 6)
-        square(7)
-        finish(0)
-        store(0)
-        root(6, 7)
-        finish(5)
         root(7, 8)
+        gate_gain(3)
         finish(4)
+        finish(5)
         store(2)
         finish(6)
+        store1(6)
         finish(7)
-        store(3)
+        store1(7)

@@ -34,47 +34,48 @@ def tile_rows_a_tanh_mask_onorm_gate_kernel(tc, qT, kT, t, v, mask, gn, og, out)
         kv = kT.rearrange("h (p j) c -> (h p) j c", j=PACK)
         mv = mask.rearrange("(s r) c -> s r c", r=PACK)
         vv = v.rearrange("h (s r) e -> s h (r e)", r=PACK)
-        ogv = og.rearrange("h (n p) e -> n p h e", p=QT)
+        ogv = og.rearrange("h (n p) e -> p n h e", p=QT)
         outv = out.rearrange("h (n p) e -> n p h e", p=QT)
 
         QCH = [[0,1],[1,2],[2,4]]
         MCH = [[0,1],[1,2],[2,4]]
-        KCH = [[0,256],[256,512]]
+        TCH = [[0,1],[1,2],[2,4]]
+        GCH = [[0,2],[2,4]]
         WG = [[0,2],[2,4],[4,6],[6,7],[7,8]]
-        NG = 4
-        k_raw = [sb.tile([P, PACK, b - a], F32, name="k_raw" + str(a)) for a, b in KCH]
-        k_bf = tiles("k_bf", 2, [P, PACK, N // 2], BF16, align_bytes=64)
-        k_codes = sb.tile([P, N], U32, name="k_codes", align_bytes=64)
-        k_scales = sb.tile([P, N], U8, name="k_scales", align_bytes=64)
+        k_raw = sb.tile([P, PACK, N], F32, name="k_raw")
+        k_bf = tiles("k_bf", 2, [P, 2, QT * PACK], BF16, align_bytes=64)
+        k_codes = tiles("k_codes", 2, [P, 2 * QT], U32, align_bytes=64)
+        k_scales = tiles("k_scales", 2, [P, 2 * QT], U8, align_bytes=64)
         q_raw = [sb.tile([P, PACK, (b - a) * QT], F32, name="q_raw" + str(a)) for a, b in QCH]
-        q_bf = [sb.tile([P, (b - a) * QT * PACK], BF16, name="q_bf" + str(a), align_bytes=64) for a, b in QCH]
-        q_codes = [sb.tile([P, (b - a) * QT], U32, name="q_codes" + str(a), align_bytes=64) for a, b in QCH]
-        q_scales = [sb.tile([P, (b - a) * QT], U8, name="q_scales" + str(a), align_bytes=64) for a, b in QCH]
+        q_bf = tiles("q_bf", TILES, [P, QT * PACK], BF16, align_bytes=64)
+        q_codes = tiles("q_codes", TILES, [P, QT], U32, align_bytes=64)
+        q_scales = tiles("q_scales", TILES, [P, QT], U8, align_bytes=64)
         m_raw = [sb.tile([P, PACK, (b - a) * QT], F32, name="m_raw" + str(a)) for a, b in MCH]
-        mt = [sb.tile([P, PACK, (b - a) * QT], F32, name="mt" + str(a)) for a, b in MCH]
+        mt = [sb.tile([P, PACK, (b - a) * QT], F32, name="mt" + str(a)) for a, b in TCH]
         v_raw = sb.tile([P, H, PACK * E], F32, name="v_raw")
         v_bf = sb.tile([P, H, PACK * E], BF16, name="v_bf", align_bytes=64)
         v_codes = sb.tile([P, H * E], U32, name="v_codes", align_bytes=64)
         v_scales = sb.tile([P, H * E], U8, name="v_scales", align_bytes=64)
         t_sb = sb.tile([P, PACK], F32, name="t_sb")
         gn_sb = sb.tile([P, E], F32, name="gn_sb")
-        og_sb = tiles("og_sb", NG, [P, UNITS // NG, E], F32)
-        th = tiles("th", NG, [P, UNITS // NG, E], F32)
-        gate = tiles("gate", NG, [P, UNITS // NG, E], F32)
+        og_sb = [[sb.tile([P, b - a, E], F32, name="og_sb" + str(a) + str(h)) for h in range(H)] for a, b in GCH]
+        th = [[sb.tile([P, b - a, E], F32, name="th" + str(a) + str(h)) for h in range(H)] for a, b in GCH]
+        gate = [[sb.tile([P, b - a, E], F32, name="gate" + str(a) + str(h)) for h in range(H)] for a, b in GCH]
         p = tiles("p", UNITS, [P, PACK * QT], F32)
         w_bf = [sb.tile([P, b - a, QT * PACK], BF16, name="w_bf" + str(a), align_bytes=64) for a, b in WG]
         w_codes = [sb.tile([P, b - a, QT], U32, name="w_codes" + str(a), align_bytes=64) for a, b in WG]
         w_scales = [sb.tile([P, b - a, QT], U8, name="w_scales" + str(a), align_bytes=64) for a, b in WG]
         sq_junk = tiles("sq_junk", UNITS, [P, E], BF16)
         ss = sb.tile([P, UNITS], F32, name="ss")
-        rms = sb.tile([P, UNITS], F32, name="rms")
         rstd = sb.tile([P, UNITS], F32, name="rstd")
-        warm2 = sb.tile([P, 1], F32, name="warm2")
         res = tiles("res", TILES, [P, H, E], F32)
         one = sb.tile([P, 1], F32, name="one")
         warm = sb.tile([P, 1], F32, name="warm")
+        warm2 = sb.tile([P, 1], F32, name="warm2")
         sc = tiles("sc", 2 * H, [P, PACK * QT], F32, pool=ps)
         ybank = tiles("ybank", 4, [P, 512], F32, pool=ps)
+        kh_raw = tiles("kh_raw", 2, [P, PACK, N // 2], F32)
+        kh_bf = [tiles("kh_bf" + str(a), 2, [P, 2, QT * PACK // 2], BF16, align_bytes=64) for a in range(2)]
 
         def chunk(chs, n):
             for i, (a, b) in enumerate(chs):
@@ -88,22 +89,23 @@ def tile_rows_a_tanh_mask_onorm_gate_kernel(tc, qT, kT, t, v, mask, gn, og, out)
             else:
                 nc.scalar.copy(out=dst, in_=src)
 
-        def ld_k(a):
-            nc.sync.dma_start(out=k_raw[a][:], in_=kv[:, :, KCH[a][0]:KCH[a][1]])
+        def ld_k(e=nc.sync):
+            e.dma_start(out=k_raw[:], in_=kv)
 
-        def ld_q(i):
+        def ld_q(i, e=nc.sync):
             a, b = QCH[i]
-            nc.sync.dma_start(out=q_raw[i][:], in_=qv[:, :, a * QT:b * QT])
+            e.dma_start(out=q_raw[i][:], in_=qv[:, :, a * QT:b * QT])
 
-        def ld_m(i):
+        def ld_m(i, e=nc.sync):
             a, b = MCH[i]
-            nc.sync.dma_start(out=m_raw[i][:], in_=mv[:, :, a * QT:b * QT])
+            e.dma_start(out=m_raw[i][:], in_=mv[:, :, a * QT:b * QT])
 
-        def ld_v():
-            nc.sync.dma_start(out=v_raw[:], in_=vv)
+        def ld_v(e=nc.sync):
+            e.dma_start(out=v_raw[:], in_=vv)
 
-        def ld_og(n):
-            nc.sync.dma_start(out=og_sb[n][:], in_=ogv[n])
+        def ld_og(i, h, e=nc.sync):
+            a, b = GCH[i]
+            e.dma_start(out=og_sb[i][h][:], in_=ogv[:, a:b, h, :])
 
         def ld_t():
             nc.scalar.dma_start(out=t_sb[:], in_=t.rearrange("(s r) o -> s (r o)", r=PACK))
@@ -115,17 +117,17 @@ def tile_rows_a_tanh_mask_onorm_gate_kernel(tc, qT, kT, t, v, mask, gn, og, out)
             nc.vector.memset(one[:], 1.0)
             nc.scalar.activation(out=warm[:], in_=one[:], func=ACT.Tanh)
 
-        def cast_k(a, b, eng):
-            cast(eng, k_bf[a][:, 2 * b:2 * b + 2, :].rearrange("p r (s j) -> p s j r", j=PACK),
-                 k_raw[a][:].rearrange("p j (s r) -> p s j r", r=PACK)[:, :, :, 2 * b:2 * b + 2])
+        def cast_k(b, eng):
+            cast(eng, k_bf[b][:].rearrange("p r (s j) -> p s j r", j=PACK),
+                 k_raw[:].rearrange("p j (s r) -> p s j r", r=PACK)[:, :, :, 2 * b:2 * b + 2])
 
-        def quant_k(a, r):
-            cols = slice(r * QT + a * 64, r * QT + (a + 1) * 64)
-            nc.vector.quantize_mx(out=k_codes[:, cols].bitcast(FP8X4), scales=k_scales[:, cols], in_=k_bf[a][:, r, :])
+        def quant_k(b):
+            nc.vector.quantize_mx(out=k_codes[b][:].bitcast(FP8X4), scales=k_scales[b][:], in_=k_bf[b][:].rearrange("p r c -> p (r c)"))
 
-        def cast_q(i, eng):
-            cast(eng, q_bf[i][:].rearrange("p (c i j) -> p c j i", i=2, j=PACK),
-                 q_raw[i][:].rearrange("p j (c i) -> p c j i", i=2))
+        def cast_q(n, eng):
+            i, c0 = chunk(QCH, n)
+            cast(eng, q_bf[n][:].rearrange("p (c i j) -> p c j i", i=2, j=PACK),
+                 q_raw[i][:, :, c0 * QT:(c0 + 1) * QT].rearrange("p j (c i) -> p c j i", i=2))
 
         def quant_q(n):
             nc.vector.quantize_mx(out=q_codes[n][:].bitcast(FP8X4), scales=q_scales[n][:], in_=q_bf[n][:])
@@ -138,44 +140,39 @@ def tile_rows_a_tanh_mask_onorm_gate_kernel(tc, qT, kT, t, v, mask, gn, og, out)
             nc.vector.quantize_mx(out=v_codes[:].bitcast(FP8X4), scales=v_scales[:], in_=v_bf[:].rearrange("p h c -> p (h c)"))
 
         def make_mt(i, eng):
+            a, b = TCH[i]
+            j, c0 = chunk(MCH, a)
+            src = m_raw[j][:, :, c0 * QT:(c0 + b - a) * QT]
             for r in range(PACK):
                 if eng == "v":
-                    nc.vector.tensor_scalar(out=mt[i][:, r, :], in0=m_raw[i][:, r, :], scalar1=t_sb[:, r:r + 1], scalar2=None, op0=ALU.mult)
+                    nc.vector.tensor_scalar(out=mt[i][:, r, :], in0=src[:, r, :], scalar1=t_sb[:, r:r + 1], scalar2=None, op0=ALU.mult)
                 else:
-                    nc.scalar.activation(out=mt[i][:, r, :], in_=m_raw[i][:, r, :], func=ACT.Copy, scale=t_sb[:, r:r + 1])
+                    nc.scalar.activation(out=mt[i][:, r, :], in_=src[:, r, :], func=ACT.Copy, scale=t_sb[:, r:r + 1])
 
-        def scores(u):
-            n, h = divmod(u, H)
+        def score(n, h, r):
             rows = slice(h * ROWS, (h + 1) * ROWS)
-            i, c0 = chunk(QCH, n)
-            qcols = slice(c0 * QT, (c0 + 1) * QT)
-            for r in range(PACK):
-                cols = slice(r * QT, (r + 1) * QT)
-                nc.tensor.matmul_mx(
-                    out=sc[2 * h + n % 2][:, cols],
-                    lhsT=k_codes[rows, cols].bitcast(FP8X4), lhsT_scale=k_scales[rows, cols],
-                    rhs=q_codes[i][rows, qcols].bitcast(FP8X4), rhs_scale=q_scales[i][rows, qcols],
-                    start=True, stop=True)
+            kc = slice((r % 2) * QT, (r % 2 + 1) * QT)
+            nc.tensor.matmul_mx(
+                out=sc[2 * h + n % 2][:, r * QT:(r + 1) * QT],
+                lhsT=k_codes[r // 2][rows, kc].bitcast(FP8X4), lhsT_scale=k_scales[r // 2][rows, kc],
+                rhs=q_codes[n][rows, :].bitcast(FP8X4), rhs_scale=q_scales[n][rows, :],
+                start=True, stop=True)
 
-        def scores2(n):
-            i, c0 = chunk(QCH, n)
-            qcols = slice(c0 * QT, (c0 + 1) * QT)
+        def scores(n):
             for r in range(PACK):
-                cols = slice(r * QT, (r + 1) * QT)
                 for h in range(H):
-                    rows = slice(h * ROWS, (h + 1) * ROWS)
-                    nc.tensor.matmul_mx(
-                        out=sc[2 * h + n % 2][:, cols],
-                        lhsT=k_codes[rows, cols].bitcast(FP8X4), lhsT_scale=k_scales[rows, cols],
-                        rhs=q_codes[i][rows, qcols].bitcast(FP8X4), rhs_scale=q_scales[i][rows, qcols],
-                        start=True, stop=True)
+                    score(n, h, r)
+
+        def scores1(u):
+            for r in range(PACK):
+                score(u // H, u % H, r)
 
         def tanh(u):
             n, h = divmod(u, H)
             nc.scalar.activation(out=p[u][:], in_=sc[2 * h + n % 2][:], func=ACT.Tanh)
 
         def weigh(u):
-            i, c0 = chunk(MCH, u // H)
+            i, c0 = chunk(TCH, u // H)
             g, x = chunk(WG, u)
             nc.vector.tensor_tensor(
                 out=w_bf[g][:, x, :].rearrange("p (c i r) -> p c r i", i=2, r=PACK),
@@ -187,7 +184,7 @@ def tile_rows_a_tanh_mask_onorm_gate_kernel(tc, qT, kT, t, v, mask, gn, og, out)
             nc.vector.quantize_mx(out=w_codes[g][:].rearrange("p u c -> p (u c)").bitcast(FP8X4), scales=w_scales[g][:].rearrange("p u c -> p (u c)"), in_=w_bf[g][:].rearrange("p u c -> p (u c)"))
 
         def y_of(u):
-            return ybank[u % 4][:, (u // 4) * E:(u // 4 + 1) * E]
+            return ybank[u // 2][:, (u % 2) * E:(u % 2 + 1) * E]
 
         def pv(u):
             g, x = chunk(WG, u)
@@ -204,18 +201,17 @@ def tile_rows_a_tanh_mask_onorm_gate_kernel(tc, qT, kT, t, v, mask, gn, og, out)
         def root(a, b):
             nc.scalar.activation(out=rstd[:, a:b], in_=ss[:, a:b], func=ACT.Abs_reciprocal_sqrt, scale=4.0 / E, bias=4.0 * 256.0 * 1e-5)
 
-        def recip(a, b):
-            nc.vector.reciprocal(out=rstd[:, a:b], in_=rms[:, a:b])
+        def gate_tanh(i, h):
+            nc.scalar.activation(out=th[i][h][:], in_=og_sb[i][h][:], func=ACT.Tanh, scale=0.5)
 
-        def gate_tanh(n):
-            nc.scalar.activation(out=th[n][:], in_=og_sb[n][:], func=ACT.Tanh, scale=0.5)
-
-        def gate_gain(n):
-            nc.vector.scalar_tensor_tensor(out=gate[n][:], in0=th[n][:], scalar=1.0, in1=gn_sb[:].unsqueeze(1).broadcast_to([P, UNITS // NG, E]), op0=ALU.add, op1=ALU.mult)
+        def gate_gain(i, h):
+            a, b = GCH[i]
+            nc.vector.scalar_tensor_tensor(out=gate[i][h][:], in0=th[i][h][:], scalar=1.0, in1=gn_sb[:].unsqueeze(1).broadcast_to([P, b - a, E]), op0=ALU.add, op1=ALU.mult)
 
         def finish(u):
             n, h = divmod(u, H)
-            nc.vector.scalar_tensor_tensor(out=res[n][:, h, :], in0=y_of(u), scalar=rstd[:, u:u + 1], in1=gate[n][:, h, :], op0=ALU.mult, op1=ALU.mult)
+            i, x = chunk(GCH, n)
+            nc.vector.scalar_tensor_tensor(out=res[n][:, h, :], in0=y_of(u), scalar=rstd[:, u:u + 1], in1=gate[i][h][:, x, :], op0=ALU.mult, op1=ALU.mult)
 
         def store(n):
             nc.sync.dma_start(out=outv[n], in_=res[n][:])
@@ -224,94 +220,49 @@ def tile_rows_a_tanh_mask_onorm_gate_kernel(tc, qT, kT, t, v, mask, gn, og, out)
             n, h = divmod(u, H)
             nc.sync.dma_start(out=outv[n][:, h, :], in_=res[n][:, h, :])
 
+        def ld_kh(a, e=nc.sync):
+            e.dma_start(out=kh_raw[a][:], in_=kv[:, :, a * 256:(a + 1) * 256])
+
+        def cast_kh(a, b, eng):
+            cast(eng, kh_bf[a][b][:].rearrange("p r (s j) -> p s j r", j=PACK),
+                 kh_raw[a][:].rearrange("p j (s r) -> p s j r", r=PACK)[:, :, :, 2 * b:2 * b + 2])
+
+        def quant_kh(a, b):
+            for x in range(2):
+                cols = slice(x * QT + a * 64, x * QT + (a + 1) * 64)
+                nc.vector.quantize_mx(out=k_codes[b][:, cols].bitcast(FP8X4), scales=k_scales[b][:, cols], in_=kh_bf[a][b][:, x, :])
+
         ld_t()
         init()
-        ld_k(1); ld_k(0); ld_q(0); ld_q(1); ld_q(2); ld_m(0); ld_og(2); ld_m(1); ld_og(0); ld_v(); ld_m(2); ld_og(3); ld_og(1); ld_gn()
-        cast_k(1, 1, "s")
-        cast_k(1, 0, "v")
-        quant_k(1, 0); quant_k(1, 1)
-        quant_k(1, 2); quant_k(1, 3)
-        cast_k(0, 1, "v")
+        ld_q(0); ld_kh(0); ld_kh(1); ld_q(1); ld_m(0); ld_q(2); ld_m(1); ld_m(2); ld_og(0, 0); ld_og(0, 1); ld_v(); ld_og(1, 0); ld_og(1, 1); ld_gn()
         cast_q(0, "v")
-        cast_k(0, 0, "s")
-        quant_k(0, 2); quant_k(0, 3)
-        quant_k(0, 0); quant_k(0, 1)
         quant_q(0)
+        cast_kh(0, 0, "v"); cast_kh(0, 1, "v")
+        quant_kh(0, 0); quant_kh(0, 1)
+        cast_kh(1, 0, "v"); cast_kh(1, 1, "s")
+        quant_kh(1, 0); quant_kh(1, 1)
+        scores1(0); scores1(1)
         cast_q(1, "v")
         quant_q(1)
-        scores(1)
-        cast_q(2, "v")
-        scores(0)
-        scores2(1)
+        scores1(2); scores1(3)
         make_mt(0, "v")
-        tanh(1)
-        quant_q(2)
-        tanh(0)
-        gate_tanh(2)
-        weigh(1)
-        tanh(3)
-        tanh(2)
-        scores2(2)
-        make_mt(1, "v")
-        weigh(0)
-        weigh(3)
-        weigh(2)
-        cast_v(0, "v")
-        scores2(3)
-        quant_w(0)
-        gate_tanh(0)
-        tanh(5)
-        cast_v(1, "s")
-        tanh(4)
-        quant_v()
-        tanh(6)
+        tanh(0); tanh(1)
+        weigh(0); cast_q(2, "v"); cast_q(3, "v"); quant_q(2); weigh(1); quant_q(3)
+        scores1(4); scores1(5)
+        tanh(2); tanh(3)
+        make_mt(1, "s")
+        scores1(6); scores1(7)
+        quant_w(0); weigh(2); weigh(3)
+        tanh(4); tanh(5); tanh(6); tanh(7)
         make_mt(2, "v")
-        pv(0)
         quant_w(1)
-        pv(1)
-        weigh(5)
-        weigh(4)
-        gate_tanh(1)
-        gate_tanh(3)
-        weigh(6)
-        quant_w(2)
-        tanh(7)
-        weigh(7)
-        quant_w(3)
-        gate_gain(1)
-        square(1)
-        pv(3)
-        square(0)
-        pv(2)
-        square(3)
-        pv(4)
-        quant_w(4)
-        square(2)
-        gate_gain(0)
+        gate_tanh(0, 0); gate_tanh(0, 1); cast_v(0, "s"); gate_tanh(1, 0); gate_tanh(1, 1)
         switch()
-        pv(5)
-        root(0, 4)
-        gate_gain(2)
-        square(4)
-        square(5)
-        pv(6)
-        finish(0)
-        square(6)
-        root(4, 6)
-        pv(7)
-        finish(1)
-        store(0)
-        finish(3)
-        square(7)
-        root(6, 7)
-        finish(2)
-        store(1)
-        root(7, 8)
-        gate_gain(3)
-        finish(4)
-        finish(5)
-        store(2)
-        finish(6)
-        store1(6)
-        finish(7)
-        store1(7)
+        weigh(4); weigh(5)
+        cast_v(1, "v"); quant_w(2); quant_v(); weigh(6)
+        pv(0); pv(1); pv(2); pv(3); pv(4); pv(5)
+        weigh(7); quant_w(3); gate_gain(0, 0); quant_w(4); gate_gain(0, 1); gate_gain(1, 0)
+        pv(6); pv(7)
+        square(0); square(1); square(2); root(0, 2); square(3)
+        square(4); root(2, 4); square(5); square(6); root(4, 6); square(7); root(6, 7); root(7, 8)
+        finish(0); finish(1); store(0); gate_gain(1, 1); finish(2); finish(3); store(1); finish(4); finish(5); store(2); finish(6); store1(6); finish(7); store1(7)

@@ -241,17 +241,17 @@ def tile_rows_a_tanh_mask_onorm_gate_kernel(tc, qT, kT, t, v, mask, gn, og, out)
         quant_kh(0, 0); quant_kh(0, 1)
         cast_kh(1, 0, "v"); cast_kh(1, 1, "s")
         quant_kh(1, 0); quant_kh(1, 1)
-        scores1(0); scores1(1)
+        scores(0)
         cast_q(1, "v")
         quant_q(1)
-        scores1(2); scores1(3)
+        scores(1)
         make_mt(0, "v")
         tanh(0); tanh(1)
         weigh(0); cast_q(2, "v"); cast_q(3, "v"); quant_q(2); weigh(1); quant_q(3)
-        scores1(4); scores1(5)
+        scores(2)
         tanh(2); tanh(3)
         make_mt(1, "s")
-        scores1(6); scores1(7)
+        scores(3)
         quant_w(0); weigh(2); weigh(3)
         tanh(4); tanh(5); tanh(6); tanh(7)
         make_mt(2, "v")

@@ -38,7 +38,7 @@ def tile_rows_a_tanh_mask_onorm_gate_kernel(tc, qT, kT, t, v, mask, gn, og, out)
         outv = out.rearrange("h (n p) e -> n p h e", p=QT)
 
         QCH = [[0,1],[1,2],[2,4]]
-        MCH = [[0,1],[1,2],[2,4]]
+        MCH = [[0,1],[1,4]]
         TCH = [[0,1],[1,2],[2,4]]
         GCH = [[0,2],[2,4]]
         WG = [[0,2],[2,4],[4,6],[6,7],[7,8]]
@@ -74,8 +74,6 @@ def tile_rows_a_tanh_mask_onorm_gate_kernel(tc, qT, kT, t, v, mask, gn, og, out)
         warm2 = sb.tile([P, 1], F32, name="warm2")
         sc = tiles("sc", 2 * H, [P, PACK * QT], F32, pool=ps)
         ybank = tiles("ybank", 4, [P, 512], F32, pool=ps)
-        kh_raw = tiles("kh_raw", 2, [P, PACK, N // 2], F32)
-        kh_bf = [tiles("kh_bf" + str(a), 2, [P, 2, QT * PACK // 2], BF16, align_bytes=64) for a in range(2)]
 
         def chunk(chs, n):
             for i, (a, b) in enumerate(chs):
@@ -220,49 +218,30 @@ def tile_rows_a_tanh_mask_onorm_gate_kernel(tc, qT, kT, t, v, mask, gn, og, out)
             n, h = divmod(u, H)
             nc.sync.dma_start(out=outv[n][:, h, :], in_=res[n][:, h, :])
 
-        def ld_kh(a, e=nc.sync):
-            e.dma_start(out=kh_raw[a][:], in_=kv[:, :, a * 256:(a + 1) * 256])
-
-        def cast_kh(a, b, eng):
-            cast(eng, kh_bf[a][b][:].rearrange("p r (s j) -> p s j r", j=PACK),
-                 kh_raw[a][:].rearrange("p j (s r) -> p s j r", r=PACK)[:, :, :, 2 * b:2 * b + 2])
-
-        def quant_kh(a, b):
-            for x in range(2):
-                cols = slice(x * QT + a * 64, x * QT + (a + 1) * 64)
-                nc.vector.quantize_mx(out=k_codes[b][:, cols].bitcast(FP8X4), scales=k_scales[b][:, cols], in_=kh_bf[a][b][:, x, :])
-
         ld_t()
         init()
-        ld_q(0); ld_kh(0); ld_kh(1); ld_q(1); ld_m(0); ld_q(2); ld_m(1); ld_m(2); ld_og(0, 0); ld_og(0, 1); ld_v(); ld_og(1, 0); ld_og(1, 1); ld_gn()
-        cast_q(0, "v")
-        quant_q(0)
-        cast_kh(0, 0, "v"); cast_kh(0, 1, "v")
-        quant_kh(0, 0); quant_kh(0, 1)
-        cast_kh(1, 0, "v"); cast_kh(1, 1, "s")
-        quant_kh(1, 0); quant_kh(1, 1)
+        ld_k(); ld_q(0); ld_q(1); ld_q(2); ld_m(0); ld_m(1); ld_v(); ld_og(0, 0); ld_og(0, 1); ld_og(1, 0); ld_og(1, 1); ld_gn()
+        cast_k(0, "v"); cast_k(1, "s")
+        cast_q(0, "v"); quant_k(0); quant_q(0); quant_k(1)
         scores(0)
         cast_q(1, "v")
         quant_q(1)
         scores(1)
-        make_mt(0, "v")
-        tanh(0); tanh(1)
-        weigh(0); cast_q(2, "v"); cast_q(3, "v"); quant_q(2); weigh(1); quant_q(3)
-        scores(2)
-        tanh(2); tanh(3)
-        make_mt(1, "s")
-        scores(3)
+        cast_q(2, "v"); cast_q(3, "v"); quant_q(2); make_mt(0, "v"); quant_q(3)
+        tanh(0); scores1(4); tanh(1); scores1(5); tanh(2); scores1(6); tanh(3); scores1(7)
+        weigh(0); weigh(1)
+        make_mt(1, "v")
         quant_w(0); weigh(2); weigh(3)
         tanh(4); tanh(5); tanh(6); tanh(7)
         make_mt(2, "v")
         quant_w(1)
-        gate_tanh(0, 0); gate_tanh(0, 1); cast_v(0, "s"); gate_tanh(1, 0); gate_tanh(1, 1)
+        cast_v(0, "s")
+        gate_tanh(0, 0); gate_tanh(0, 1); gate_tanh(1, 0); gate_tanh(1, 1)
         switch()
-        weigh(4); weigh(5)
-        cast_v(1, "v"); quant_w(2); quant_v(); weigh(6)
+        weigh(4); cast_v(1, "v"); weigh(5); quant_v()
+        weigh(6); quant_w(2)
         pv(0); pv(1); pv(2); pv(3); pv(4); pv(5)
-        weigh(7); quant_w(3); gate_gain(0, 0); quant_w(4); gate_gain(0, 1); gate_gain(1, 0)
+        weigh(7); quant_w(3); gate_gain(0, 0); quant_w(4); gate_gain(0, 1)
         pv(6); pv(7)
-        square(0); square(1); square(2); root(0, 2); square(3)
-        square(4); root(2, 4); square(5); square(6); root(4, 6); square(7); root(6, 7); root(7, 8)
-        finish(0); finish(1); store(0); gate_gain(1, 1); finish(2); finish(3); store(1); finish(4); finish(5); store(2); finish(6); store1(6); finish(7); store1(7)
+        square(0); square(1); square(2); square(3); root(0, 2); square(4); root(2, 4); square(5); square(6); root(4, 6); square(7); root(6, 7); root(7, 8)
+        finish(0); finish(1); store(0); gate_gain(1, 0); finish(2); finish(3); store(1); gate_gain(1, 1); finish(4); finish(6); finish(5); store(2); finish(7); store(3)

@@ -38,10 +38,10 @@ def tile_rows_a_tanh_mask_onorm_gate_kernel(tc, qT, kT, t, v, mask, gn, og, out)
         outv = out.rearrange("h (n p) e -> n p h e", p=QT)
 
         QCH = [[0,1],[1,2],[2,4]]
-        MCH = [[0,1],[1,4]]
+        MCH = [[0,1],[1,2],[2,4]]
         TCH = [[0,1],[1,2],[2,4]]
         GCH = [[0,2],[2,4]]
-        WG = [[0,2],[2,4],[4,6],[6,7],[7,8]]
+        WG = [[0,2],[2,4],[4,6],[6,8]]
         k_raw = sb.tile([P, PACK, N], F32, name="k_raw")
         k_bf = tiles("k_bf", 2, [P, 2, QT * PACK], BF16, align_bytes=64)
         k_codes = tiles("k_codes", 2, [P, 2 * QT], U32, align_bytes=64)
@@ -220,28 +220,27 @@ def tile_rows_a_tanh_mask_onorm_gate_kernel(tc, qT, kT, t, v, mask, gn, og, out)
 
         ld_t()
         init()
-        ld_k(); ld_q(0); ld_q(1); ld_q(2); ld_m(0); ld_m(1); ld_v(); ld_og(0, 0); ld_og(0, 1); ld_og(1, 0); ld_og(1, 1); ld_gn()
+        ld_k(); ld_q(0); ld_q(1); ld_q(2); ld_m(0); ld_m(1); ld_v(); ld_m(2); ld_og(0, 0); ld_og(0, 1); ld_gn(); ld_og(1, 0); ld_og(1, 1)
         cast_k(0, "v"); cast_k(1, "s")
         cast_q(0, "v"); quant_k(0); quant_q(0); quant_k(1)
         scores(0)
-        cast_q(1, "v")
+        cast_q(1, "s")
         quant_q(1)
         scores(1)
         cast_q(2, "v"); cast_q(3, "v"); quant_q(2); make_mt(0, "v"); quant_q(3)
         tanh(0); scores1(4); tanh(1); scores1(5); tanh(2); scores1(6); tanh(3); scores1(7)
-        weigh(0); weigh(1)
-        make_mt(1, "v")
-        quant_w(0); weigh(2); weigh(3)
+        weigh(0); make_mt(1, "v"); weigh(1)
+        cast_v(0, "s"); cast_v(1, "v")
+        weigh(2); quant_w(0); weigh(3); quant_v()
+        pv(0); pv(1)
         tanh(4); tanh(5); tanh(6); tanh(7)
-        make_mt(2, "v")
-        quant_w(1)
-        cast_v(0, "s")
+        make_mt(2, "v"); quant_w(1)
+        pv(2); pv(3)
         gate_tanh(0, 0); gate_tanh(0, 1); gate_tanh(1, 0); gate_tanh(1, 1)
+        square(0); square(1)
         switch()
-        weigh(4); cast_v(1, "v"); weigh(5); quant_v()
-        weigh(6); quant_w(2)
-        pv(0); pv(1); pv(2); pv(3); pv(4); pv(5)
-        weigh(7); quant_w(3); gate_gain(0, 0); quant_w(4); gate_gain(0, 1)
-        pv(6); pv(7)
-        square(0); square(1); square(2); square(3); root(0, 2); square(4); root(2, 4); square(5); square(6); root(4, 6); square(7); root(6, 7); root(7, 8)
-        finish(0); finish(1); store(0); gate_gain(1, 0); finish(2); finish(3); store(1); gate_gain(1, 1); finish(4); finish(6); finish(5); store(2); finish(7); store(3)
+        root(0, 2)
+        weigh(4); weigh(5); weigh(6); quant_w(2); weigh(7); gate_gain(0, 0); quant_w(3); gate_gain(0, 1)
+        pv(4); pv(5); pv(6); pv(7)
+        square(2); square(3); square(4); square(5); root(2, 4); root(4, 6); square(6); square(7); root(6, 8)
+        finish(0); gate_gain(1, 0); finish(1); store(0); finish(2); finish(3); store(1); gate_gain(1, 1); finish(4); finish(5); store(2); finish(6); store1(6); finish(7); store1(7)

@@ -74,6 +74,8 @@ def tile_rows_a_tanh_mask_onorm_gate_kernel(tc, qT, kT, t, v, mask, gn, og, out)
         warm2 = sb.tile([P, 1], F32, name="warm2")
         sc = tiles("sc", 2 * H, [P, PACK * QT], F32, pool=ps)
         ybank = tiles("ybank", 4, [P, 512], F32, pool=ps)
+        kh_raw = tiles("kh_raw", 2, [P, PACK, N // 2], F32)
+        kh_bf = [tiles("kh_bf" + str(a), 2, [P, 2, QT * PACK // 2], BF16, align_bytes=64) for a in range(2)]
 
         def chunk(chs, n):
             for i, (a, b) in enumerate(chs):
@@ -218,11 +220,29 @@ def tile_rows_a_tanh_mask_onorm_gate_kernel(tc, qT, kT, t, v, mask, gn, og, out)
             n, h = divmod(u, H)
             nc.sync.dma_start(out=outv[n][:, h, :], in_=res[n][:, h, :])
 
+        def ld_kh(a, e=nc.sync):
+            e.dma_start(out=kh_raw[a][:], in_=kv[:, :, a * 256:(a + 1) * 256])
+
+        def cast_kh(a, b, eng):
+            cast(eng, kh_bf[a][b][:].rearrange("p r (s j) -> p s j r", j=PACK),
+                 kh_raw[a][:].rearrange("p j (s r) -> p s j r", r=PACK)[:, :, :, 2 * b:2 * b + 2])
+
+        def quant_kh(a, b):
+            for x in range(2):
+                cols = slice(x * QT + a * 64, x * QT + (a + 1) * 64)
+                nc.vector.quantize_mx(out=k_codes[b][:, cols].bitcast(FP8X4), scales=k_scales[b][:, cols], in_=kh_bf[a][b][:, x, :])
+
+        def warm_pe(count):
+            for i in range(count):
+                nc.tensor.matmul_mx(out=ybank[3][:, 3 * E:4 * E], lhsT=q_codes[0][:].bitcast(FP8X4), lhsT_scale=q_scales[0][:],
+                                    rhs=q_codes[0][:].bitcast(FP8X4), rhs_scale=q_scales[0][:], start=True, stop=True)
+
         ld_t()
         init()
-        ld_k(); ld_q(0); ld_q(1); ld_q(2); ld_m(0); ld_m(1); ld_v(); ld_m(2); ld_og(0, 0); ld_og(0, 1); ld_gn(); ld_og(1, 0); ld_og(1, 1)
-        cast_k(0, "v"); cast_k(1, "s")
-        cast_q(0, "v"); quant_k(0); quant_q(0); quant_k(1)
+        ld_q(0); ld_kh(0); ld_kh(1); ld_q(1); ld_q(2); ld_m(0); ld_m(1); ld_v(); ld_m(2); ld_og(0, 0); ld_og(0, 1); ld_gn(); ld_og(1, 0); ld_og(1, 1)
+        cast_q(0, "v"); quant_q(0)
+        cast_kh(0, 0, "v"); cast_kh(0, 1, "v"); quant_kh(0, 0); quant_kh(0, 1)
+        cast_kh(1, 0, "v"); cast_kh(1, 1, "v"); quant_kh(1, 0); quant_kh(1, 1)
         scores(0)
         cast_q(1, "s")
         quant_q(1)

@@ -34,48 +34,47 @@ def tile_rows_a_tanh_mask_onorm_gate_kernel(tc, qT, kT, t, v, mask, gn, og, out)
         kv = kT.rearrange("h (p j) c -> (h p) j c", j=PACK)
         mv = mask.rearrange("(s r) c -> s r c", r=PACK)
         vv = v.rearrange("h (s r) e -> s h (r e)", r=PACK)
-        ogv = og.rearrange("h (n p) e -> p n h e", p=QT)
+        ogv = og.rearrange("h (n p) e -> n p h e", p=QT)
         outv = out.rearrange("h (n p) e -> n p h e", p=QT)
 
         QCH = [[0,1],[1,2],[2,4]]
         MCH = [[0,1],[1,2],[2,4]]
-        TCH = [[0,1],[1,2],[2,4]]
-        GCH = [[0,2],[2,4]]
+        KCH = [[0,256],[256,512]]
         WG = [[0,2],[2,4],[4,6],[6,8]]
-        k_raw = sb.tile([P, PACK, N], F32, name="k_raw")
-        k_bf = tiles("k_bf", 2, [P, 2, QT * PACK], BF16, align_bytes=64)
-        k_codes = tiles("k_codes", 2, [P, 2 * QT], U32, align_bytes=64)
-        k_scales = tiles("k_scales", 2, [P, 2 * QT], U8, align_bytes=64)
+        NG = 4
+        k_raw = [sb.tile([P, PACK, b - a], F32, name="k_raw" + str(a)) for a, b in KCH]
+        k_bf = tiles("k_bf", 2, [P, PACK, N // 2], BF16, align_bytes=64)
+        k_codes = sb.tile([P, N], U32, name="k_codes", align_bytes=64)
+        k_scales = sb.tile([P, N], U8, name="k_scales", align_bytes=64)
         q_raw = [sb.tile([P, PACK, (b - a) * QT], F32, name="q_raw" + str(a)) for a, b in QCH]
-        q_bf = tiles("q_bf", TILES, [P, QT * PACK], BF16, align_bytes=64)
-        q_codes = tiles("q_codes", TILES, [P, QT], U32, align_bytes=64)
-        q_scales = tiles("q_scales", TILES, [P, QT], U8, align_bytes=64)
+        q_bf = [sb.tile([P, (b - a) * QT * PACK], BF16, name="q_bf" + str(a), align_bytes=64) for a, b in QCH]
+        q_codes = [sb.tile([P, (b - a) * QT], U32, name="q_codes" + str(a), align_bytes=64) for a, b in QCH]
+        q_scales = [sb.tile([P, (b - a) * QT], U8, name="q_scales" + str(a), align_bytes=64) for a, b in QCH]
         m_raw = [sb.tile([P, PACK, (b - a) * QT], F32, name="m_raw" + str(a)) for a, b in MCH]
-        mt = [sb.tile([P, PACK, (b - a) * QT], F32, name="mt" + str(a)) for a, b in TCH]
+        mt = [sb.tile([P, PACK, (b - a) * QT], F32, name="mt" + str(a)) for a, b in MCH]
         v_raw = sb.tile([P, H, PACK * E], F32, name="v_raw")
         v_bf = sb.tile([P, H, PACK * E], BF16, name="v_bf", align_bytes=64)
         v_codes = sb.tile([P, H * E], U32, name="v_codes", align_bytes=64)
         v_scales = sb.tile([P, H * E], U8, name="v_scales", align_bytes=64)
         t_sb = sb.tile([P, PACK], F32, name="t_sb")
         gn_sb = sb.tile([P, E], F32, name="gn_sb")
-        og_sb = [[sb.tile([P, b - a, E], F32, name="og_sb" + str(a) + str(h)) for h in range(H)] for a, b in GCH]
-        th = [[sb.tile([P, b - a, E], F32, name="th" + str(a) + str(h)) for h in range(H)] for a, b in GCH]
-        gate = [[sb.tile([P, b - a, E], F32, name="gate" + str(a) + str(h)) for h in range(H)] for a, b in GCH]
+        og_sb = tiles("og_sb", NG, [P, UNITS // NG, E], F32)
+        th = tiles("th", NG, [P, UNITS // NG, E], F32)
+        gate = tiles("gate", NG, [P, UNITS // NG, E], F32)
         p = tiles("p", UNITS, [P, PACK * QT], F32)
         w_bf = [sb.tile([P, b - a, QT * PACK], BF16, name="w_bf" + str(a), align_bytes=64) for a, b in WG]
         w_codes = [sb.tile([P, b - a, QT], U32, name="w_codes" + str(a), align_bytes=64) for a, b in WG]
         w_scales = [sb.tile([P, b - a, QT], U8, name="w_scales" + str(a), align_bytes=64) for a, b in WG]
         sq_junk = tiles("sq_junk", UNITS, [P, E], BF16)
         ss = sb.tile([P, UNITS], F32, name="ss")
+        rms = sb.tile([P, UNITS], F32, name="rms")
         rstd = sb.tile([P, UNITS], F32, name="rstd")
+        warm2 = sb.tile([P, 1], F32, name="warm2")
         res = tiles("res", TILES, [P, H, E], F32)
         one = sb.tile([P, 1], F32, name="one")
         warm = sb.tile([P, 1], F32, name="warm")
-        warm2 = sb.tile([P, 1], F32, name="warm2")
         sc = tiles("sc", 2 * H, [P, PACK * QT], F32, pool=ps)
         ybank = tiles("ybank", 4, [P, 512], F32, pool=ps)
-        kh_raw = tiles("kh_raw", 2, [P, PACK, N // 2], F32)
-        kh_bf = [tiles("kh_bf" + str(a), 2, [P, 2, QT * PACK // 2], BF16, align_bytes=64) for a in range(2)]
 
         def chunk(chs, n):
             for i, (a, b) in enumerate(chs):
@@ -89,23 +88,22 @@ def tile_rows_a_tanh_mask_onorm_gate_kernel(tc, qT, kT, t, v, mask, gn, og, out)
             else:
                 nc.scalar.copy(out=dst, in_=src)
 
-        def ld_k(e=nc.sync):
-            e.dma_start(out=k_raw[:], in_=kv)
+        def ld_k(a):
+            nc.sync.dma_start(out=k_raw[a][:], in_=kv[:, :, KCH[a][0]:KCH[a][1]])
 
-        def ld_q(i, e=nc.sync):
+        def ld_q(i):
             a, b = QCH[i]
-            e.dma_start(out=q_raw[i][:], in_=qv[:, :, a * QT:b * QT])
+            nc.sync.dma_start(out=q_raw[i][:], in_=qv[:, :, a * QT:b * QT])
 
-        def ld_m(i, e=nc.sync):
+        def ld_m(i):
             a, b = MCH[i]
-            e.dma_start(out=m_raw[i][:], in_=mv[:, :, a * QT:b * QT])
+            nc.sync.dma_start(out=m_raw[i][:], in_=mv[:, :, a * QT:b * QT])
 
-        def ld_v(e=nc.sync):
-            e.dma_start(out=v_raw[:], in_=vv)
+        def ld_v():
+            nc.sync.dma_start(out=v_raw[:], in_=vv)
 
-        def ld_og(i, h, e=nc.sync):
-            a, b = GCH[i]
-            e.dma_start(out=og_sb[i][h][:], in_=ogv[:, a:b, h, :])
+        def ld_og(n):
+            nc.sync.dma_start(out=og_sb[n][:], in_=ogv[n])
 
         def ld_t():
             nc.scalar.dma_start(out=t_sb[:], in_=t.rearrange("(s r) o -> s (r o)", r=PACK))
@@ -117,17 +115,17 @@ def tile_rows_a_tanh_mask_onorm_gate_kernel(tc, qT, kT, t, v, mask, gn, og, out)
             nc.vector.memset(one[:], 1.0)
             nc.scalar.activation(out=warm[:], in_=one[:], func=ACT.Tanh)
 
-        def cast_k(b, eng):
-            cast(eng, k_bf[b][:].rearrange("p r (s j) -> p s j r", j=PACK),
-                 k_raw[:].rearrange("p j (s r) -> p s j r", r=PACK)[:, :, :, 2 * b:2 * b + 2])
+        def cast_k(a, b, eng):
+            cast(eng, k_bf[a][:, 2 * b:2 * b + 2, :].rearrange("p r (s j) -> p s j r", j=PACK),
+                 k_raw[a][:].rearrange("p j (s r) -> p s j r", r=PACK)[:, :, :, 2 * b:2 * b + 2])
 
-        def quant_k(b):
-            nc.vector.quantize_mx(out=k_codes[b][:].bitcast(FP8X4), scales=k_scales[b][:], in_=k_bf[b][:].rearrange("p r c -> p (r c)"))
+        def quant_k(a, r):
+            cols = slice(r * QT + a * 64, r * QT + (a + 1) * 64)
+            nc.vector.quantize_mx(out=k_codes[:, cols].bitcast(FP8X4), scales=k_scales[:, cols], in_=k_bf[a][:, r, :])
 
-        def cast_q(n, eng):
-            i, c0 = chunk(QCH, n)
-            cast(eng, q_bf[n][:].rearrange("p (c i j) -> p c j i", i=2, j=PACK),
-                 q_raw[i][:, :, c0 * QT:(c0 + 1) * QT].rearrange("p j (c i) -> p c j i", i=2))
+        def cast_q(i, eng):
+            cast(eng, q_bf[i][:].rearrange("p (c i j) -> p c j i", i=2, j=PACK),
+                 q_raw[i][:].rearrange("p j (c i) -> p c j i", i=2))
 
         def quant_q(n):
             nc.vector.quantize_mx(out=q_codes[n][:].bitcast(FP8X4), scales=q_scales[n][:], in_=q_bf[n][:])
@@ -140,39 +138,44 @@ def tile_rows_a_tanh_mask_onorm_gate_kernel(tc, qT, kT, t, v, mask, gn, og, out)
             nc.vector.quantize_mx(out=v_codes[:].bitcast(FP8X4), scales=v_scales[:], in_=v_bf[:].rearrange("p h c -> p (h c)"))
 
         def make_mt(i, eng):
-            a, b = TCH[i]
-            j, c0 = chunk(MCH, a)
-            src = m_raw[j][:, :, c0 * QT:(c0 + b - a) * QT]
             for r in range(PACK):
                 if eng == "v":
-                    nc.vector.tensor_scalar(out=mt[i][:, r, :], in0=src[:, r, :], scalar1=t_sb[:, r:r + 1], scalar2=None, op0=ALU.mult)
+                    nc.vector.tensor_scalar(out=mt[i][:, r, :], in0=m_raw[i][:, r, :], scalar1=t_sb[:, r:r + 1], scalar2=None, op0=ALU.mult)
                 else:
-                    nc.scalar.activation(out=mt[i][:, r, :], in_=src[:, r, :], func=ACT.Copy, scale=t_sb[:, r:r + 1])
+                    nc.scalar.activation(out=mt[i][:, r, :], in_=m_raw[i][:, r, :], func=ACT.Copy, scale=t_sb[:, r:r + 1])
 
-        def score(n, h, r):
+        def scores(u):
+            n, h = divmod(u, H)
             rows = slice(h * ROWS, (h + 1) * ROWS)
-            kc = slice((r % 2) * QT, (r % 2 + 1) * QT)
-            nc.tensor.matmul_mx(
-                out=sc[2 * h + n % 2][:, r * QT:(r + 1) * QT],
-                lhsT=k_codes[r // 2][rows, kc].bitcast(FP8X4), lhsT_scale=k_scales[r // 2][rows, kc],
-                rhs=q_codes[n][rows, :].bitcast(FP8X4), rhs_scale=q_scales[n][rows, :],
-                start=True, stop=True)
-
-        def scores(n):
+            i, c0 = chunk(QCH, n)
+            qcols = slice(c0 * QT, (c0 + 1) * QT)
             for r in range(PACK):
+                cols = slice(r * QT, (r + 1) * QT)
+                nc.tensor.matmul_mx(
+                    out=sc[2 * h + n % 2][:, cols],
+                    lhsT=k_codes[rows, cols].bitcast(FP8X4), lhsT_scale=k_scales[rows, cols],
+                    rhs=q_codes[i][rows, qcols].bitcast(FP8X4), rhs_scale=q_scales[i][rows, qcols],
+                    start=True, stop=True)
+
+        def scores2(n):
+            i, c0 = chunk(QCH, n)
+            qcols = slice(c0 * QT, (c0 + 1) * QT)
+            for r in range(PACK):
+                cols = slice(r * QT, (r + 1) * QT)
                 for h in range(H):
-                    score(n, h, r)
-
-        def scores1(u):
-            for r in range(PACK):
-                score(u // H, u % H, r)
+                    rows = slice(h * ROWS, (h + 1) * ROWS)
+                    nc.tensor.matmul_mx(
+                        out=sc[2 * h + n % 2][:, cols],
+                        lhsT=k_codes[rows, cols].bitcast(FP8X4), lhsT_scale=k_scales[rows, cols],
+                        rhs=q_codes[i][rows, qcols].bitcast(FP8X4), rhs_scale=q_scales[i][rows, qcols],
+                        start=True, stop=True)
 
         def tanh(u):
             n, h = divmod(u, H)
             nc.scalar.activation(out=p[u][:], in_=sc[2 * h + n % 2][:], func=ACT.Tanh)
 
         def weigh(u):
-            i, c0 = chunk(TCH, u // H)
+            i, c0 = chunk(MCH, u // H)
             g, x = chunk(WG, u)
             nc.vector.tensor_tensor(
                 out=w_bf[g][:, x, :].rearrange("p (c i r) -> p c r i", i=2, r=PACK),
@@ -201,17 +204,18 @@ def tile_rows_a_tanh_mask_onorm_gate_kernel(tc, qT, kT, t, v, mask, gn, og, out)
         def root(a, b):
             nc.scalar.activation(out=rstd[:, a:b], in_=ss[:, a:b], func=ACT.Abs_reciprocal_sqrt, scale=4.0 / E, bias=4.0 * 256.0 * 1e-5)
 
-        def gate_tanh(i, h):
-            nc.scalar.activation(out=th[i][h][:], in_=og_sb[i][h][:], func=ACT.Tanh, scale=0.5)
+        def recip(a, b):
+            nc.vector.reciprocal(out=rstd[:, a:b], in_=rms[:, a:b])
 
-        def gate_gain(i, h):
-            a, b = GCH[i]
-            nc.vector.scalar_tensor_tensor(out=gate[i][h][:], in0=th[i][h][:], scalar=1.0, in1=gn_sb[:].unsqueeze(1).broadcast_to([P, b - a, E]), op0=ALU.add, op1=ALU.mult)
+        def gate_tanh(n):
+            nc.scalar.activation(out=th[n][:], in_=og_sb[n][:], func=ACT.Tanh, scale=0.5)
+
+        def gate_gain(n):
+            nc.vector.scalar_tensor_tensor(out=gate[n][:], in0=th[n][:], scalar=1.0, in1=gn_sb[:].unsqueeze(1).broadcast_to([P, UNITS // NG, E]), op0=ALU.add, op1=ALU.mult)
 
         def finish(u):
             n, h = divmod(u, H)
-            i, x = chunk(GCH, n)
-            nc.vector.scalar_tensor_tensor(out=res[n][:, h, :], in0=y_of(u), scalar=rstd[:, u:u + 1], in1=gate[i][h][:, x, :], op0=ALU.mult, op1=ALU.mult)
+            nc.vector.scalar_tensor_tensor(out=res[n][:, h, :], in0=y_of(u), scalar=rstd[:, u:u + 1], in1=gate[n][:, h, :], op0=ALU.mult, op1=ALU.mult)
 
         def store(n):
             nc.sync.dma_start(out=outv[n], in_=res[n][:])
@@ -220,35 +224,18 @@ def tile_rows_a_tanh_mask_onorm_gate_kernel(tc, qT, kT, t, v, mask, gn, og, out)
             n, h = divmod(u, H)
             nc.sync.dma_start(out=outv[n][:, h, :], in_=res[n][:, h, :])
 
-        def ld_kh(a, e=nc.sync):
-            e.dma_start(out=kh_raw[a][:], in_=kv[:, :, a * 256:(a + 1) * 256])
-
-        def cast_kh(a, b, eng):
-            cast(eng, kh_bf[a][b][:].rearrange("p r (s j) -> p s j r", j=PACK),
-                 kh_raw[a][:].rearrange("p j (s r) -> p s j r", r=PACK)[:, :, :, 2 * b:2 * b + 2])
-
-        def quant_kh(a, b):
-            for x in range(2):
-                cols = slice(x * QT + a * 64, x * QT + (a + 1) * 64)
-                nc.vector.quantize_mx(out=k_codes[b][:, cols].bitcast(FP8X4), scales=k_scales[b][:, cols], in_=kh_bf[a][b][:, x, :])
-
-        def warm_pe(count):
-            for i in range(count):
-                nc.tensor.matmul_mx(out=ybank[3][:, 3 * E:4 * E], lhsT=q_codes[0][:].bitcast(FP8X4), lhsT_scale=q_scales[0][:],
-                                    rhs=q_codes[0][:].bitcast(FP8X4), rhs_scale=q_scales[0][:], start=True, stop=True)
-
         ld_t()
         init()
-        ld_q(0); ld_kh(0); ld_kh(1); ld_q(1); ld_q(2); ld_m(0); ld_m(1); ld_v(); ld_m(2); ld_og(0, 0); ld_og(0, 1); ld_gn(); ld_og(1, 0); ld_og(1, 1)
+        ld_q(0); ld_k(0); ld_k(1); ld_q(1); ld_q(2); ld_m(0); ld_m(1); ld_v(); ld_m(2); ld_og(0); ld_og(1); ld_gn(); ld_og(2); ld_og(3)
         cast_q(0, "v"); quant_q(0)
-        cast_kh(0, 0, "v"); cast_kh(0, 1, "v"); quant_kh(0, 0); quant_kh(0, 1)
-        cast_kh(1, 0, "v"); cast_kh(1, 1, "v"); quant_kh(1, 0); quant_kh(1, 1)
-        scores(0)
+        cast_k(0, 0, "v"); cast_k(0, 1, "v"); quant_k(0, 0); quant_k(0, 1); quant_k(0, 2); quant_k(0, 3)
+        cast_k(1, 0, "v"); cast_k(1, 1, "v"); quant_k(1, 0); quant_k(1, 1); quant_k(1, 2); quant_k(1, 3)
+        scores2(0)
         cast_q(1, "s")
         quant_q(1)
-        scores(1)
-        cast_q(2, "v"); cast_q(3, "v"); quant_q(2); make_mt(0, "v"); quant_q(3)
-        tanh(0); scores1(4); tanh(1); scores1(5); tanh(2); scores1(6); tanh(3); scores1(7)
+        scores2(1)
+        cast_q(2, "v"); make_mt(0, "v"); quant_q(2)
+        tanh(0); scores(4); tanh(1); scores(5); tanh(2); scores(6); tanh(3); scores(7)
         weigh(0); make_mt(1, "v"); weigh(1)
         cast_v(0, "s"); cast_v(1, "v")
         weigh(2); quant_w(0); weigh(3); quant_v()
@@ -256,11 +243,11 @@ def tile_rows_a_tanh_mask_onorm_gate_kernel(tc, qT, kT, t, v, mask, gn, og, out)
         tanh(4); tanh(5); tanh(6); tanh(7)
         make_mt(2, "v"); quant_w(1)
         pv(2); pv(3)
-        gate_tanh(0, 0); gate_tanh(0, 1); gate_tanh(1, 0); gate_tanh(1, 1)
+        gate_tanh(0); gate_tanh(1); gate_tanh(2); gate_tanh(3)
         square(0); square(1)
         switch()
         root(0, 2)
-        weigh(4); weigh(5); weigh(6); quant_w(2); weigh(7); gate_gain(0, 0); quant_w(3); gate_gain(0, 1)
+        weigh(4); weigh(5); weigh(6); quant_w(2); weigh(7); gate_gain(0); quant_w(3); gate_gain(1)
         pv(4); pv(5); pv(6); pv(7)
         square(2); square(3); square(4); square(5); root(2, 4); root(4, 6); square(6); square(7); root(6, 8)
-        finish(0); gate_gain(1, 0); finish(1); store(0); finish(2); finish(3); store(1); gate_gain(1, 1); finish(4); finish(5); store(2); finish(6); store1(6); finish(7); store1(7)
+        finish(0); finish(1); store(0); gate_gain(2); finish(2); finish(3); store(1); gate_gain(3); finish(4); finish(5); store(2); finish(6); store1(6); finish(7); store1(7)

@@ -42,23 +42,23 @@ def tile_rows_a_tanh_mask_onorm_gate_kernel(tc, qT, kT, t, v, mask, gn, og, out)
         KCH = [[0,256],[256,512]]
         WG = [[0,2],[2,4],[4,6],[6,8]]
         NG = 4
-        k_raw = [sb.tile([P, PACK, b - a], F32, name="k_raw" + str(a)) for a, b in KCH]
+        k_raw = [sb.tile([P, PACK, b - a], F32, name="k_raw" + str(a), align_bytes=256) for a, b in KCH]
         k_bf = tiles("k_bf", 2, [P, PACK, N // 2], BF16, align_bytes=64)
         k_codes = sb.tile([P, N], U32, name="k_codes", align_bytes=64)
         k_scales = sb.tile([P, N], U8, name="k_scales", align_bytes=64)
-        q_raw = [sb.tile([P, PACK, (b - a) * QT], F32, name="q_raw" + str(a)) for a, b in QCH]
+        q_raw = [sb.tile([P, PACK, (b - a) * QT], F32, name="q_raw" + str(a), align_bytes=256) for a, b in QCH]
         q_bf = [sb.tile([P, (b - a) * QT * PACK], BF16, name="q_bf" + str(a), align_bytes=64) for a, b in QCH]
         q_codes = [sb.tile([P, (b - a) * QT], U32, name="q_codes" + str(a), align_bytes=64) for a, b in QCH]
         q_scales = [sb.tile([P, (b - a) * QT], U8, name="q_scales" + str(a), align_bytes=64) for a, b in QCH]
-        m_raw = [sb.tile([P, PACK, (b - a) * QT], F32, name="m_raw" + str(a)) for a, b in MCH]
+        m_raw = [sb.tile([P, PACK, (b - a) * QT], F32, name="m_raw" + str(a), align_bytes=256) for a, b in MCH]
         mt = [sb.tile([P, PACK, (b - a) * QT], F32, name="mt" + str(a)) for a, b in MCH]
-        v_raw = sb.tile([P, H, PACK * E], F32, name="v_raw")
+        v_raw = sb.tile([P, H, PACK * E], F32, name="v_raw", align_bytes=256)
         v_bf = sb.tile([P, H, PACK * E], BF16, name="v_bf", align_bytes=64)
         v_codes = sb.tile([P, H * E], U32, name="v_codes", align_bytes=64)
         v_scales = sb.tile([P, H * E], U8, name="v_scales", align_bytes=64)
         t_sb = sb.tile([P, PACK], F32, name="t_sb")
-        gn_sb = sb.tile([P, E], F32, name="gn_sb")
-        og_sb = tiles("og_sb", NG, [P, UNITS // NG, E], F32)
+        gn_sb = sb.tile([P, E], F32, name="gn_sb", align_bytes=256)
+        og_sb = tiles("og_sb", NG, [P, UNITS // NG, E], F32, align_bytes=256)
         th = tiles("th", NG, [P, UNITS // NG, E], F32)
         gate = tiles("gate", NG, [P, UNITS // NG, E], F32)
         p = tiles("p", UNITS, [P, PACK * QT], F32)
@@ -70,7 +70,7 @@ def tile_rows_a_tanh_mask_onorm_gate_kernel(tc, qT, kT, t, v, mask, gn, og, out)
         rms = sb.tile([P, UNITS], F32, name="rms")
         rstd = sb.tile([P, UNITS], F32, name="rstd")
         warm2 = sb.tile([P, 1], F32, name="warm2")
-        res = tiles("res", TILES, [P, H, E], F32)
+        res = tiles("res", TILES, [P, H, E], F32, align_bytes=256)
         one = sb.tile([P, 1], F32, name="one")
         warm = sb.tile([P, 1], F32, name="warm")
         sc = tiles("sc", 2 * H, [P, PACK * QT], F32, pool=ps)

@@ -37,7 +37,8 @@ def tile_rows_a_tanh_mask_onorm_gate_kernel(tc, qT, kT, t, v, mask, gn, og, out)
         ogv = og.rearrange("h (n p) e -> n p h e", p=QT)
         outv = out.rearrange("h (n p) e -> n p h e", p=QT)
 
-        QCH = [[0,1],[1,2],[2,4]]
+        QCH = [[0,1],[1,2],[2,3],[3,4]]
+        QT_OF = [[0,1],[1,2],[2,3],[3,4]]
         MCH = [[0,1],[1,2],[2,4]]
         KCH = [[0,256],[256,512]]
         WG = [[0,2],[2,4],[4,6],[6,8]]
@@ -47,9 +48,9 @@ def tile_rows_a_tanh_mask_onorm_gate_kernel(tc, qT, kT, t, v, mask, gn, og, out)
         k_codes = sb.tile([P, N], U32, name="k_codes", align_bytes=64)
         k_scales = sb.tile([P, N], U8, name="k_scales", align_bytes=64)
         q_raw = [sb.tile([P, PACK, (b - a) * QT], F32, name="q_raw" + str(a), align_bytes=256) for a, b in QCH]
-        q_bf = [sb.tile([P, (b - a) * QT * PACK], BF16, name="q_bf" + str(a), align_bytes=64) for a, b in QCH]
-        q_codes = [sb.tile([P, (b - a) * QT], U32, name="q_codes" + str(a), align_bytes=64) for a, b in QCH]
-        q_scales = [sb.tile([P, (b - a) * QT], U8, name="q_scales" + str(a), align_bytes=64) for a, b in QCH]
+        q_bf = tiles("q_bf", TILES, [P, QT * PACK], BF16, align_bytes=256)
+        q_codes = tiles("q_codes", TILES, [P, QT], U32, align_bytes=256)
+        q_scales = tiles("q_scales", TILES, [P, QT], U8, align_bytes=256)
         m_raw = [sb.tile([P, PACK, (b - a) * QT], F32, name="m_raw" + str(a), align_bytes=256) for a, b in MCH]
         mt = [sb.tile([P, PACK, (b - a) * QT], F32, name="mt" + str(a)) for a, b in MCH]
         v_raw = sb.tile([P, H, PACK * E], F32, name="v_raw", align_bytes=256)
@@ -123,9 +124,10 @@ def tile_rows_a_tanh_mask_onorm_gate_kernel(tc, qT, kT, t, v, mask, gn, og, out)
             cols = slice(r * QT + a * 64, r * QT + (a + 1) * 64)
             nc.vector.quantize_mx(out=k_codes[:, cols].bitcast(FP8X4), scales=k_scales[:, cols], in_=k_bf[a][:, r, :])
 
-        def cast_q(i, eng):
-            cast(eng, q_bf[i][:].rearrange("p (c i j) -> p c j i", i=2, j=PACK),
-                 q_raw[i][:].rearrange("p j (c i) -> p c j i", i=2))
+        def cast_q(n, eng):
+            i, c0 = chunk(QCH, n)
+            cast(eng, q_bf[n][:].rearrange("p (c i j) -> p c j i", i=2, j=PACK),
+                 q_raw[i][:, :, c0 * QT:(c0 + 1) * QT].rearrange("p j (c i) -> p c j i", i=2))
 
         def quant_q(n):
             nc.vector.quantize_mx(out=q_codes[n][:].bitcast(FP8X4), scales=q_scales[n][:], in_=q_bf[n][:])
@@ -147,7 +149,7 @@ def tile_rows_a_tanh_mask_onorm_gate_kernel(tc, qT, kT, t, v, mask, gn, og, out)
         def scores(u):
             n, h = divmod(u, H)
             rows = slice(h * ROWS, (h + 1) * ROWS)
-            i, c0 = chunk(QCH, n)
+            i, c0 = chunk(QT_OF, n)
             qcols = slice(c0 * QT, (c0 + 1) * QT)
             for r in range(PACK):
                 cols = slice(r * QT, (r + 1) * QT)
@@ -158,7 +160,7 @@ def tile_rows_a_tanh_mask_onorm_gate_kernel(tc, qT, kT, t, v, mask, gn, og, out)
                     start=True, stop=True)
 
         def scores2(n):
-            i, c0 = chunk(QCH, n)
+            i, c0 = chunk(QT_OF, n)
             qcols = slice(c0 * QT, (c0 + 1) * QT)
             for r in range(PACK):
                 cols = slice(r * QT, (r + 1) * QT)
@@ -224,25 +226,31 @@ def tile_rows_a_tanh_mask_onorm_gate_kernel(tc, qT, kT, t, v, mask, gn, og, out)
             n, h = divmod(u, H)
             nc.sync.dma_start(out=outv[n][:, h, :], in_=res[n][:, h, :])
 
+        def warm_pe(count):
+            for i in range(count):
+                nc.tensor.matmul_mx(out=ybank[3][:, 3 * E:4 * E], lhsT=q_codes[0][:].bitcast(FP8X4), lhsT_scale=q_scales[0][:],
+                                    rhs=q_codes[0][:].bitcast(FP8X4), rhs_scale=q_scales[0][:], start=True, stop=True)
+
         ld_t()
         init()
-        ld_q(0); ld_k(0); ld_k(1); ld_q(1); ld_q(2); ld_m(0); ld_m(1); ld_v(); ld_m(2); ld_og(0); ld_og(1); ld_gn(); ld_og(2); ld_og(3)
+        ld_q(0); ld_k(0); ld_k(1); ld_q(1); ld_q(2); ld_m(0); ld_q(3); ld_m(1); ld_v(); ld_m(2); ld_og(0); ld_og(1); ld_gn(); ld_og(2); ld_og(3)
         cast_q(0, "v"); quant_q(0)
         cast_k(0, 0, "v"); cast_k(0, 1, "v"); quant_k(0, 0); quant_k(0, 1); quant_k(0, 2); quant_k(0, 3)
         cast_k(1, 0, "v"); cast_k(1, 1, "v"); quant_k(1, 0); quant_k(1, 1); quant_k(1, 2); quant_k(1, 3)
         scores2(0)
         cast_q(1, "s")
-        quant_q(1)
+        cast_q(2, "v"); quant_q(1); quant_q(2)
         scores2(1)
-        cast_q(2, "v"); make_mt(0, "v"); quant_q(2)
-        tanh(0); scores(4); tanh(1); scores(5); tanh(2); scores(6); tanh(3); scores(7)
-        weigh(0); make_mt(1, "v"); weigh(1)
-        cast_v(0, "s"); cast_v(1, "v")
-        weigh(2); quant_w(0); weigh(3); quant_v()
-        pv(0); pv(1)
-        tanh(4); tanh(5); tanh(6); tanh(7)
-        make_mt(2, "v"); quant_w(1)
-        pv(2); pv(3)
+        make_mt(0, "v"); cast_q(3, "v")
+        tanh(0); scores(4); tanh(1); scores(5)
+        weigh(0); quant_q(3); make_mt(1, "v"); weigh(1)
+        tanh(2); scores(6); tanh(3); scores(7)
+        tanh(4)
+        cast_v(0, "s"); cast_v(1, "s")
+        weigh(2); quant_w(0); weigh(3)
+        tanh(5); tanh(6); tanh(7)
+        make_mt(2, "v"); quant_v(); quant_w(1)
+        pv(0); pv(1); pv(2); pv(3)
         gate_tanh(0); gate_tanh(1); gate_tanh(2); gate_tanh(3)
         square(0); square(1)
         switch()

@@ -235,6 +235,7 @@ def tile_rows_a_tanh_mask_onorm_gate_kernel(tc, qT, kT, t, v, mask, gn, og, out)
         init()
         ld_q(0); ld_k(0); ld_k(1); ld_q(1); ld_q(2); ld_m(0); ld_q(3); ld_m(1); ld_v(); ld_m(2); ld_og(0); ld_og(1); ld_gn(); ld_og(2); ld_og(3)
         cast_q(0, "v"); quant_q(0)
+        warm_pe(20)
         cast_k(0, 0, "v"); cast_k(0, 1, "v"); quant_k(0, 0); quant_k(0, 1); quant_k(0, 2); quant_k(0, 3)
         cast_k(1, 0, "v"); cast_k(1, 1, "v"); quant_k(1, 0); quant_k(1, 1); quant_k(1, 2); quant_k(1, 3)
         scores2(0)

@@ -247,8 +247,8 @@ def tile_rows_a_tanh_mask_onorm_gate_kernel(tc, qT, kT, t, v, mask, gn, og, out)
         weigh(0); quant_q(3); make_mt(1, "v"); weigh(1)
         tanh(2); scores(6); tanh(3); scores(7)
         tanh(4)
-        cast_v(0, "s"); cast_v(1, "s")
-        weigh(2); quant_w(0); weigh(3)
+        cast_v(0, "s")
+        weigh(2); cast_v(1, "v"); quant_w(0); weigh(3)
         tanh(5); tanh(6); tanh(7)
         make_mt(2, "v"); quant_v(); quant_w(1)
         pv(0); pv(1); pv(2); pv(3)

@@ -235,7 +235,7 @@ def tile_rows_a_tanh_mask_onorm_gate_kernel(tc, qT, kT, t, v, mask, gn, og, out)
         init()
         ld_q(0); ld_k(0); ld_k(1); ld_q(1); ld_q(2); ld_m(0); ld_q(3); ld_m(1); ld_v(); ld_m(2); ld_og(0); ld_og(1); ld_gn(); ld_og(2); ld_og(3)
         cast_q(0, "v"); quant_q(0)
-        warm_pe(20)
+        warm_pe(16)
         cast_k(0, 0, "v"); cast_k(0, 1, "v"); quant_k(0, 0); quant_k(0, 1); quant_k(0, 2); quant_k(0, 3)
         cast_k(1, 0, "v"); cast_k(1, 1, "v"); quant_k(1, 0); quant_k(1, 1); quant_k(1, 2); quant_k(1, 3)
         scores2(0)

@@ -17,6 +17,13 @@ ROWS = D // PACK
 QT = 128
 TILES = NQ // QT
 UNITS = TILES * H
+HALF = N // 2
+WINDOW = HALF // PACK
+MASK_LOADS = ((0, 1), (1, 2), (2, 3), (3, 4))
+K_LOADS = ((0, 256), (256, 384), (384, 512))
+DMA_ALIGN = 256
+SPLIT_FIRST = True
+Y_PLACE = ((0, 0), (0, 1), (1, 0), (1, 1), (2, 0), (2, 1), (3, 0), (3, 1))
 FLOPS = 2 * H * N * NQ * D + 2 * H * NQ * N * E
 
 
@@ -27,236 +34,230 @@ def tile_rows_a_tanh_mask_onorm_gate_kernel(tc, qT, kT, t, v, mask, gn, og, out)
         ps = ctx.enter_context(tc.psum_pool(name="ps", bufs=1))
         ctx.enter_context(tc.manual_schedule())
 
-        def tiles(name, count, shape, dtype, pool=sb, **kw):
-            return [pool.tile(shape, dtype, name=name + str(i), **kw) for i in range(count)]
+        def tiles(name, count, shape, dtype):
+            return [sb.tile(shape, dtype, name=name + str(i), align_bytes=DMA_ALIGN) for i in range(count)]
 
-        qv = qT.rearrange("h (p j) c -> (h p) j c", j=PACK)
-        kv = kT.rearrange("h (p j) c -> (h p) j c", j=PACK)
-        mv = mask.rearrange("(s r) c -> s r c", r=PACK)
-        vv = v.rearrange("h (s r) e -> s h (r e)", r=PACK)
-        ogv = og.rearrange("h (n p) e -> n p h e", p=QT)
-        outv = out.rearrange("h (n p) e -> n p h e", p=QT)
+        def tile(name, shape, dtype):
+            return sb.tile(shape, dtype, name=name, align_bytes=DMA_ALIGN)
 
-        QCH = [[0,1],[1,2],[2,3],[3,4]]
-        QT_OF = [[0,1],[1,2],[2,3],[3,4]]
-        MCH = [[0,1],[1,2],[2,4]]
-        KCH = [[0,256],[256,512]]
-        WG = [[0,2],[2,4],[4,6],[6,8]]
-        NG = 4
-        k_raw = [sb.tile([P, PACK, b - a], F32, name="k_raw" + str(a), align_bytes=256) for a, b in KCH]
-        k_bf = tiles("k_bf", 2, [P, PACK, N // 2], BF16, align_bytes=64)
-        k_codes = sb.tile([P, N], U32, name="k_codes", align_bytes=64)
-        k_scales = sb.tile([P, N], U8, name="k_scales", align_bytes=64)
-        q_raw = [sb.tile([P, PACK, (b - a) * QT], F32, name="q_raw" + str(a), align_bytes=256) for a, b in QCH]
-        q_bf = tiles("q_bf", TILES, [P, QT * PACK], BF16, align_bytes=256)
-        q_codes = tiles("q_codes", TILES, [P, QT], U32, align_bytes=256)
-        q_scales = tiles("q_scales", TILES, [P, QT], U8, align_bytes=256)
-        m_raw = [sb.tile([P, PACK, (b - a) * QT], F32, name="m_raw" + str(a), align_bytes=256) for a, b in MCH]
-        mt = [sb.tile([P, PACK, (b - a) * QT], F32, name="mt" + str(a)) for a, b in MCH]
-        v_raw = sb.tile([P, H, PACK * E], F32, name="v_raw", align_bytes=256)
-        v_bf = sb.tile([P, H, PACK * E], BF16, name="v_bf", align_bytes=64)
-        v_codes = sb.tile([P, H * E], U32, name="v_codes", align_bytes=64)
-        v_scales = sb.tile([P, H * E], U8, name="v_scales", align_bytes=64)
-        t_sb = sb.tile([P, PACK], F32, name="t_sb")
-        gn_sb = sb.tile([P, E], F32, name="gn_sb", align_bytes=256)
-        og_sb = tiles("og_sb", NG, [P, UNITS // NG, E], F32, align_bytes=256)
-        th = tiles("th", NG, [P, UNITS // NG, E], F32)
-        gate = tiles("gate", NG, [P, UNITS // NG, E], F32)
-        p = tiles("p", UNITS, [P, PACK * QT], F32)
-        w_bf = [sb.tile([P, b - a, QT * PACK], BF16, name="w_bf" + str(a), align_bytes=64) for a, b in WG]
-        w_codes = [sb.tile([P, b - a, QT], U32, name="w_codes" + str(a), align_bytes=64) for a, b in WG]
-        w_scales = [sb.tile([P, b - a, QT], U8, name="w_scales" + str(a), align_bytes=64) for a, b in WG]
-        sq_junk = tiles("sq_junk", UNITS, [P, E], BF16)
-        ss = sb.tile([P, UNITS], F32, name="ss")
-        rms = sb.tile([P, UNITS], F32, name="rms")
-        rstd = sb.tile([P, UNITS], F32, name="rstd")
-        warm2 = sb.tile([P, 1], F32, name="warm2")
-        res = tiles("res", TILES, [P, H, E], F32, align_bytes=256)
-        one = sb.tile([P, 1], F32, name="one")
-        warm = sb.tile([P, 1], F32, name="warm")
-        sc = tiles("sc", 2 * H, [P, PACK * QT], F32, pool=ps)
-        ybank = tiles("ybank", 4, [P, 512], F32, pool=ps)
+        k_raw = [tile("k_raw" + str(a), [P, PACK, b - a], F32) for a, b in K_LOADS]
+        k_bf = tiles("k_bf", 2, [P, PACK, HALF], BF16)
+        k_codes = tile("k_codes", [P, N], U32)
+        k_scales = tile("k_scales", [P, N], U8)
+        q_raw = tiles("q_raw", TILES, [P, PACK, QT], F32)
+        q_bf = tiles("q_bf", TILES, [P, QT * PACK], BF16)
+        q_codes = tiles("q_codes", TILES, [P, QT], U32)
+        q_scales = tiles("q_scales", TILES, [P, QT], U8)
+        mask_raw = [tile("mask_raw" + str(a), [P, PACK, (b - a) * QT], F32) for a, b in MASK_LOADS]
+        mask_t = [tile("mask_t" + str(a), [P, PACK, (b - a) * QT], F32) for a, b in MASK_LOADS]
+        v_raw = tile("v_raw", [P, H, PACK * E], F32)
+        v_bf = tile("v_bf", [P, H, PACK * E], BF16)
+        v_codes = tile("v_codes", [P, H * E], U32)
+        v_scales = tile("v_scales", [P, H * E], U8)
+        t_sb = tile("t_sb", [P, PACK], F32)
+        gn_sb = tile("gn_sb", [P, E], F32)
+        og_sb = tiles("og_sb", TILES, [P, H, E], F32)
+        og_tanh = tiles("og_tanh", TILES, [P, H, E], F32)
+        gate = tiles("gate", TILES, [P, H, E], F32)
+        weights = tiles("weights", UNITS, [P, PACK * QT], F32)
+        w_bf = tiles("w_bf", TILES, [P, H, QT * PACK], BF16)
+        w_codes = tiles("w_codes", TILES, [P, H, QT], U32)
+        w_scales = tiles("w_scales", TILES, [P, H, QT], U8)
+        squares = tiles("squares", UNITS, [P, E], BF16)
+        sums = tile("sums", [P, UNITS], F32)
+        inv_rms = tile("inv_rms", [P, UNITS], F32)
+        result = tiles("result", TILES, [P, H, E], F32)
+        score_bank = [ps.tile([P, PACK * QT], F32, name="score_bank" + str(i)) for i in range(2 * H)]
+        y_bank = [ps.tile([P, PACK * QT], F32, name="y_bank" + str(i)) for i in range(TILES)]
 
-        def chunk(chs, n):
-            for i, (a, b) in enumerate(chs):
-                if a <= n < b:
-                    return i, n - a
-            raise ValueError(n)
+        def load_columns(dst, src, first, count):
+            nc.sync.dma_start(out=dst[:], in_=src[:, :, first:first + count])
 
-        def cast(eng, dst, src):
-            if eng == "v":
+        def load_q(n):
+            load_columns(q_raw[n], qT.rearrange("h (p j) c -> (h p) j c", j=PACK), n * QT, QT)
+
+        def load_k(a):
+            load_columns(k_raw[a], kT.rearrange("h (p j) c -> (h p) j c", j=PACK), K_LOADS[a][0], K_LOADS[a][1] - K_LOADS[a][0])
+
+        def load_mask(m):
+            a, b = MASK_LOADS[m]
+            load_columns(mask_raw[m], mask.rearrange("(s r) c -> s r c", r=PACK), a * QT, (b - a) * QT)
+
+        def load_og(n):
+            nc.sync.dma_start(out=og_sb[n][:], in_=og.rearrange("h (n p) e -> n p h e", p=QT)[n])
+
+        def copy(engine, dst, src):
+            if engine is nc.vector:
                 nc.vector.tensor_copy(out=dst, in_=src)
             else:
                 nc.scalar.copy(out=dst, in_=src)
 
-        def ld_k(a):
-            nc.sync.dma_start(out=k_raw[a][:], in_=kv[:, :, KCH[a][0]:KCH[a][1]])
+        def round_to_words(engine, dst, src):
+            copy(engine, dst.rearrange("p (c i j) -> p c j i", i=2, j=PACK), src.rearrange("p j (c i) -> p c j i", i=2))
 
-        def ld_q(i):
-            a, b = QCH[i]
-            nc.sync.dma_start(out=q_raw[i][:], in_=qv[:, :, a * QT:b * QT])
+        def quantize(codes, scales, src):
+            nc.vector.quantize_mx(out=codes.bitcast(FP8X4), scales=scales, in_=src)
 
-        def ld_m(i):
-            a, b = MCH[i]
-            nc.sync.dma_start(out=m_raw[i][:], in_=mv[:, :, a * QT:b * QT])
+        def round_k(engine, i, b):
+            first, last = K_LOADS[i]
+            a = first // HALF
+            window = k_bf[a][:, 2 * b:2 * b + 2, first - a * HALF:last - a * HALF]
+            copy(engine, window.rearrange("p r (s j) -> p s j r", j=PACK),
+                 k_raw[i][:].rearrange("p j (s r) -> p s j r", r=PACK)[:, :, :, 2 * b:2 * b + 2])
 
-        def ld_v():
-            nc.sync.dma_start(out=v_raw[:], in_=vv)
+        def quantize_k(a, r):
+            cols = slice(r * QT + a * WINDOW, r * QT + (a + 1) * WINDOW)
+            quantize(k_codes[:, cols], k_scales[:, cols], k_bf[a][:, r, :])
 
-        def ld_og(n):
-            nc.sync.dma_start(out=og_sb[n][:], in_=ogv[n])
+        def round_q(engine, n):
+            round_to_words(engine, q_bf[n][:], q_raw[n][:])
 
-        def ld_t():
-            nc.scalar.dma_start(out=t_sb[:], in_=t.rearrange("(s r) o -> s (r o)", r=PACK))
+        def quantize_q(n):
+            quantize(q_codes[n][:], q_scales[n][:], q_bf[n][:])
 
-        def ld_gn():
-            nc.sync.dma_start(out=gn_sb[:], in_=gn)
+        def round_v(engine, h):
+            round_to_words(engine, v_bf[:, h, :], v_raw[:, h, :].rearrange("p (j e) -> p j e", j=PACK))
 
-        def init():
-            nc.vector.memset(one[:], 1.0)
-            nc.scalar.activation(out=warm[:], in_=one[:], func=ACT.Tanh)
+        def quantize_v():
+            quantize(v_codes[:], v_scales[:], v_bf[:].rearrange("p h c -> p (h c)"))
 
-        def cast_k(a, b, eng):
-            cast(eng, k_bf[a][:, 2 * b:2 * b + 2, :].rearrange("p r (s j) -> p s j r", j=PACK),
-                 k_raw[a][:].rearrange("p j (s r) -> p s j r", r=PACK)[:, :, :, 2 * b:2 * b + 2])
-
-        def quant_k(a, r):
-            cols = slice(r * QT + a * 64, r * QT + (a + 1) * 64)
-            nc.vector.quantize_mx(out=k_codes[:, cols].bitcast(FP8X4), scales=k_scales[:, cols], in_=k_bf[a][:, r, :])
-
-        def cast_q(n, eng):
-            i, c0 = chunk(QCH, n)
-            cast(eng, q_bf[n][:].rearrange("p (c i j) -> p c j i", i=2, j=PACK),
-                 q_raw[i][:, :, c0 * QT:(c0 + 1) * QT].rearrange("p j (c i) -> p c j i", i=2))
-
-        def quant_q(n):
-            nc.vector.quantize_mx(out=q_codes[n][:].bitcast(FP8X4), scales=q_scales[n][:], in_=q_bf[n][:])
-
-        def cast_v(h, eng):
-            cast(eng, v_bf[:, h, :].rearrange("p (c i j) -> p c j i", i=2, j=PACK),
-                 v_raw[:, h, :].rearrange("p (j c i) -> p c j i", i=2, j=PACK))
-
-        def quant_v():
-            nc.vector.quantize_mx(out=v_codes[:].bitcast(FP8X4), scales=v_scales[:], in_=v_bf[:].rearrange("p h c -> p (h c)"))
-
-        def make_mt(i, eng):
-            for r in range(PACK):
-                if eng == "v":
-                    nc.vector.tensor_scalar(out=mt[i][:, r, :], in0=m_raw[i][:, r, :], scalar1=t_sb[:, r:r + 1], scalar2=None, op0=ALU.mult)
+        def scale_mask(m, rs=range(PACK), engine=None):
+            for r in rs:
+                if engine is nc.scalar:
+                    nc.scalar.activation(out=mask_t[m][:, r, :], in_=mask_raw[m][:, r, :], func=ACT.Copy, scale=t_sb[:, r:r + 1])
                 else:
-                    nc.scalar.activation(out=mt[i][:, r, :], in_=m_raw[i][:, r, :], func=ACT.Copy, scale=t_sb[:, r:r + 1])
+                    nc.vector.tensor_scalar(out=mask_t[m][:, r, :], in0=mask_raw[m][:, r, :], scalar1=t_sb[:, r:r + 1],
+                                            scalar2=None, op0=ALU.mult)
 
-        def scores(u):
+        def score_bank_of(u, r):
             n, h = divmod(u, H)
-            rows = slice(h * ROWS, (h + 1) * ROWS)
-            i, c0 = chunk(QT_OF, n)
-            qcols = slice(c0 * QT, (c0 + 1) * QT)
-            for r in range(PACK):
-                cols = slice(r * QT, (r + 1) * QT)
-                nc.tensor.matmul_mx(
-                    out=sc[2 * h + n % 2][:, cols],
-                    lhsT=k_codes[rows, cols].bitcast(FP8X4), lhsT_scale=k_scales[rows, cols],
-                    rhs=q_codes[i][rows, qcols].bitcast(FP8X4), rhs_scale=q_scales[i][rows, qcols],
-                    start=True, stop=True)
+            if SPLIT_FIRST and h == 0:
+                return score_bank[r // 2] if n == 0 else score_bank[(n + 1) % 2]
+            return score_bank[2 * h + n % 2]
 
-        def scores2(n):
-            i, c0 = chunk(QT_OF, n)
-            qcols = slice(c0 * QT, (c0 + 1) * QT)
-            for r in range(PACK):
-                cols = slice(r * QT, (r + 1) * QT)
-                for h in range(H):
-                    rows = slice(h * ROWS, (h + 1) * ROWS)
-                    nc.tensor.matmul_mx(
-                        out=sc[2 * h + n % 2][:, cols],
-                        lhsT=k_codes[rows, cols].bitcast(FP8X4), lhsT_scale=k_scales[rows, cols],
-                        rhs=q_codes[i][rows, qcols].bitcast(FP8X4), rhs_scale=q_scales[i][rows, qcols],
-                        start=True, stop=True)
-
-        def tanh(u):
+        def score_pass(u, r):
             n, h = divmod(u, H)
-            nc.scalar.activation(out=p[u][:], in_=sc[2 * h + n % 2][:], func=ACT.Tanh)
+            rows, cols = slice(h * ROWS, (h + 1) * ROWS), slice(r * QT, (r + 1) * QT)
+            nc.tensor.matmul_mx(out=score_bank_of(u, r)[:, cols],
+                                lhsT=k_codes[rows, cols].bitcast(FP8X4), lhsT_scale=k_scales[rows, cols],
+                                rhs=q_codes[n][rows, :].bitcast(FP8X4), rhs_scale=q_scales[n][rows, :],
+                                start=True, stop=True)
+
+        def scores_unit(u):
+            for r in range(PACK):
+                score_pass(u, r)
+
+        def scores_pair(ua, ub):
+            for r in range(PACK):
+                score_pass(ua, r)
+                score_pass(ub, r)
+
+        def scores_tile(n):
+            scores_pair(H * n, H * n + 1)
+
+        def tanh(u, first=0, last=PACK):
+            cols = slice(first * QT, last * QT)
+            nc.scalar.activation(out=weights[u][:, cols], in_=score_bank_of(u, first)[:, cols], func=ACT.Tanh)
+
+        def warm_up(count):
+            for i in range(count):
+                nc.tensor.matmul_mx(out=y_bank[TILES - 1][:, 3 * E:4 * E], lhsT=q_codes[0][:].bitcast(FP8X4), lhsT_scale=q_scales[0][:],
+                                    rhs=q_codes[0][:].bitcast(FP8X4), rhs_scale=q_scales[0][:], start=True, stop=True)
 
         def weigh(u):
-            i, c0 = chunk(MCH, u // H)
-            g, x = chunk(WG, u)
-            nc.vector.tensor_tensor(
-                out=w_bf[g][:, x, :].rearrange("p (c i r) -> p c r i", i=2, r=PACK),
-                in0=p[u][:].rearrange("p (r c i) -> p c r i", i=2, r=PACK),
-                in1=mt[i][:, :, c0 * QT:(c0 + 1) * QT].rearrange("p r (c i) -> p c r i", i=2),
-                op=ALU.mult)
+            n, h = divmod(u, H)
+            m = [i for i, (a, b) in enumerate(MASK_LOADS) if a <= n < b][0]
+            first = (n - MASK_LOADS[m][0]) * QT
+            nc.vector.tensor_tensor(out=w_bf[n][:, h, :].rearrange("p (c i r) -> p c r i", i=2, r=PACK),
+                                    in0=weights[u][:].rearrange("p (r c i) -> p c r i", i=2, r=PACK),
+                                    in1=mask_t[m][:, :, first:first + QT].rearrange("p r (c i) -> p c r i", i=2),
+                                    op=ALU.mult)
 
-        def quant_w(g):
-            nc.vector.quantize_mx(out=w_codes[g][:].rearrange("p u c -> p (u c)").bitcast(FP8X4), scales=w_scales[g][:].rearrange("p u c -> p (u c)"), in_=w_bf[g][:].rearrange("p u c -> p (u c)"))
+        def quantize_w(n, first=0, last=H):
+            quantize(w_codes[n][:, first:last, :].rearrange("p h c -> p (h c)"), w_scales[n][:, first:last, :].rearrange("p h c -> p (h c)"),
+                     w_bf[n][:, first:last, :].rearrange("p h c -> p (h c)"))
 
         def y_of(u):
-            return ybank[u // 2][:, (u % 2) * E:(u % 2 + 1) * E]
+            bank, place = Y_PLACE[u]
+            return y_bank[bank][:, place * E:(place + 1) * E]
 
-        def pv(u):
-            g, x = chunk(WG, u)
-            cols = slice((u % H) * E, (u % H + 1) * E)
-            nc.tensor.matmul_mx(out=y_of(u), lhsT=w_codes[g][:, x, :].bitcast(FP8X4), lhsT_scale=w_scales[g][:, x, :],
-                                rhs=v_codes[:, cols].bitcast(FP8X4), rhs_scale=v_scales[:, cols], start=True, stop=True)
+        def values(u):
+            n, h = divmod(u, H)
+            cols = slice(h * E, (h + 1) * E)
+            nc.tensor.matmul_mx(out=y_of(u),
+                                lhsT=w_codes[n][:, h, :].bitcast(FP8X4), lhsT_scale=w_scales[n][:, h, :],
+                                rhs=v_codes[:, cols].bitcast(FP8X4), rhs_scale=v_scales[:, cols],
+                                start=True, stop=True)
 
         def square(u):
-            nc.scalar.activation(out=sq_junk[u][:], in_=y_of(u), func=ACT.Square, accum_out=ss[:, u:u + 1])
+            nc.scalar.activation(out=squares[u][:], in_=y_of(u), func=ACT.Square, accum_out=sums[:, u:u + 1])
 
-        def switch():
-            nc.scalar.activation(out=warm2[:], in_=one[:], func=ACT.Abs_reciprocal_sqrt)
-
-        def root(a, b):
-            nc.scalar.activation(out=rstd[:, a:b], in_=ss[:, a:b], func=ACT.Abs_reciprocal_sqrt, scale=4.0 / E, bias=4.0 * 256.0 * 1e-5)
-
-        def recip(a, b):
-            nc.vector.reciprocal(out=rstd[:, a:b], in_=rms[:, a:b])
+        def root(first, last):
+            nc.scalar.activation(out=inv_rms[:, first:last], in_=sums[:, first:last], func=ACT.Abs_reciprocal_sqrt,
+                                 scale=4.0 / E, bias=4.0 * 256.0 * 1e-5)
 
         def gate_tanh(n):
-            nc.scalar.activation(out=th[n][:], in_=og_sb[n][:], func=ACT.Tanh, scale=0.5)
+            nc.scalar.activation(out=og_tanh[n][:], in_=og_sb[n][:], func=ACT.Tanh, scale=0.5)
 
         def gate_gain(n):
-            nc.vector.scalar_tensor_tensor(out=gate[n][:], in0=th[n][:], scalar=1.0, in1=gn_sb[:].unsqueeze(1).broadcast_to([P, UNITS // NG, E]), op0=ALU.add, op1=ALU.mult)
+            nc.vector.scalar_tensor_tensor(out=gate[n][:], in0=og_tanh[n][:], scalar=1.0,
+                                           in1=gn_sb[:].unsqueeze(1).broadcast_to([P, H, E]), op0=ALU.add, op1=ALU.mult)
 
         def finish(u):
             n, h = divmod(u, H)
-            nc.vector.scalar_tensor_tensor(out=res[n][:, h, :], in0=y_of(u), scalar=rstd[:, u:u + 1], in1=gate[n][:, h, :], op0=ALU.mult, op1=ALU.mult)
+            nc.vector.scalar_tensor_tensor(out=result[n][:, h, :], in0=y_of(u), scalar=inv_rms[:, u:u + 1],
+                                           in1=gate[n][:, h, :], op0=ALU.mult, op1=ALU.mult)
+
+        out_tiles = out.rearrange("h (n p) e -> n p h e", p=QT)
 
         def store(n):
-            nc.sync.dma_start(out=outv[n], in_=res[n][:])
+            nc.sync.dma_start(out=out_tiles[n], in_=result[n][:])
 
-        def store1(u):
+        def store_unit(u):
             n, h = divmod(u, H)
-            nc.sync.dma_start(out=outv[n][:, h, :], in_=res[n][:, h, :])
+            nc.sync.dma_start(out=out_tiles[n][:, h, :], in_=result[n][:, h, :])
 
-        def warm_pe(count):
-            for i in range(count):
-                nc.tensor.matmul_mx(out=ybank[3][:, 3 * E:4 * E], lhsT=q_codes[0][:].bitcast(FP8X4), lhsT_scale=q_scales[0][:],
-                                    rhs=q_codes[0][:].bitcast(FP8X4), rhs_scale=q_scales[0][:], start=True, stop=True)
+        def load_t():
+            nc.scalar.dma_start(out=t_sb[:], in_=t.rearrange("(s r) o -> s (r o)", r=PACK))
 
-        ld_t()
-        init()
-        ld_q(0); ld_k(0); ld_k(1); ld_q(1); ld_q(2); ld_m(0); ld_q(3); ld_m(1); ld_v(); ld_m(2); ld_og(0); ld_og(1); ld_gn(); ld_og(2); ld_og(3)
-        cast_q(0, "v"); quant_q(0)
-        warm_pe(16)
-        cast_k(0, 0, "v"); cast_k(0, 1, "v"); quant_k(0, 0); quant_k(0, 1); quant_k(0, 2); quant_k(0, 3)
-        cast_k(1, 0, "v"); cast_k(1, 1, "v"); quant_k(1, 0); quant_k(1, 1); quant_k(1, 2); quant_k(1, 3)
-        scores2(0)
-        cast_q(1, "s")
-        cast_q(2, "v"); quant_q(1); quant_q(2)
-        scores2(1)
-        make_mt(0, "v"); cast_q(3, "v")
-        tanh(0); scores(4); tanh(1); scores(5)
-        weigh(0); quant_q(3); make_mt(1, "v"); weigh(1)
-        tanh(2); scores(6); tanh(3); scores(7)
-        tanh(4)
-        cast_v(0, "s")
-        weigh(2); cast_v(1, "v"); quant_w(0); weigh(3)
-        tanh(5); tanh(6); tanh(7)
-        make_mt(2, "v"); quant_v(); quant_w(1)
-        pv(0); pv(1); pv(2); pv(3)
-        gate_tanh(0); gate_tanh(1); gate_tanh(2); gate_tanh(3)
-        square(0); square(1)
-        switch()
-        root(0, 2)
-        weigh(4); weigh(5); weigh(6); quant_w(2); weigh(7); gate_gain(0); quant_w(3); gate_gain(1)
-        pv(4); pv(5); pv(6); pv(7)
-        square(2); square(3); square(4); square(5); root(2, 4); root(4, 6); square(6); square(7); root(6, 8)
-        finish(0); finish(1); store(0); gate_gain(2); finish(2); finish(3); store(1); gate_gain(3); finish(4); finish(5); store(2); finish(6); store1(6); finish(7); store1(7)
+        def load_v():
+            nc.sync.dma_start(out=v_raw[:], in_=v.rearrange("h (s r) e -> s h (r e)", r=PACK))
+
+        def load_gn():
+            nc.sync.dma_start(out=gn_sb[:], in_=gn)
+
+        V, S = nc.vector, nc.scalar
+
+        def finish_tile(n):
+            finish(H * n)
+            finish(H * n + 1)
+            nc.sync.dma_start(out=out_tiles[n], in_=result[n][:])
+
+        load_t()
+        load_q(0); load_k(0); load_k(1); load_k(2); load_q(1); load_mask(0); load_q(2); load_q(3); load_mask(1); load_v(); load_mask(2); load_og(0); load_og(1); load_og(2); load_og(3); load_mask(3); load_gn()
+        round_q(V, 0); quantize_q(0)
+        warm_up(16)
+        round_k(V, 0, 0); round_k(V, 0, 1); quantize_k(0, 0); quantize_k(0, 1); quantize_k(0, 2); quantize_k(0, 3)
+        round_k(S, 1, 0); round_k(S, 1, 1)
+        round_k(V, 2, 0); round_k(V, 2, 1); quantize_k(1, 0); quantize_k(1, 1); quantize_k(1, 2); quantize_k(1, 3)
+        scores_tile(0)
+        round_q(V, 1); scale_mask(0, (0, 1)); quantize_q(1); scale_mask(0, (2, 3))
+        tanh(0, 0, 2); tanh(0, 2, 4)
+        scores_tile(1)
+        tanh(1)
+        round_q(V, 2); weigh(0); quantize_q(2); weigh(1)
+        scores_tile(2)
+        tanh(2); tanh(3); round_q(S, 3)
+        scale_mask(1); quantize_w(0); weigh(2); quantize_q(3)
+        scores_tile(3)
+        tanh(4); tanh(5); round_v(S, 0); gate_tanh(0); tanh(6); tanh(7)
+        round_v(V, 1); weigh(3); scale_mask(2); quantize_w(1); quantize_v(); weigh(4); weigh(5)
+        values(0); values(1); values(2); values(3)
+        gate_tanh(1); gate_tanh(2); square(0); square(1); square(2); square(3); gate_tanh(3); root(0, 4)
+        scale_mask(3); quantize_w(2)
+        values(4); values(5)
+        weigh(6); weigh(7); gate_gain(0); quantize_w(3); gate_gain(1)
+        values(6); values(7)
+        square(4); square(5); square(6); square(7); root(4, 6); root(6, 8)
+        gate_gain(2); gate_gain(3); finish_tile(0); finish_tile(1); finish_tile(2)
+        finish(6); store_unit(6); finish(7); store_unit(7)

@@ -67,6 +67,9 @@ def tile_rows_a_tanh_mask_onorm_gate_kernel(tc, qT, kT, t, v, mask, gn, og, out)
         sums = tile("sums", [P, UNITS], F32)
         inv_rms = tile("inv_rms", [P, UNITS], F32)
         result = tiles("result", TILES, [P, H, E], F32)
+        warm_bf = tile("warm_bf", [P, QT * PACK], BF16)
+        warm_codes = tile("warm_codes", [P, QT], U32)
+        warm_scales = tile("warm_scales", [P, QT], U8)
         score_bank = [ps.tile([P, PACK * QT], F32, name="score_bank" + str(i)) for i in range(2 * H)]
         y_bank = [ps.tile([P, PACK * QT], F32, name="y_bank" + str(i)) for i in range(TILES)]
 
@@ -109,14 +112,15 @@ def tile_rows_a_tanh_mask_onorm_gate_kernel(tc, qT, kT, t, v, mask, gn, og, out)
             cols = slice(r * QT + a * WINDOW, r * QT + (a + 1) * WINDOW)
             quantize(k_codes[:, cols], k_scales[:, cols], k_bf[a][:, r, :])
 
-        def round_q(engine, n):
-            round_to_words(engine, q_bf[n][:], q_raw[n][:])
+        def round_q(engine, n, first=0, last=QT):
+            round_to_words(engine, q_bf[n][:, first * PACK:last * PACK], q_raw[n][:, :, first:last])
 
         def quantize_q(n):
             quantize(q_codes[n][:], q_scales[n][:], q_bf[n][:])
 
-        def round_v(engine, h):
-            round_to_words(engine, v_bf[:, h, :], v_raw[:, h, :].rearrange("p (j e) -> p j e", j=PACK))
+        def round_v(engine, h, first=0, last=E):
+            round_to_words(engine, v_bf[:, h, first * PACK:last * PACK],
+                           v_raw[:, h, :].rearrange("p (j e) -> p j e", j=PACK)[:, :, first:last])
 
         def quantize_v():
             quantize(v_codes[:], v_scales[:], v_bf[:].rearrange("p h c -> p (h c)"))
@@ -164,6 +168,15 @@ def tile_rows_a_tanh_mask_onorm_gate_kernel(tc, qT, kT, t, v, mask, gn, og, out)
                 nc.tensor.matmul_mx(out=y_bank[TILES - 1][:, 3 * E:4 * E], lhsT=q_codes[0][:].bitcast(FP8X4), lhsT_scale=q_scales[0][:],
                                     rhs=q_codes[0][:].bitcast(FP8X4), rhs_scale=q_scales[0][:], start=True, stop=True)
 
+        def make_warm_operand():
+            nc.vector.memset(warm_bf[:], 1.0)
+            quantize(warm_codes[:], warm_scales[:], warm_bf[:])
+
+        def warm_early(count):
+            for i in range(count):
+                nc.tensor.matmul_mx(out=y_bank[TILES - 1][:, 3 * E:4 * E], lhsT=warm_codes[:].bitcast(FP8X4), lhsT_scale=warm_scales[:],
+                                    rhs=warm_codes[:].bitcast(FP8X4), rhs_scale=warm_scales[:], start=True, stop=True)
+
         def weigh(u):
             n, h = divmod(u, H)
             m = [i for i, (a, b) in enumerate(MASK_LOADS) if a <= n < b][0]
@@ -199,9 +212,13 @@ def tile_rows_a_tanh_mask_onorm_gate_kernel(tc, qT, kT, t, v, mask, gn, og, out)
         def gate_tanh(n):
             nc.scalar.activation(out=og_tanh[n][:], in_=og_sb[n][:], func=ACT.Tanh, scale=0.5)
 
-        def gate_gain(n):
-            nc.vector.scalar_tensor_tensor(out=gate[n][:], in0=og_tanh[n][:], scalar=1.0,
-                                           in1=gn_sb[:].unsqueeze(1).broadcast_to([P, H, E]), op0=ALU.add, op1=ALU.mult)
+        def gate_gain(n, first=0, last=H):
+            nc.vector.scalar_tensor_tensor(out=gate[n][:, first:last, :], in0=og_tanh[n][:, first:last, :], scalar=1.0,
+                                           in1=gn_sb[:].unsqueeze(1).broadcast_to([P, last - first, E]), op0=ALU.add, op1=ALU.mult)
+
+        def finish_store(u):
+            finish(u)
+            store_unit(u)
 
         def finish(u):
             n, h = divmod(u, H)
@@ -234,26 +251,26 @@ def tile_rows_a_tanh_mask_onorm_gate_kernel(tc, qT, kT, t, v, mask, gn, og, out)
             nc.sync.dma_start(out=out_tiles[n], in_=result[n][:])
 
         load_t()
-        load_q(0); load_k(0); load_k(1); load_k(2); load_q(1); load_mask(0); load_q(2); load_q(3); load_mask(1); load_v(); load_mask(2); load_og(0); load_og(1); load_og(2); load_og(3); load_mask(3); load_gn()
+        load_q(0); load_k(0); load_k(1); load_k(2); load_q(1); load_mask(0); load_q(2); load_mask(1); load_q(3); load_v(); load_mask(2); load_og(0); load_og(1); load_og(2); load_og(3); load_mask(3); load_gn()
         round_q(V, 0); quantize_q(0)
         warm_up(16)
         round_k(V, 0, 0); round_k(V, 0, 1); quantize_k(0, 0); quantize_k(0, 1); quantize_k(0, 2); quantize_k(0, 3)
         round_k(S, 1, 0); round_k(S, 1, 1)
         round_k(V, 2, 0); round_k(V, 2, 1); quantize_k(1, 0); quantize_k(1, 1); quantize_k(1, 2); quantize_k(1, 3)
         scores_tile(0)
-        round_q(V, 1); scale_mask(0, (0, 1)); quantize_q(1); scale_mask(0, (2, 3))
+        round_q(V, 1); quantize_q(1); scale_mask(0)
         tanh(0, 0, 2); tanh(0, 2, 4)
-        scores_tile(1)
+        scores_unit(2); scores_unit(3)
         tanh(1)
         round_q(V, 2); weigh(0); quantize_q(2); weigh(1)
-        scores_tile(2)
+        scores_unit(4); scores_unit(5)
         tanh(2); tanh(3); round_q(S, 3)
         scale_mask(1); quantize_w(0); weigh(2); quantize_q(3)
-        scores_tile(3)
+        scores_unit(6); scores_unit(7)
         tanh(4); tanh(5); round_v(S, 0); gate_tanh(0); tanh(6); tanh(7)
-        round_v(V, 1); weigh(3); scale_mask(2); quantize_w(1); quantize_v(); weigh(4); weigh(5)
+        weigh(3); round_v(V, 1); scale_mask(2); quantize_w(1); quantize_v(); weigh(4); weigh(5)
         values(0); values(1); values(2); values(3)
-        gate_tanh(1); gate_tanh(2); square(0); square(1); square(2); square(3); gate_tanh(3); root(0, 4)
+        gate_tanh(1); gate_tanh(2); gate_tanh(3); square(0); square(1); square(2); square(3); root(0, 4)
         scale_mask(3); quantize_w(2)
         values(4); values(5)
         weigh(6); weigh(7); gate_gain(0); quantize_w(3); gate_gain(1)

@@ -19,11 +19,11 @@ TILES = NQ // QT
 UNITS = TILES * H
 HALF = N // 2
 WINDOW = HALF // PACK
-MASK_LOADS = ((0, 1), (1, 2), (2, 3), (3, 4))
+MASK_LOADS = ((0, 1), (1, 2), (2, 4))
 K_LOADS = ((0, 256), (256, 384), (384, 512))
 DMA_ALIGN = 256
 SPLIT_FIRST = True
-Y_PLACE = ((0, 0), (0, 1), (1, 0), (1, 1), (2, 0), (2, 1), (3, 0), (3, 1))
+Y_PLACE = ((0, 0), (0, 1), (1, 0), (1, 1), (2, 0), (2, 1), (2, 2), (3, 0))
 FLOPS = 2 * H * N * NQ * D + 2 * H * NQ * N * E
 
 
@@ -251,30 +251,29 @@ def tile_rows_a_tanh_mask_onorm_gate_kernel(tc, qT, kT, t, v, mask, gn, og, out)
             nc.sync.dma_start(out=out_tiles[n], in_=result[n][:])
 
         load_t()
-        load_q(0); load_k(0); load_k(1); load_k(2); load_q(1); load_mask(0); load_q(2); load_mask(1); load_q(3); load_v(); load_mask(2); load_og(0); load_og(1); load_og(2); load_og(3); load_mask(3); load_gn()
+        load_q(0); load_k(0); load_k(1); load_k(2); load_q(1); load_mask(0); load_q(2); load_q(3); load_mask(1); load_v(); load_mask(2); load_og(0); load_og(1); load_og(2); load_og(3); load_gn()
         round_q(V, 0); quantize_q(0)
         warm_up(16)
         round_k(V, 0, 0); round_k(V, 0, 1); quantize_k(0, 0); quantize_k(0, 1); quantize_k(0, 2); quantize_k(0, 3)
         round_k(S, 1, 0); round_k(S, 1, 1)
         round_k(V, 2, 0); round_k(V, 2, 1); quantize_k(1, 0); quantize_k(1, 1); quantize_k(1, 2); quantize_k(1, 3)
         scores_tile(0)
-        round_q(V, 1); quantize_q(1); scale_mask(0)
+        round_q(S, 1); scale_mask(0); quantize_q(1)
         tanh(0, 0, 2); tanh(0, 2, 4)
         scores_unit(2); scores_unit(3)
-        tanh(1)
-        round_q(V, 2); weigh(0); quantize_q(2); weigh(1)
+        tanh(1); round_q(S, 3)
+        round_q(V, 2); weigh(0); quantize_q(2); weigh(1); quantize_q(3)
         scores_unit(4); scores_unit(5)
-        tanh(2); tanh(3); round_q(S, 3)
-        scale_mask(1); quantize_w(0); weigh(2); quantize_q(3)
+        tanh(2); tanh(3)
         scores_unit(6); scores_unit(7)
-        tanh(4); tanh(5); round_v(S, 0); gate_tanh(0); tanh(6); tanh(7)
-        weigh(3); round_v(V, 1); scale_mask(2); quantize_w(1); quantize_v(); weigh(4); weigh(5)
+        scale_mask(1); quantize_w(0); weigh(2); weigh(3)
+        tanh(4); tanh(5); round_v(S, 0); tanh(6); tanh(7)
+        round_v(V, 1); scale_mask(2); quantize_w(1); quantize_v(); weigh(4); weigh(5)
         values(0); values(1); values(2); values(3)
-        gate_tanh(1); gate_tanh(2); gate_tanh(3); square(0); square(1); square(2); square(3); root(0, 4)
-        scale_mask(3); quantize_w(2)
+        gate_tanh(0); gate_tanh(1); gate_tanh(2); gate_tanh(3); square(0); square(1); square(2); square(3); root(0, 4)
+        weigh(6); quantize_w(2)
         values(4); values(5)
-        weigh(6); weigh(7); gate_gain(0); quantize_w(3); gate_gain(1)
+        weigh(7); quantize_w(3, 0, 1); gate_gain(0, 0, 1); quantize_w(3, 1, 2); gate_gain(0, 1, 2); gate_gain(1)
         values(6); values(7)
         square(4); square(5); square(6); square(7); root(4, 6); root(6, 8)
-        gate_gain(2); gate_gain(3); finish_tile(0); finish_tile(1); finish_tile(2)
-        finish(6); store_unit(6); finish(7); store_unit(7)
+        gate_gain(2); gate_gain(3); finish_tile(0); finish_tile(1); finish_tile(2); finish_tile(3)

@@ -20,7 +20,7 @@ UNITS = TILES * H
 HALF = N // 2
 WINDOW = HALF // PACK
 MASK_LOADS = ((0, 1), (1, 2), (2, 4))
-K_LOADS = ((0, 256), (256, 384), (384, 512))
+K_LOADS = ((0, 256), (256, 416), (416, 512))
 DMA_ALIGN = 256
 SPLIT_FIRST = True
 Y_PLACE = ((0, 0), (0, 1), (1, 0), (1, 1), (2, 0), (2, 1), (2, 2), (3, 0))
@@ -253,7 +253,7 @@ def tile_rows_a_tanh_mask_onorm_gate_kernel(tc, qT, kT, t, v, mask, gn, og, out)
         load_t()
         load_q(0); load_k(0); load_k(1); load_k(2); load_q(1); load_mask(0); load_q(2); load_q(3); load_mask(1); load_v(); load_mask(2); load_og(0); load_og(1); load_og(2); load_og(3); load_gn()
         round_q(V, 0); quantize_q(0)
-        warm_up(16)
+        warm_up(12)
         round_k(V, 0, 0); round_k(V, 0, 1); quantize_k(0, 0); quantize_k(0, 1); quantize_k(0, 2); quantize_k(0, 3)
         round_k(S, 1, 0); round_k(S, 1, 1)
         round_k(V, 2, 0); round_k(V, 2, 1); quantize_k(1, 0); quantize_k(1, 1); quantize_k(1, 2); quantize_k(1, 3)

@@ -20,7 +20,7 @@ UNITS = TILES * H
 HALF = N // 2
 WINDOW = HALF // PACK
 MASK_LOADS = ((0, 1), (1, 2), (2, 4))
-K_LOADS = ((0, 256), (256, 416), (416, 512))
+K_LOADS = ((0, 256), (256, 384), (384, 512))
 DMA_ALIGN = 256
 SPLIT_FIRST = True
 Y_PLACE = ((0, 0), (0, 1), (1, 0), (1, 1), (2, 0), (2, 1), (2, 2), (3, 0))

@@ -251,7 +251,7 @@ def tile_rows_a_tanh_mask_onorm_gate_kernel(tc, qT, kT, t, v, mask, gn, og, out)
             nc.sync.dma_start(out=out_tiles[n], in_=result[n][:])
 
         load_t()
-        load_q(0); load_k(0); load_k(1); load_k(2); load_q(1); load_mask(0); load_q(2); load_q(3); load_mask(1); load_v(); load_mask(2); load_og(0); load_og(1); load_og(2); load_og(3); load_gn()
+        load_q(0); load_k(0); load_k(1); load_k(2); load_q(1); load_mask(0); load_q(2); load_mask(1); load_q(3); load_v(); load_mask(2); load_og(0); load_og(1); load_og(2); load_og(3); load_gn()
         round_q(V, 0); quantize_q(0)
         warm_up(12)
         round_k(V, 0, 0); round_k(V, 0, 1); quantize_k(0, 0); quantize_k(0, 1); quantize_k(0, 2); quantize_k(0, 3)
@@ -261,12 +261,12 @@ def tile_rows_a_tanh_mask_onorm_gate_kernel(tc, qT, kT, t, v, mask, gn, og, out)
         round_q(S, 1); scale_mask(0); quantize_q(1)
         tanh(0, 0, 2); tanh(0, 2, 4)
         scores_unit(2); scores_unit(3)
-        tanh(1); round_q(S, 3)
-        round_q(V, 2); weigh(0); quantize_q(2); weigh(1); quantize_q(3)
+        tanh(1); scale_mask(1, range(PACK), S)
+        round_q(V, 2); weigh(0); quantize_q(2); weigh(1); round_q(V, 3); quantize_w(0); quantize_q(3)
         scores_unit(4); scores_unit(5)
         tanh(2); tanh(3)
         scores_unit(6); scores_unit(7)
-        scale_mask(1); quantize_w(0); weigh(2); weigh(3)
+        weigh(2); weigh(3)
         tanh(4); tanh(5); round_v(S, 0); tanh(6); tanh(7)
         round_v(V, 1); scale_mask(2); quantize_w(1); quantize_v(); weigh(4); weigh(5)
         values(0); values(1); values(2); values(3)

@@ -17,13 +17,16 @@ ROWS = D // PACK
 QT = 128
 TILES = NQ // QT
 UNITS = TILES * H
+PAIRS = TILES // 2
+PAIR_UNITS = 2 * H
+LAST = TILES - 1
 HALF = N // 2
 WINDOW = HALF // PACK
-MASK_LOADS = ((0, 1), (1, 2), (2, 4))
-K_LOADS = ((0, 256), (256, 384), (384, 512))
+K_LOADS = ((0, HALF), (HALF, 3 * N // 4), (3 * N // 4, N))
+MASK_LOADS = ((0, 1), (1, 2), (2, TILES))
+Y_PLACES = [divmod(u, H) for u in range(UNITS - 2)] + [(LAST - 1, H), (LAST, 0)]
+WARM_UP_PASSES = 12
 DMA_ALIGN = 256
-SPLIT_FIRST = True
-Y_PLACE = ((0, 0), (0, 1), (1, 0), (1, 1), (2, 0), (2, 1), (2, 2), (3, 0))
 FLOPS = 2 * H * N * NQ * D + 2 * H * NQ * N * E
 
 
@@ -56,9 +59,9 @@ def tile_rows_a_tanh_mask_onorm_gate_kernel(tc, qT, kT, t, v, mask, gn, og, out)
         v_scales = tile("v_scales", [P, H * E], U8)
         t_sb = tile("t_sb", [P, PACK], F32)
         gn_sb = tile("gn_sb", [P, E], F32)
-        og_sb = tiles("og_sb", TILES, [P, H, E], F32)
-        og_tanh = tiles("og_tanh", TILES, [P, H, E], F32)
-        gate = tiles("gate", TILES, [P, H, E], F32)
+        og_sb = tiles("og_sb", PAIRS, [P, PAIR_UNITS, E], F32)
+        og_tanh = tiles("og_tanh", PAIRS, [P, PAIR_UNITS, E], F32)
+        gate = tiles("gate", PAIRS, [P, PAIR_UNITS, E], F32)
         weights = tiles("weights", UNITS, [P, PACK * QT], F32)
         w_bf = tiles("w_bf", TILES, [P, H, QT * PACK], BF16)
         w_codes = tiles("w_codes", TILES, [P, H, QT], U32)
@@ -67,27 +70,25 @@ def tile_rows_a_tanh_mask_onorm_gate_kernel(tc, qT, kT, t, v, mask, gn, og, out)
         sums = tile("sums", [P, UNITS], F32)
         inv_rms = tile("inv_rms", [P, UNITS], F32)
         result = tiles("result", TILES, [P, H, E], F32)
-        warm_bf = tile("warm_bf", [P, QT * PACK], BF16)
-        warm_codes = tile("warm_codes", [P, QT], U32)
-        warm_scales = tile("warm_scales", [P, QT], U8)
         score_bank = [ps.tile([P, PACK * QT], F32, name="score_bank" + str(i)) for i in range(2 * H)]
         y_bank = [ps.tile([P, PACK * QT], F32, name="y_bank" + str(i)) for i in range(TILES)]
 
-        def load_columns(dst, src, first, count):
-            nc.sync.dma_start(out=dst[:], in_=src[:, :, first:first + count])
+        def load_columns(dst, src, first, last):
+            nc.sync.dma_start(out=dst[:], in_=src[:, :, first:last])
 
         def load_q(n):
-            load_columns(q_raw[n], qT.rearrange("h (p j) c -> (h p) j c", j=PACK), n * QT, QT)
+            load_columns(q_raw[n], qT.rearrange("h (p j) c -> (h p) j c", j=PACK), n * QT, (n + 1) * QT)
 
-        def load_k(a):
-            load_columns(k_raw[a], kT.rearrange("h (p j) c -> (h p) j c", j=PACK), K_LOADS[a][0], K_LOADS[a][1] - K_LOADS[a][0])
+        def load_k(i):
+            load_columns(k_raw[i], kT.rearrange("h (p j) c -> (h p) j c", j=PACK), *K_LOADS[i])
 
         def load_mask(m):
             a, b = MASK_LOADS[m]
-            load_columns(mask_raw[m], mask.rearrange("(s r) c -> s r c", r=PACK), a * QT, (b - a) * QT)
+            load_columns(mask_raw[m], mask.rearrange("(s r) c -> s r c", r=PACK), a * QT, b * QT)
 
         def load_og(n):
-            nc.sync.dma_start(out=og_sb[n][:], in_=og.rearrange("h (n p) e -> n p h e", p=QT)[n])
+            pair, first = divmod(H * n, PAIR_UNITS)
+            nc.sync.dma_start(out=og_sb[pair][:, first:first + H, :], in_=og.rearrange("h (n p) e -> n p h e", p=QT)[n])
 
         def copy(engine, dst, src):
             if engine is nc.vector:
@@ -101,43 +102,50 @@ def tile_rows_a_tanh_mask_onorm_gate_kernel(tc, qT, kT, t, v, mask, gn, og, out)
         def quantize(codes, scales, src):
             nc.vector.quantize_mx(out=codes.bitcast(FP8X4), scales=scales, in_=src)
 
-        def round_k(engine, i, b):
+        def round_k(engine, i):
             first, last = K_LOADS[i]
-            a = first // HALF
-            window = k_bf[a][:, 2 * b:2 * b + 2, first - a * HALF:last - a * HALF]
-            copy(engine, window.rearrange("p r (s j) -> p s j r", j=PACK),
-                 k_raw[i][:].rearrange("p j (s r) -> p s j r", r=PACK)[:, :, :, 2 * b:2 * b + 2])
+            half = first // HALF
+            for r in (0, 2):
+                window = k_bf[half][:, r:r + 2, first - half * HALF:last - half * HALF]
+                copy(engine, window.rearrange("p r (s j) -> p s j r", j=PACK),
+                     k_raw[i][:].rearrange("p j (s r) -> p s j r", r=PACK)[:, :, :, r:r + 2])
 
-        def quantize_k(a, r):
-            cols = slice(r * QT + a * WINDOW, r * QT + (a + 1) * WINDOW)
-            quantize(k_codes[:, cols], k_scales[:, cols], k_bf[a][:, r, :])
+        def quantize_k(half):
+            for r in range(PACK):
+                cols = slice(r * QT + half * WINDOW, r * QT + (half + 1) * WINDOW)
+                quantize(k_codes[:, cols], k_scales[:, cols], k_bf[half][:, r, :])
 
-        def round_q(engine, n, first=0, last=QT):
-            round_to_words(engine, q_bf[n][:, first * PACK:last * PACK], q_raw[n][:, :, first:last])
+        def round_q(engine, n):
+            round_to_words(engine, q_bf[n][:], q_raw[n][:])
 
         def quantize_q(n):
             quantize(q_codes[n][:], q_scales[n][:], q_bf[n][:])
 
-        def round_v(engine, h, first=0, last=E):
-            round_to_words(engine, v_bf[:, h, first * PACK:last * PACK],
-                           v_raw[:, h, :].rearrange("p (j e) -> p j e", j=PACK)[:, :, first:last])
+        def round_v(engine, h):
+            round_to_words(engine, v_bf[:, h, :], v_raw[:, h, :].rearrange("p (j e) -> p j e", j=PACK))
 
         def quantize_v():
             quantize(v_codes[:], v_scales[:], v_bf[:].rearrange("p h c -> p (h c)"))
 
-        def scale_mask(m, rs=range(PACK), engine=None):
-            for r in rs:
-                if engine is nc.scalar:
-                    nc.scalar.activation(out=mask_t[m][:, r, :], in_=mask_raw[m][:, r, :], func=ACT.Copy, scale=t_sb[:, r:r + 1])
+        def scale_mask(engine, m):
+            for r in range(PACK):
+                dst, src, scale = mask_t[m][:, r, :], mask_raw[m][:, r, :], t_sb[:, r:r + 1]
+                if engine is nc.vector:
+                    nc.vector.tensor_scalar(out=dst, in0=src, scalar1=scale, scalar2=None, op0=ALU.mult)
                 else:
-                    nc.vector.tensor_scalar(out=mask_t[m][:, r, :], in0=mask_raw[m][:, r, :], scalar1=t_sb[:, r:r + 1],
-                                            scalar2=None, op0=ALU.mult)
+                    nc.scalar.activation(out=dst, in_=src, func=ACT.Copy, scale=scale)
+
+        def warm_up():
+            for i in range(WARM_UP_PASSES):
+                nc.tensor.matmul_mx(out=y_bank[LAST][:, (PACK - 1) * E:PACK * E],
+                                    lhsT=q_codes[0][:].bitcast(FP8X4), lhsT_scale=q_scales[0][:],
+                                    rhs=q_codes[0][:].bitcast(FP8X4), rhs_scale=q_scales[0][:], start=True, stop=True)
 
         def score_bank_of(u, r):
             n, h = divmod(u, H)
-            if SPLIT_FIRST and h == 0:
-                return score_bank[r // 2] if n == 0 else score_bank[(n + 1) % 2]
-            return score_bank[2 * h + n % 2]
+            if u == 0:
+                return score_bank[r // 2]
+            return score_bank[2 * h + (n + 1 - h) % 2]
 
         def score_pass(u, r):
             n, h = divmod(u, H)
@@ -147,35 +155,14 @@ def tile_rows_a_tanh_mask_onorm_gate_kernel(tc, qT, kT, t, v, mask, gn, og, out)
                                 rhs=q_codes[n][rows, :].bitcast(FP8X4), rhs_scale=q_scales[n][rows, :],
                                 start=True, stop=True)
 
-        def scores_unit(u):
-            for r in range(PACK):
-                score_pass(u, r)
-
-        def scores_pair(ua, ub):
-            for r in range(PACK):
-                score_pass(ua, r)
-                score_pass(ub, r)
-
-        def scores_tile(n):
-            scores_pair(H * n, H * n + 1)
+        def scores(n):
+            for u in (H * n, H * n + 1):
+                for r in range(PACK):
+                    score_pass(u, r)
 
         def tanh(u, first=0, last=PACK):
             cols = slice(first * QT, last * QT)
             nc.scalar.activation(out=weights[u][:, cols], in_=score_bank_of(u, first)[:, cols], func=ACT.Tanh)
-
-        def warm_up(count):
-            for i in range(count):
-                nc.tensor.matmul_mx(out=y_bank[TILES - 1][:, 3 * E:4 * E], lhsT=q_codes[0][:].bitcast(FP8X4), lhsT_scale=q_scales[0][:],
-                                    rhs=q_codes[0][:].bitcast(FP8X4), rhs_scale=q_scales[0][:], start=True, stop=True)
-
-        def make_warm_operand():
-            nc.vector.memset(warm_bf[:], 1.0)
-            quantize(warm_codes[:], warm_scales[:], warm_bf[:])
-
-        def warm_early(count):
-            for i in range(count):
-                nc.tensor.matmul_mx(out=y_bank[TILES - 1][:, 3 * E:4 * E], lhsT=warm_codes[:].bitcast(FP8X4), lhsT_scale=warm_scales[:],
-                                    rhs=warm_codes[:].bitcast(FP8X4), rhs_scale=warm_scales[:], start=True, stop=True)
 
         def weigh(u):
             n, h = divmod(u, H)
@@ -187,93 +174,129 @@ def tile_rows_a_tanh_mask_onorm_gate_kernel(tc, qT, kT, t, v, mask, gn, og, out)
                                     op=ALU.mult)
 
         def quantize_w(n, first=0, last=H):
-            quantize(w_codes[n][:, first:last, :].rearrange("p h c -> p (h c)"), w_scales[n][:, first:last, :].rearrange("p h c -> p (h c)"),
+            quantize(w_codes[n][:, first:last, :].rearrange("p h c -> p (h c)"),
+                     w_scales[n][:, first:last, :].rearrange("p h c -> p (h c)"),
                      w_bf[n][:, first:last, :].rearrange("p h c -> p (h c)"))
 
         def y_of(u):
-            bank, place = Y_PLACE[u]
+            bank, place = Y_PLACES[u]
             return y_bank[bank][:, place * E:(place + 1) * E]
 
-        def values(u):
-            n, h = divmod(u, H)
-            cols = slice(h * E, (h + 1) * E)
-            nc.tensor.matmul_mx(out=y_of(u),
-                                lhsT=w_codes[n][:, h, :].bitcast(FP8X4), lhsT_scale=w_scales[n][:, h, :],
-                                rhs=v_codes[:, cols].bitcast(FP8X4), rhs_scale=v_scales[:, cols],
-                                start=True, stop=True)
+        def values(n):
+            for h in range(H):
+                cols = slice(h * E, (h + 1) * E)
+                nc.tensor.matmul_mx(out=y_of(H * n + h),
+                                    lhsT=w_codes[n][:, h, :].bitcast(FP8X4), lhsT_scale=w_scales[n][:, h, :],
+                                    rhs=v_codes[:, cols].bitcast(FP8X4), rhs_scale=v_scales[:, cols],
+                                    start=True, stop=True)
 
-        def square(u):
-            nc.scalar.activation(out=squares[u][:], in_=y_of(u), func=ACT.Square, accum_out=sums[:, u:u + 1])
+        def sum_squares(n):
+            for u in (H * n, H * n + 1):
+                nc.scalar.activation(out=squares[u][:], in_=y_of(u), func=ACT.Square, accum_out=sums[:, u:u + 1])
 
-        def root(first, last):
-            nc.scalar.activation(out=inv_rms[:, first:last], in_=sums[:, first:last], func=ACT.Abs_reciprocal_sqrt,
+        def inverse_rms(first, last):
+            cols = slice(H * first, H * last)
+            nc.scalar.activation(out=inv_rms[:, cols], in_=sums[:, cols], func=ACT.Abs_reciprocal_sqrt,
                                  scale=4.0 / E, bias=4.0 * 256.0 * 1e-5)
 
-        def gate_tanh(n):
-            nc.scalar.activation(out=og_tanh[n][:], in_=og_sb[n][:], func=ACT.Tanh, scale=0.5)
+        def gate_tanh(pair):
+            nc.scalar.activation(out=og_tanh[pair][:], in_=og_sb[pair][:], func=ACT.Tanh, scale=0.5)
 
-        def gate_gain(n, first=0, last=H):
-            nc.vector.scalar_tensor_tensor(out=gate[n][:, first:last, :], in0=og_tanh[n][:, first:last, :], scalar=1.0,
-                                           in1=gn_sb[:].unsqueeze(1).broadcast_to([P, last - first, E]), op0=ALU.add, op1=ALU.mult)
+        def gate_gain(pair, first=0, last=PAIR_UNITS):
+            nc.vector.scalar_tensor_tensor(out=gate[pair][:, first:last, :], in0=og_tanh[pair][:, first:last, :], scalar=1.0,
+                                           in1=gn_sb[:].unsqueeze(1).broadcast_to([P, last - first, E]),
+                                           op0=ALU.add, op1=ALU.mult)
 
-        def finish_store(u):
-            finish(u)
-            store_unit(u)
+        def finish(n):
+            for h in range(H):
+                u = H * n + h
+                nc.vector.scalar_tensor_tensor(out=result[n][:, h, :], in0=y_of(u), scalar=inv_rms[:, u:u + 1],
+                                               in1=gate[u // PAIR_UNITS][:, u % PAIR_UNITS, :], op0=ALU.mult, op1=ALU.mult)
+            nc.sync.dma_start(out=out.rearrange("h (n p) e -> n p h e", p=QT)[n], in_=result[n][:])
 
-        def finish(u):
-            n, h = divmod(u, H)
-            nc.vector.scalar_tensor_tensor(out=result[n][:, h, :], in0=y_of(u), scalar=inv_rms[:, u:u + 1],
-                                           in1=gate[n][:, h, :], op0=ALU.mult, op1=ALU.mult)
+        nc.scalar.dma_start(out=t_sb[:], in_=t.rearrange("(s r) o -> s (r o)", r=PACK))
+        load_q(0)
+        for i in range(len(K_LOADS)):
+            load_k(i)
+        load_q(1)
+        load_mask(0)
+        load_q(2)
+        load_mask(1)
+        load_q(3)
+        nc.sync.dma_start(out=v_raw[:], in_=v.rearrange("h (s r) e -> s h (r e)", r=PACK))
+        load_mask(2)
+        for n in range(TILES):
+            load_og(n)
+        nc.sync.dma_start(out=gn_sb[:], in_=gn)
 
-        out_tiles = out.rearrange("h (n p) e -> n p h e", p=QT)
+        round_q(nc.vector, 0)
+        quantize_q(0)
+        warm_up()
+        round_k(nc.vector, 0)
+        quantize_k(0)
+        round_k(nc.scalar, 1)
+        round_k(nc.vector, 2)
+        quantize_k(1)
+        for r in range(PACK):
+            for h in range(H):
+                score_pass(h, r)
 
-        def store(n):
-            nc.sync.dma_start(out=out_tiles[n], in_=result[n][:])
+        round_q(nc.scalar, 1)
+        scale_mask(nc.vector, 0)
+        quantize_q(1)
+        tanh(0, 0, 2)
+        tanh(0, 2, PACK)
+        scores(1)
+        tanh(1)
+        scale_mask(nc.scalar, 1)
+        round_q(nc.vector, 2)
+        weigh(0)
+        quantize_q(2)
+        weigh(1)
+        round_q(nc.vector, 3)
+        quantize_w(0)
+        quantize_q(3)
+        scores(2)
+        tanh(2)
+        tanh(3)
+        scores(3)
+        weigh(2)
+        weigh(3)
 
-        def store_unit(u):
-            n, h = divmod(u, H)
-            nc.sync.dma_start(out=out_tiles[n][:, h, :], in_=result[n][:, h, :])
+        tanh(4)
+        tanh(5)
+        round_v(nc.scalar, 0)
+        tanh(6)
+        tanh(7)
+        round_v(nc.vector, 1)
+        scale_mask(nc.vector, 2)
+        quantize_w(1)
+        quantize_v()
+        weigh(4)
+        weigh(5)
+        values(0)
+        values(1)
 
-        def load_t():
-            nc.scalar.dma_start(out=t_sb[:], in_=t.rearrange("(s r) o -> s (r o)", r=PACK))
+        for pair in range(PAIRS):
+            gate_tanh(pair)
+        sum_squares(0)
+        sum_squares(1)
+        inverse_rms(0, 2)
 
-        def load_v():
-            nc.sync.dma_start(out=v_raw[:], in_=v.rearrange("h (s r) e -> s h (r e)", r=PACK))
+        weigh(6)
+        quantize_w(2)
+        values(2)
+        weigh(7)
+        quantize_w(LAST, 0, 1)
+        gate_gain(0, 0, 1)
+        quantize_w(LAST, 1, H)
+        gate_gain(0, 1, PAIR_UNITS)
+        values(LAST)
+        sum_squares(2)
+        sum_squares(LAST)
+        inverse_rms(2, LAST)
+        inverse_rms(LAST, TILES)
 
-        def load_gn():
-            nc.sync.dma_start(out=gn_sb[:], in_=gn)
-
-        V, S = nc.vector, nc.scalar
-
-        def finish_tile(n):
-            finish(H * n)
-            finish(H * n + 1)
-            nc.sync.dma_start(out=out_tiles[n], in_=result[n][:])
-
-        load_t()
-        load_q(0); load_k(0); load_k(1); load_k(2); load_q(1); load_mask(0); load_q(2); load_mask(1); load_q(3); load_v(); load_mask(2); load_og(0); load_og(1); load_og(2); load_og(3); load_gn()
-        round_q(V, 0); quantize_q(0)
-        warm_up(12)
-        round_k(V, 0, 0); round_k(V, 0, 1); quantize_k(0, 0); quantize_k(0, 1); quantize_k(0, 2); quantize_k(0, 3)
-        round_k(S, 1, 0); round_k(S, 1, 1)
-        round_k(V, 2, 0); round_k(V, 2, 1); quantize_k(1, 0); quantize_k(1, 1); quantize_k(1, 2); quantize_k(1, 3)
-        scores_tile(0)
-        round_q(S, 1); scale_mask(0); quantize_q(1)
-        tanh(0, 0, 2); tanh(0, 2, 4)
-        scores_unit(2); scores_unit(3)
-        tanh(1); scale_mask(1, range(PACK), S)
-        round_q(V, 2); weigh(0); quantize_q(2); weigh(1); round_q(V, 3); quantize_w(0); quantize_q(3)
-        scores_unit(4); scores_unit(5)
-        tanh(2); tanh(3)
-        scores_unit(6); scores_unit(7)
-        weigh(2); weigh(3)
-        tanh(4); tanh(5); round_v(S, 0); tanh(6); tanh(7)
-        round_v(V, 1); scale_mask(2); quantize_w(1); quantize_v(); weigh(4); weigh(5)
-        values(0); values(1); values(2); values(3)
-        gate_tanh(0); gate_tanh(1); gate_tanh(2); gate_tanh(3); square(0); square(1); square(2); square(3); root(0, 4)
-        weigh(6); quantize_w(2)
-        values(4); values(5)
-        weigh(7); quantize_w(3, 0, 1); gate_gain(0, 0, 1); quantize_w(3, 1, 2); gate_gain(0, 1, 2); gate_gain(1)
-        values(6); values(7)
-        square(4); square(5); square(6); square(7); root(4, 6); root(6, 8)
-        gate_gain(2); gate_gain(3); finish_tile(0); finish_tile(1); finish_tile(2); finish_tile(3)
+        gate_gain(1)
+        for n in range(TILES):
+            finish(n)

@@ -97,7 +97,7 @@ def tile_rows_a_tanh_mask_onorm_gate_kernel(tc, qT, kT, t, v, mask, gn, og, out)
                 nc.scalar.copy(out=dst, in_=src)
 
         def round_to_words(engine, dst, src):
-            copy(engine, dst.rearrange("p (c i j) -> p c j i", i=2, j=PACK), src.rearrange("p j (c i) -> p c j i", i=2))
+            copy(engine, dst.rearrange("p (c i j) -> p c j i", i=4, j=PACK), src.rearrange("p j (c i) -> p c j i", i=4))
 
         def quantize(codes, scales, src):
             nc.vector.quantize_mx(out=codes.bitcast(FP8X4), scales=scales, in_=src)

@@ -25,7 +25,6 @@ WINDOW = HALF // PACK
 K_LOADS = ((0, HALF), (HALF, 3 * N // 4), (3 * N // 4, N))
 MASK_LOADS = ((0, 1), (1, 2), (2, TILES))
 Y_PLACES = [divmod(u, H) for u in range(UNITS - 2)] + [(LAST - 1, H), (LAST, 0)]
-WARM_UP_PASSES = 12
 DMA_ALIGN = 256
 FLOPS = 2 * H * N * NQ * D + 2 * H * NQ * N * E
 
@@ -135,12 +134,6 @@ def tile_rows_a_tanh_mask_onorm_gate_kernel(tc, qT, kT, t, v, mask, gn, og, out)
                 else:
                     nc.scalar.activation(out=dst, in_=src, func=ACT.Copy, scale=scale)
 
-        def warm_up():
-            for i in range(WARM_UP_PASSES):
-                nc.tensor.matmul_mx(out=y_bank[LAST][:, (PACK - 1) * E:PACK * E],
-                                    lhsT=q_codes[0][:].bitcast(FP8X4), lhsT_scale=q_scales[0][:],
-                                    rhs=q_codes[0][:].bitcast(FP8X4), rhs_scale=q_scales[0][:], start=True, stop=True)
-
         def score_bank_of(u, r):
             n, h = divmod(u, H)
             if u == 0:
@@ -231,7 +224,6 @@ def tile_rows_a_tanh_mask_onorm_gate_kernel(tc, qT, kT, t, v, mask, gn, og, out)
 
         round_q(nc.vector, 0)
         quantize_q(0)
-        warm_up()
         round_k(nc.vector, 0)
         quantize_k(0)
         round_k(nc.scalar, 1)

@@ -52,7 +52,7 @@ def tile_rows_a_tanh_mask_onorm_gate_kernel(tc, qT, kT, t, v, mask, gn, og, out)
         q_scales = tiles("q_scales", TILES, [P, QT], U8)
         mask_raw = [tile("mask_raw" + str(a), [P, PACK, (b - a) * QT], F32) for a, b in MASK_LOADS]
         mask_t = [tile("mask_t" + str(a), [P, PACK, (b - a) * QT], F32) for a, b in MASK_LOADS]
-        v_raw = tile("v_raw", [P, H, PACK * E], F32)
+        v_raw = tiles("v_raw", H, [P, PACK * E], F32)
         v_bf = tile("v_bf", [P, H, PACK * E], BF16)
         v_codes = tile("v_codes", [P, H * E], U32)
         v_scales = tile("v_scales", [P, H * E], U8)
@@ -121,7 +121,7 @@ def tile_rows_a_tanh_mask_onorm_gate_kernel(tc, qT, kT, t, v, mask, gn, og, out)
             quantize(q_codes[n][:], q_scales[n][:], q_bf[n][:])
 
         def round_v(engine, h):
-            round_to_words(engine, v_bf[:, h, :], v_raw[:, h, :].rearrange("p (j e) -> p j e", j=PACK))
+            round_to_words(engine, v_bf[:, h, :], v_raw[h][:].rearrange("p (j e) -> p j e", j=PACK))
 
         def quantize_v():
             quantize(v_codes[:], v_scales[:], v_bf[:].rearrange("p h c -> p (h c)"))
@@ -216,7 +216,8 @@ def tile_rows_a_tanh_mask_onorm_gate_kernel(tc, qT, kT, t, v, mask, gn, og, out)
         load_q(2)
         load_mask(1)
         load_q(3)
-        nc.sync.dma_start(out=v_raw[:], in_=v.rearrange("h (s r) e -> s h (r e)", r=PACK))
+        for h in range(H):
+            nc.sync.dma_start(out=v_raw[h][:], in_=v.rearrange("h (s r) e -> h s (r e)", r=PACK)[h])
         load_mask(2)
         for n in range(TILES):
             load_og(n)

@@ -205,7 +205,10 @@ def tile_rows_a_tanh_mask_onorm_gate_kernel(tc, qT, kT, t, v, mask, gn, og, out)
                 u = H * n + h
                 nc.vector.scalar_tensor_tensor(out=result[n][:, h, :], in0=y_of(u), scalar=inv_rms[:, u:u + 1],
                                                in1=gate[u // PAIR_UNITS][:, u % PAIR_UNITS, :], op0=ALU.mult, op1=ALU.mult)
-            nc.sync.dma_start(out=out.rearrange("h (n p) e -> n p h e", p=QT)[n], in_=result[n][:])
+                if n == LAST:
+                    nc.sync.dma_start(out=out[h, n * QT:(n + 1) * QT, :], in_=result[n][:, h, :])
+            if n < LAST:
+                nc.sync.dma_start(out=out.rearrange("h (n p) e -> n p h e", p=QT)[n], in_=result[n][:])
 
         nc.scalar.dma_start(out=t_sb[:], in_=t.rearrange("(s r) o -> s (r o)", r=PACK))
         load_q(0)

@@ -228,6 +228,9 @@ def tile_rows_a_tanh_mask_onorm_gate_kernel(tc, qT, kT, t, v, mask, gn, og, out)
 
         round_q(nc.vector, 0)
         quantize_q(0)
+        for i in range(12):
+            nc.tensor.matmul_mx(out=y_bank[LAST][:, E:2 * E], lhsT=q_codes[0][:].bitcast(FP8X4), lhsT_scale=q_scales[0][:],
+                                rhs=q_codes[0][:].bitcast(FP8X4), rhs_scale=q_scales[0][:], start=True, stop=True)
         round_k(nc.vector, 0)
         quantize_k(0)
         round_k(nc.scalar, 1)

@@ -183,8 +183,8 @@ def tile_rows_a_tanh_mask_onorm_gate_kernel(tc, qT, kT, t, v, mask, gn, og, out)
                                     rhs=v_codes[:, cols].bitcast(FP8X4), rhs_scale=v_scales[:, cols],
                                     start=True, stop=True)
 
-        def sum_squares(n):
-            for u in (H * n, H * n + 1):
+        def sum_squares(first, last):
+            for u in range(first, last):
                 nc.scalar.activation(out=squares[u][:], in_=y_of(u), func=ACT.Square, accum_out=sums[:, u:u + 1])
 
         def inverse_rms(first, last):
@@ -278,8 +278,7 @@ def tile_rows_a_tanh_mask_onorm_gate_kernel(tc, qT, kT, t, v, mask, gn, og, out)
 
         for pair in range(PAIRS):
             gate_tanh(pair)
-        sum_squares(0)
-        sum_squares(1)
+        sum_squares(0, 4)
         inverse_rms(0, 2)
 
         weigh(6)
@@ -291,9 +290,9 @@ def tile_rows_a_tanh_mask_onorm_gate_kernel(tc, qT, kT, t, v, mask, gn, og, out)
         quantize_w(LAST, 1, H)
         gate_gain(0, 1, PAIR_UNITS)
         values(LAST)
-        sum_squares(2)
-        sum_squares(LAST)
+        sum_squares(4, 7)
         inverse_rms(2, LAST)
+        sum_squares(7, 8)
         inverse_rms(LAST, TILES)
 
         gate_gain(1)

@@ -104,10 +104,13 @@ def tile_rows_a_tanh_mask_onorm_gate_kernel(tc, qT, kT, t, v, mask, gn, og, out)
         def round_k(engine, i):
             first, last = K_LOADS[i]
             half = first // HALF
-            for r in (0, 2):
-                window = k_bf[half][:, r:r + 2, first - half * HALF:last - half * HALF]
-                copy(engine, window.rearrange("p r (s j) -> p s j r", j=PACK),
-                     k_raw[i][:].rearrange("p j (s r) -> p s j r", r=PACK)[:, :, :, r:r + 2])
+            window = k_bf[half][:, :, first - half * HALF:last - half * HALF].rearrange("p (g r) (s j) -> p g s j r", r=2, j=PACK)
+            source = k_raw[i][:].rearrange("p j (s g r) -> p g s j r", g=2, r=2)
+            if engine is nc.scalar:
+                copy(engine, window, source)
+            else:
+                for g in range(2):
+                    copy(engine, window[:, g], source[:, g])
 
         def quantize_k(half):
             for r in range(PACK):

@@ -191,7 +191,7 @@ def tile_rows_a_tanh_mask_onorm_gate_kernel(tc, qT, kT, t, v, mask, gn, og, out)
                 nc.scalar.activation(out=squares[u][:], in_=y_of(u), func=ACT.Square, accum_out=sums[:, u:u + 1])
 
         def inverse_rms(first, last):
-            cols = slice(H * first, H * last)
+            cols = slice(first, last)
             nc.scalar.activation(out=inv_rms[:, cols], in_=sums[:, cols], func=ACT.Abs_reciprocal_sqrt,
                                  scale=4.0 / E, bias=4.0 * 256.0 * 1e-5)
 
@@ -282,7 +282,7 @@ def tile_rows_a_tanh_mask_onorm_gate_kernel(tc, qT, kT, t, v, mask, gn, og, out)
         for pair in range(PAIRS):
             gate_tanh(pair)
         sum_squares(0, 4)
-        inverse_rms(0, 2)
+        inverse_rms(0, 4)
 
         weigh(6)
         quantize_w(2)
@@ -294,9 +294,10 @@ def tile_rows_a_tanh_mask_onorm_gate_kernel(tc, qT, kT, t, v, mask, gn, og, out)
         gate_gain(0, 1, PAIR_UNITS)
         values(LAST)
         sum_squares(4, 7)
-        inverse_rms(2, LAST)
+        inverse_rms(4, 6)
         sum_squares(7, 8)
-        inverse_rms(LAST, TILES)
+        inverse_rms(6, 7)
+        inverse_rms(7, 8)
 
         gate_gain(1)
         for n in range(TILES):

@@ -129,8 +129,8 @@ def tile_rows_a_tanh_mask_onorm_gate_kernel(tc, qT, kT, t, v, mask, gn, og, out)
         def quantize_v():
             quantize(v_codes[:], v_scales[:], v_bf[:].rearrange("p h c -> p (h c)"))
 
-        def scale_mask(engine, m):
-            for r in range(PACK):
+        def scale_mask(engine, m, rows=range(PACK)):
+            for r in rows:
                 dst, src, scale = mask_t[m][:, r, :], mask_raw[m][:, r, :], t_sb[:, r:r + 1]
                 if engine is nc.vector:
                     nc.vector.tensor_scalar(out=dst, in0=src, scalar1=scale, scalar2=None, op0=ALU.mult)
@@ -193,15 +193,14 @@ def tile_rows_a_tanh_mask_onorm_gate_kernel(tc, qT, kT, t, v, mask, gn, og, out)
         def inverse_rms(first, last):
             cols = slice(first, last)
             nc.scalar.activation(out=inv_rms[:, cols], in_=sums[:, cols], func=ACT.Abs_reciprocal_sqrt,
-                                 scale=4.0 / E, bias=4.0 * 256.0 * 1e-5)
+                                 scale=1.0 / E, bias=256.0 * 1e-5)
 
         def gate_tanh(pair):
-            nc.scalar.activation(out=og_tanh[pair][:], in_=og_sb[pair][:], func=ACT.Tanh, scale=0.5)
+            nc.scalar.activation(out=og_tanh[pair][:], in_=og_sb[pair][:], func=ACT.Sigmoid)
 
-        def gate_gain(pair, first=0, last=PAIR_UNITS):
-            nc.vector.scalar_tensor_tensor(out=gate[pair][:, first:last, :], in0=og_tanh[pair][:, first:last, :], scalar=1.0,
-                                           in1=gn_sb[:].unsqueeze(1).broadcast_to([P, last - first, E]),
-                                           op0=ALU.add, op1=ALU.mult)
+        def gate_gain(pair, first=0, last=PAIR_UNITS, engine=nc.vector):
+            engine.tensor_tensor(out=gate[pair][:, first:last, :], in0=og_tanh[pair][:, first:last, :],
+                                 in1=gn_sb[:].unsqueeze(1).broadcast_to([P, last - first, E]), op=ALU.mult)
 
         def finish(n):
             for h in range(H):
@@ -229,6 +228,8 @@ def tile_rows_a_tanh_mask_onorm_gate_kernel(tc, qT, kT, t, v, mask, gn, og, out)
             load_og(n)
         nc.sync.dma_start(out=gn_sb[:], in_=gn)
 
+        table_probe = tile("table_probe", [P, 1], F32)
+        nc.scalar.activation(out=table_probe[:], in_=t_sb[:, 0:1], func=ACT.Sigmoid)
         round_q(nc.vector, 0)
         quantize_q(0)
         for i in range(12):
@@ -250,12 +251,13 @@ def tile_rows_a_tanh_mask_onorm_gate_kernel(tc, qT, kT, t, v, mask, gn, og, out)
         tanh(0, 2, PACK)
         scores(1)
         tanh(1)
-        scale_mask(nc.scalar, 1)
+        scale_mask(nc.scalar, 1, range(3))
         round_q(nc.vector, 2)
         weigh(0)
         quantize_q(2)
         weigh(1)
         round_q(nc.vector, 3)
+        scale_mask(nc.vector, 1, (3,))
         quantize_w(0)
         quantize_q(3)
         scores(2)
@@ -281,6 +283,7 @@ def tile_rows_a_tanh_mask_onorm_gate_kernel(tc, qT, kT, t, v, mask, gn, og, out)
 
         for pair in range(PAIRS):
             gate_tanh(pair)
+        gate_gain(1, 2, 4, nc.gpsimd)
         sum_squares(0, 4)
         inverse_rms(0, 4)
 
@@ -299,6 +302,6 @@ def tile_rows_a_tanh_mask_onorm_gate_kernel(tc, qT, kT, t, v, mask, gn, og, out)
         inverse_rms(6, 7)
         inverse_rms(7, 8)
 
-        gate_gain(1)
+        gate_gain(1, 0, 2)
         for n in range(TILES):
             finish(n)

@@ -72,6 +72,11 @@ def tile_rows_a_tanh_mask_onorm_gate_kernel(tc, qT, kT, t, v, mask, gn, og, out)
         score_bank = [ps.tile([P, PACK * QT], F32, name="score_bank" + str(i)) for i in range(2 * H)]
         y_bank = [ps.tile([P, PACK * QT], F32, name="y_bank" + str(i)) for i in range(TILES)]
 
+        last_gate = w_bf[LAST][:, 1, :].bitcast(F32).rearrange("p (h e) -> p h e", h=H)
+
+        def gate_of(u):
+            return last_gate[:, u % H, :] if u // H == LAST else gate[u // PAIR_UNITS][:, u % PAIR_UNITS, :]
+
         def load_columns(dst, src, first, last):
             nc.sync.dma_start(out=dst[:], in_=src[:, :, first:last])
 
@@ -206,7 +211,7 @@ def tile_rows_a_tanh_mask_onorm_gate_kernel(tc, qT, kT, t, v, mask, gn, og, out)
             for h in range(H):
                 u = H * n + h
                 nc.vector.scalar_tensor_tensor(out=result[n][:, h, :], in0=y_of(u), scalar=inv_rms[:, u:u + 1],
-                                               in1=gate[u // PAIR_UNITS][:, u % PAIR_UNITS, :], op0=ALU.mult, op1=ALU.mult)
+                                               in1=gate_of(u), op0=ALU.mult, op1=ALU.mult)
                 if n == LAST:
                     nc.sync.dma_start(out=out[h, n * QT:(n + 1) * QT, :], in_=result[n][:, h, :])
             if n < LAST:
@@ -283,7 +288,6 @@ def tile_rows_a_tanh_mask_onorm_gate_kernel(tc, qT, kT, t, v, mask, gn, og, out)
 
         for pair in range(PAIRS):
             gate_tanh(pair)
-        gate_gain(1, 2, 4, nc.gpsimd)
         sum_squares(0, 4)
         inverse_rms(0, 4)
 
@@ -294,6 +298,7 @@ def tile_rows_a_tanh_mask_onorm_gate_kernel(tc, qT, kT, t, v, mask, gn, og, out)
         quantize_w(LAST, 0, 1)
         gate_gain(0, 0, 1)
         quantize_w(LAST, 1, H)
+        nc.gpsimd.tensor_tensor(out=last_gate, in0=og_tanh[1][:, H:, :], in1=gn_sb[:].unsqueeze(1).broadcast_to([P, H, E]), op=ALU.mult)
         gate_gain(0, 1, PAIR_UNITS)
         values(LAST)
         sum_squares(4, 7)

@@ -272,9 +272,9 @@ def tile_rows_a_tanh_mask_onorm_gate_kernel(tc, qT, kT, t, v, mask, gn, og, out)
         weigh(2)
         weigh(3)
 
+        round_v(nc.scalar, 0)
         tanh(4)
         tanh(5)
-        round_v(nc.scalar, 0)
         tanh(6)
         tanh(7)
         round_v(nc.vector, 1)

@@ -58,9 +58,9 @@ def tile_rows_a_tanh_mask_onorm_gate_kernel(tc, qT, kT, t, v, mask, gn, og, out)
         v_scales = tile("v_scales", [P, H * E], U8)
         t_sb = tile("t_sb", [P, PACK], F32)
         gn_sb = tile("gn_sb", [P, E], F32)
-        og_sb = tiles("og_sb", PAIRS, [P, PAIR_UNITS, E], F32)
-        og_tanh = tiles("og_tanh", PAIRS, [P, PAIR_UNITS, E], F32)
-        gate = tiles("gate", PAIRS, [P, PAIR_UNITS, E], F32)
+        og_sb = tiles("og_sb", H, [P, TILES, E], F32)
+        sigmoid = tile("sigmoid", [P, H, TILES, E], F32)
+        gate = tile("gate", [P, H, TILES, E], F32)
         weights = tiles("weights", UNITS, [P, PACK * QT], F32)
         w_bf = tiles("w_bf", TILES, [P, H, QT * PACK], BF16)
         w_codes = tiles("w_codes", TILES, [P, H, QT], U32)
@@ -75,7 +75,7 @@ def tile_rows_a_tanh_mask_onorm_gate_kernel(tc, qT, kT, t, v, mask, gn, og, out)
         last_gate = w_bf[LAST][:, 1, :].bitcast(F32).rearrange("p (h e) -> p h e", h=H)
 
         def gate_of(u):
-            return last_gate[:, u % H, :] if u // H == LAST else gate[u // PAIR_UNITS][:, u % PAIR_UNITS, :]
+            return last_gate[:, u % H, :] if u // H == LAST else gate[:, u % H, u // H, :]
 
         def load_columns(dst, src, first, last):
             nc.sync.dma_start(out=dst[:], in_=src[:, :, first:last])
@@ -90,9 +90,8 @@ def tile_rows_a_tanh_mask_onorm_gate_kernel(tc, qT, kT, t, v, mask, gn, og, out)
             a, b = MASK_LOADS[m]
             load_columns(mask_raw[m], mask.rearrange("(s r) c -> s r c", r=PACK), a * QT, b * QT)
 
-        def load_og(n):
-            pair, first = divmod(H * n, PAIR_UNITS)
-            nc.sync.dma_start(out=og_sb[pair][:, first:first + H, :], in_=og.rearrange("h (n p) e -> n p h e", p=QT)[n])
+        def load_og(h):
+            nc.sync.dma_start(out=og_sb[h][:], in_=og.rearrange("h (n p) e -> h p n e", p=QT)[h])
 
         def copy(engine, dst, src):
             if engine is nc.vector:
@@ -200,12 +199,13 @@ def tile_rows_a_tanh_mask_onorm_gate_kernel(tc, qT, kT, t, v, mask, gn, og, out)
             nc.scalar.activation(out=inv_rms[:, cols], in_=sums[:, cols], func=ACT.Abs_reciprocal_sqrt,
                                  scale=1.0 / E, bias=256.0 * 1e-5)
 
-        def gate_tanh(pair):
-            nc.scalar.activation(out=og_tanh[pair][:], in_=og_sb[pair][:], func=ACT.Sigmoid)
+        def gate_tanh(h):
+            nc.scalar.activation(out=sigmoid[:, h], in_=og_sb[h][:], func=ACT.Sigmoid)
 
-        def gate_gain(pair, first=0, last=PAIR_UNITS, engine=nc.vector):
-            engine.tensor_tensor(out=gate[pair][:, first:last, :], in0=og_tanh[pair][:, first:last, :],
-                                 in1=gn_sb[:].unsqueeze(1).broadcast_to([P, last - first, E]), op=ALU.mult)
+        def gate_gain(heads, first, last):
+            shape = [P, heads.stop - heads.start, last - first, E]
+            nc.vector.tensor_tensor(out=gate[:, heads, first:last, :], in0=sigmoid[:, heads, first:last, :],
+                                    in1=gn_sb[:].unsqueeze(1).unsqueeze(1).broadcast_to(shape), op=ALU.mult)
 
         def finish(n):
             for h in range(H):
@@ -228,10 +228,12 @@ def tile_rows_a_tanh_mask_onorm_gate_kernel(tc, qT, kT, t, v, mask, gn, og, out)
         load_q(3)
         for h in range(H):
             nc.sync.dma_start(out=v_raw[h][:], in_=v.rearrange("h (s r) e -> h s (r e)", r=PACK)[h])
-        load_mask(2)
-        for n in range(TILES):
-            load_og(n)
-        nc.sync.dma_start(out=gn_sb[:], in_=gn)
+        for n in range(2, TILES):
+            nc.sync.dma_start(out=mask_raw[2][:, :, (n - 2) * QT:(n - 1) * QT], in_=mask.rearrange("(s r) c -> s r c", r=PACK)[:, :, n * QT:(n + 1) * QT])
+        for h in range(H):
+            load_og(h)
+        for h in range(H):
+            nc.sync.dma_start(out=gn_sb[h * ROWS:(h + 1) * ROWS, :], in_=gn[h * ROWS:(h + 1) * ROWS, :])
 
         table_probe = tile("table_probe", [P, 1], F32)
         nc.scalar.activation(out=table_probe[:], in_=t_sb[:, 0:1], func=ACT.Sigmoid)
@@ -256,13 +258,12 @@ def tile_rows_a_tanh_mask_onorm_gate_kernel(tc, qT, kT, t, v, mask, gn, og, out)
         tanh(0, 2, PACK)
         scores(1)
         tanh(1)
-        scale_mask(nc.scalar, 1, range(3))
+        scale_mask(nc.scalar, 1)
         round_q(nc.vector, 2)
         weigh(0)
         quantize_q(2)
         weigh(1)
         round_q(nc.vector, 3)
-        scale_mask(nc.vector, 1, (3,))
         quantize_w(0)
         quantize_q(3)
         scores(2)
@@ -286,8 +287,8 @@ def tile_rows_a_tanh_mask_onorm_gate_kernel(tc, qT, kT, t, v, mask, gn, og, out)
         values(0)
         values(1)
 
-        for pair in range(PAIRS):
-            gate_tanh(pair)
+        for h in range(H):
+            gate_tanh(h)
         sum_squares(0, 4)
         inverse_rms(0, 4)
 
@@ -296,10 +297,10 @@ def tile_rows_a_tanh_mask_onorm_gate_kernel(tc, qT, kT, t, v, mask, gn, og, out)
         values(2)
         weigh(7)
         quantize_w(LAST, 0, 1)
-        gate_gain(0, 0, 1)
+        gate_gain(slice(0, 1), 0, 1)
         quantize_w(LAST, 1, H)
-        nc.gpsimd.tensor_tensor(out=last_gate, in0=og_tanh[1][:, H:, :], in1=gn_sb[:].unsqueeze(1).broadcast_to([P, H, E]), op=ALU.mult)
-        gate_gain(0, 1, PAIR_UNITS)
+        nc.gpsimd.tensor_tensor(out=last_gate, in0=sigmoid[:, :, LAST, :], in1=gn_sb[:].unsqueeze(1).broadcast_to([P, H, E]), op=ALU.mult)
+        gate_gain(slice(1, 2), 0, 1)
         values(LAST)
         sum_squares(4, 7)
         inverse_rms(4, 6)
@@ -307,6 +308,6 @@ def tile_rows_a_tanh_mask_onorm_gate_kernel(tc, qT, kT, t, v, mask, gn, og, out)
         inverse_rms(6, 7)
         inverse_rms(7, 8)
 
-        gate_gain(1, 0, 2)
+        gate_gain(slice(0, H), 1, LAST)
         for n in range(TILES):
             finish(n)

@@ -224,12 +224,12 @@ def tile_rows_a_tanh_mask_onorm_gate_kernel(tc, qT, kT, t, v, mask, gn, og, out)
         load_q(1)
         load_mask(0)
         load_q(2)
-        load_mask(1)
+        for rows in (slice(0, 2), slice(2, PACK)):
+            nc.sync.dma_start(out=mask_raw[1][:, rows, :], in_=mask.rearrange("(s r) c -> s r c", r=PACK)[:, rows, QT:2 * QT])
         load_q(3)
         for h in range(H):
             nc.sync.dma_start(out=v_raw[h][:], in_=v.rearrange("h (s r) e -> h s (r e)", r=PACK)[h])
-        for n in range(2, TILES):
-            nc.sync.dma_start(out=mask_raw[2][:, :, (n - 2) * QT:(n - 1) * QT], in_=mask.rearrange("(s r) c -> s r c", r=PACK)[:, :, n * QT:(n + 1) * QT])
+        load_mask(2)
         for h in range(H):
             load_og(h)
         for h in range(H):
@@ -258,8 +258,9 @@ def tile_rows_a_tanh_mask_onorm_gate_kernel(tc, qT, kT, t, v, mask, gn, og, out)
         tanh(0, 2, PACK)
         scores(1)
         tanh(1)
-        scale_mask(nc.scalar, 1)
+        scale_mask(nc.scalar, 1, (2, 3))
         round_q(nc.vector, 2)
+        scale_mask(nc.vector, 1, (0, 1))
         weigh(0)
         quantize_q(2)
         weigh(1)

@@ -90,6 +90,9 @@ def tile_rows_a_tanh_mask_onorm_gate_kernel(tc, qT, kT, t, v, mask, gn, og, out)
             a, b = MASK_LOADS[m]
             load_columns(mask_raw[m], mask.rearrange("(s r) c -> s r c", r=PACK), a * QT, b * QT)
 
+        def load_mask_rows(n, rows):
+            nc.sync.dma_start(out=mask_raw[n][:, rows, :], in_=mask.rearrange("(s r) c -> s r c", r=PACK)[:, rows, n * QT:(n + 1) * QT])
+
         def load_og(h):
             nc.sync.dma_start(out=og_sb[h][:], in_=og.rearrange("h (n p) e -> h p n e", p=QT)[h])
 
@@ -222,18 +225,18 @@ def tile_rows_a_tanh_mask_onorm_gate_kernel(tc, qT, kT, t, v, mask, gn, og, out)
         for i in range(len(K_LOADS)):
             load_k(i)
         load_q(1)
-        load_mask(0)
+        load_mask_rows(0, slice(0, 2))
         load_q(2)
-        for rows in (slice(0, 2), slice(2, PACK)):
-            nc.sync.dma_start(out=mask_raw[1][:, rows, :], in_=mask.rearrange("(s r) c -> s r c", r=PACK)[:, rows, QT:2 * QT])
+        load_mask_rows(0, slice(2, PACK))
+        load_mask_rows(1, slice(0, 2))
+        load_mask_rows(1, slice(2, PACK))
         load_q(3)
         for h in range(H):
             nc.sync.dma_start(out=v_raw[h][:], in_=v.rearrange("h (s r) e -> h s (r e)", r=PACK)[h])
         load_mask(2)
         for h in range(H):
             load_og(h)
-        for h in range(H):
-            nc.sync.dma_start(out=gn_sb[h * ROWS:(h + 1) * ROWS, :], in_=gn[h * ROWS:(h + 1) * ROWS, :])
+        nc.sync.dma_start(out=gn_sb[:], in_=gn)
 
         table_probe = tile("table_probe", [P, 1], F32)
         nc.scalar.activation(out=table_probe[:], in_=t_sb[:, 0:1], func=ACT.Sigmoid)
@@ -252,7 +255,7 @@ def tile_rows_a_tanh_mask_onorm_gate_kernel(tc, qT, kT, t, v, mask, gn, og, out)
                 score_pass(h, r)
 
         round_q(nc.scalar, 1)
-        scale_mask(nc.vector, 0)
+        scale_mask(nc.vector, 0, (0, 1))
         quantize_q(1)
         tanh(0, 0, 2)
         tanh(0, 2, PACK)
@@ -260,9 +263,10 @@ def tile_rows_a_tanh_mask_onorm_gate_kernel(tc, qT, kT, t, v, mask, gn, og, out)
         tanh(1)
         scale_mask(nc.scalar, 1, (2, 3))
         round_q(nc.vector, 2)
+        scale_mask(nc.vector, 0, (2, 3))
         scale_mask(nc.vector, 1, (0, 1))
-        weigh(0)
         quantize_q(2)
+        weigh(0)
         weigh(1)
         round_q(nc.vector, 3)
         quantize_w(0)

@@ -225,8 +225,8 @@ def tile_rows_a_tanh_mask_onorm_gate_kernel(tc, qT, kT, t, v, mask, gn, og, out)
         for i in range(len(K_LOADS)):
             load_k(i)
         load_q(1)
-        load_mask_rows(0, slice(0, 2))
         load_q(2)
+        load_mask_rows(0, slice(0, 2))
         load_mask_rows(0, slice(2, PACK))
         load_mask_rows(1, slice(0, 2))
         load_mask_rows(1, slice(2, PACK))
@@ -255,17 +255,16 @@ def tile_rows_a_tanh_mask_onorm_gate_kernel(tc, qT, kT, t, v, mask, gn, og, out)
                 score_pass(h, r)
 
         round_q(nc.scalar, 1)
-        scale_mask(nc.vector, 0, (0, 1))
+        round_q(nc.vector, 2)
         quantize_q(1)
         tanh(0, 0, 2)
         tanh(0, 2, PACK)
         scores(1)
         tanh(1)
         scale_mask(nc.scalar, 1, (2, 3))
-        round_q(nc.vector, 2)
-        scale_mask(nc.vector, 0, (2, 3))
-        scale_mask(nc.vector, 1, (0, 1))
+        scale_mask(nc.vector, 0)
         quantize_q(2)
+        scale_mask(nc.vector, 1, (0, 1))
         weigh(0)
         weigh(1)
         round_q(nc.vector, 3)

@@ -77,6 +77,10 @@ def tile_rows_a_tanh_mask_onorm_gate_kernel(tc, qT, kT, t, v, mask, gn, og, out)
         def gate_of(u):
             return last_gate[:, u % H, :] if u // H == LAST else gate[:, u % H, u // H, :]
 
+        ones = tile("ones", [P, QT * PACK], BF16)
+        ones_codes = tile("ones_codes", [P, QT], U32)
+        ones_scales = tile("ones_scales", [P, QT], U8)
+
         def load_columns(dst, src, first, last):
             nc.sync.dma_start(out=dst[:], in_=src[:, :, first:last])
 
@@ -240,11 +244,13 @@ def tile_rows_a_tanh_mask_onorm_gate_kernel(tc, qT, kT, t, v, mask, gn, og, out)
 
         table_probe = tile("table_probe", [P, 1], F32)
         nc.scalar.activation(out=table_probe[:], in_=t_sb[:, 0:1], func=ACT.Sigmoid)
+        nc.vector.memset(ones[:], 1.0)
+        quantize(ones_codes[:], ones_scales[:], ones[:])
+        for i in range(32):
+            nc.tensor.matmul_mx(out=y_bank[LAST][:, E:2 * E], lhsT=ones_codes[:].bitcast(FP8X4), lhsT_scale=ones_scales[:],
+                                rhs=ones_codes[:].bitcast(FP8X4), rhs_scale=ones_scales[:], start=True, stop=True)
         round_q(nc.vector, 0)
         quantize_q(0)
-        for i in range(12):
-            nc.tensor.matmul_mx(out=y_bank[LAST][:, E:2 * E], lhsT=q_codes[0][:].bitcast(FP8X4), lhsT_scale=q_scales[0][:],
-                                rhs=q_codes[0][:].bitcast(FP8X4), rhs_scale=q_scales[0][:], start=True, stop=True)
         round_k(nc.vector, 0)
         quantize_k(0)
         round_k(nc.scalar, 1)

@@ -290,8 +290,8 @@ def tile_rows_a_tanh_mask_onorm_gate_kernel(tc, qT, kT, t, v, mask, gn, og, out)
         tanh(7)
         round_v(nc.vector, 1)
         scale_mask(nc.vector, 2)
-        quantize_w(1)
         quantize_v()
+        quantize_w(1)
         weigh(4)
         weigh(5)
         values(0)

@@ -59,8 +59,8 @@ def tile_rows_a_tanh_mask_onorm_gate_kernel(tc, qT, kT, t, v, mask, gn, og, out)
         t_sb = tile("t_sb", [P, PACK], F32)
         gn_sb = tile("gn_sb", [P, E], F32)
         og_sb = tiles("og_sb", H, [P, TILES, E], F32)
-        sigmoid = tile("sigmoid", [P, H, TILES, E], F32)
-        gate = tile("gate", [P, H, TILES, E], F32)
+        sigmoid = tile("sigmoid", [P, UNITS, E], F32)
+        gate = tile("gate", [P, UNITS, E], F32)
         weights = tiles("weights", UNITS, [P, PACK * QT], F32)
         w_bf = tiles("w_bf", TILES, [P, H, QT * PACK], BF16)
         w_codes = tiles("w_codes", TILES, [P, H, QT], U32)
@@ -75,7 +75,7 @@ def tile_rows_a_tanh_mask_onorm_gate_kernel(tc, qT, kT, t, v, mask, gn, og, out)
         last_gate = w_bf[LAST][:, 1, :].bitcast(F32).rearrange("p (h e) -> p h e", h=H)
 
         def gate_of(u):
-            return last_gate[:, u % H, :] if u // H == LAST else gate[:, u % H, u // H, :]
+            return last_gate[:, u % H, :] if u // H == LAST else gate[:, u, :]
 
         ones = tile("ones", [P, QT * PACK], BF16)
         ones_codes = tile("ones_codes", [P, QT], U32)
@@ -207,12 +207,11 @@ def tile_rows_a_tanh_mask_onorm_gate_kernel(tc, qT, kT, t, v, mask, gn, og, out)
                                  scale=1.0 / E, bias=256.0 * 1e-5)
 
         def gate_tanh(h):
-            nc.scalar.activation(out=sigmoid[:, h], in_=og_sb[h][:], func=ACT.Sigmoid)
+            nc.scalar.activation(out=sigmoid[:, h::H, :], in_=og_sb[h][:], func=ACT.Sigmoid)
 
-        def gate_gain(heads, first, last):
-            shape = [P, heads.stop - heads.start, last - first, E]
-            nc.vector.tensor_tensor(out=gate[:, heads, first:last, :], in0=sigmoid[:, heads, first:last, :],
-                                    in1=gn_sb[:].unsqueeze(1).unsqueeze(1).broadcast_to(shape), op=ALU.mult)
+        def gate_gain(first, last):
+            nc.vector.tensor_tensor(out=gate[:, first:last, :], in0=sigmoid[:, first:last, :],
+                                    in1=gn_sb[:].unsqueeze(1).broadcast_to([P, last - first, E]), op=ALU.mult)
 
         def finish(n):
             for h in range(H):
@@ -307,10 +306,10 @@ def tile_rows_a_tanh_mask_onorm_gate_kernel(tc, qT, kT, t, v, mask, gn, og, out)
         values(2)
         weigh(7)
         quantize_w(LAST, 0, 1)
-        gate_gain(slice(0, 1), 0, 1)
+        gate_gain(0, 1)
         quantize_w(LAST, 1, H)
-        nc.gpsimd.tensor_tensor(out=last_gate, in0=sigmoid[:, :, LAST, :], in1=gn_sb[:].unsqueeze(1).broadcast_to([P, H, E]), op=ALU.mult)
-        gate_gain(slice(1, 2), 0, 1)
+        nc.gpsimd.tensor_tensor(out=last_gate, in0=sigmoid[:, H * LAST:, :], in1=gn_sb[:].unsqueeze(1).broadcast_to([P, H, E]), op=ALU.mult)
+        gate_gain(1, H)
         values(LAST)
         sum_squares(4, 7)
         inverse_rms(4, 6)
@@ -318,6 +317,6 @@ def tile_rows_a_tanh_mask_onorm_gate_kernel(tc, qT, kT, t, v, mask, gn, og, out)
         inverse_rms(6, 7)
         inverse_rms(7, 8)
 
-        gate_gain(slice(0, H), 1, LAST)
+        gate_gain(H, H * LAST)
         for n in range(TILES):
             finish(n)

@@ -77,10 +77,6 @@ def tile_rows_a_tanh_mask_onorm_gate_kernel(tc, qT, kT, t, v, mask, gn, og, out)
         def gate_of(u):
             return last_gate[:, u % H, :] if u // H == LAST else gate[:, u, :]
 
-        ones = tile("ones", [P, QT * PACK], BF16)
-        ones_codes = tile("ones_codes", [P, QT], U32)
-        ones_scales = tile("ones_scales", [P, QT], U8)
-
         def load_columns(dst, src, first, last):
             nc.sync.dma_start(out=dst[:], in_=src[:, :, first:last])
 
@@ -243,13 +239,11 @@ def tile_rows_a_tanh_mask_onorm_gate_kernel(tc, qT, kT, t, v, mask, gn, og, out)
 
         table_probe = tile("table_probe", [P, 1], F32)
         nc.scalar.activation(out=table_probe[:], in_=t_sb[:, 0:1], func=ACT.Sigmoid)
-        nc.vector.memset(ones[:], 1.0)
-        quantize(ones_codes[:], ones_scales[:], ones[:])
-        for i in range(32):
-            nc.tensor.matmul_mx(out=y_bank[LAST][:, E:2 * E], lhsT=ones_codes[:].bitcast(FP8X4), lhsT_scale=ones_scales[:],
-                                rhs=ones_codes[:].bitcast(FP8X4), rhs_scale=ones_scales[:], start=True, stop=True)
         round_q(nc.vector, 0)
         quantize_q(0)
+        for i in range(12):
+            nc.tensor.matmul_mx(out=y_bank[LAST][:, E:2 * E], lhsT=q_codes[0][:].bitcast(FP8X4), lhsT_scale=q_scales[0][:],
+                                rhs=q_codes[0][:].bitcast(FP8X4), rhs_scale=q_scales[0][:], start=True, stop=True)
         round_k(nc.vector, 0)
         quantize_k(0)
         round_k(nc.scalar, 1)

@@ -260,13 +260,14 @@ def tile_rows_a_tanh_mask_onorm_gate_kernel(tc, qT, kT, t, v, mask, gn, og, out)
         tanh(0, 2, PACK)
         scores(1)
         tanh(1)
-        scale_mask(nc.scalar, 1, (2, 3))
+        scale_mask(nc.scalar, 1, (3,))
         scale_mask(nc.vector, 0)
         quantize_q(2)
         scale_mask(nc.vector, 1, (0, 1))
         weigh(0)
         weigh(1)
         round_q(nc.vector, 3)
+        scale_mask(nc.vector, 1, (2,))
         quantize_w(0)
         quantize_q(3)
         scores(2)

@@ -17,13 +17,13 @@ ROWS = D // PACK
 QT = 128
 TILES = NQ // QT
 UNITS = TILES * H
-PAIRS = TILES // 2
-PAIR_UNITS = 2 * H
 LAST = TILES - 1
 HALF = N // 2
 WINDOW = HALF // PACK
 K_LOADS = ((0, HALF), (HALF, 3 * N // 4), (3 * N // 4, N))
-MASK_LOADS = ((0, 1), (1, 2), (2, TILES))
+MASK_PARTS = ((0, 1), (1, 2), (2, TILES))
+ROW_HALVES = (slice(0, PACK // 2), slice(PACK // 2, PACK))
+WARM_UP_PASSES = 12
 Y_PLACES = [divmod(u, H) for u in range(UNITS - 2)] + [(LAST - 1, H), (LAST, 0)]
 DMA_ALIGN = 256
 FLOPS = 2 * H * N * NQ * D + 2 * H * NQ * N * E
@@ -50,9 +50,9 @@ def tile_rows_a_tanh_mask_onorm_gate_kernel(tc, qT, kT, t, v, mask, gn, og, out)
         q_bf = tiles("q_bf", TILES, [P, QT * PACK], BF16)
         q_codes = tiles("q_codes", TILES, [P, QT], U32)
         q_scales = tiles("q_scales", TILES, [P, QT], U8)
-        mask_raw = [tile("mask_raw" + str(a), [P, PACK, (b - a) * QT], F32) for a, b in MASK_LOADS]
-        mask_t = [tile("mask_t" + str(a), [P, PACK, (b - a) * QT], F32) for a, b in MASK_LOADS]
-        v_raw = tiles("v_raw", H, [P, PACK * E], F32)
+        mask_raw = [tile("mask_raw" + str(a), [P, PACK, (b - a) * QT], F32) for a, b in MASK_PARTS]
+        mask_t = [tile("mask_t" + str(a), [P, PACK, (b - a) * QT], F32) for a, b in MASK_PARTS]
+        v_raw = tile("v_raw", [P, H, PACK * E], F32)
         v_bf = tile("v_bf", [P, H, PACK * E], BF16)
         v_codes = tile("v_codes", [P, H * E], U32)
         v_scales = tile("v_scales", [P, H * E], U8)
@@ -69,10 +69,11 @@ def tile_rows_a_tanh_mask_onorm_gate_kernel(tc, qT, kT, t, v, mask, gn, og, out)
         sums = tile("sums", [P, UNITS], F32)
         inv_rms = tile("inv_rms", [P, UNITS], F32)
         result = tiles("result", TILES, [P, H, E], F32)
+        table_probe = tile("table_probe", [P, 1], F32)
         score_bank = [ps.tile([P, PACK * QT], F32, name="score_bank" + str(i)) for i in range(2 * H)]
         y_bank = [ps.tile([P, PACK * QT], F32, name="y_bank" + str(i)) for i in range(TILES)]
 
-        last_gate = w_bf[LAST][:, 1, :].bitcast(F32).rearrange("p (h e) -> p h e", h=H)
+        last_gate = w_bf[LAST][:, H - 1, :].bitcast(F32).rearrange("p (h e) -> p h e", h=H)
 
         def gate_of(u):
             return last_gate[:, u % H, :] if u // H == LAST else gate[:, u, :]
@@ -86,12 +87,9 @@ def tile_rows_a_tanh_mask_onorm_gate_kernel(tc, qT, kT, t, v, mask, gn, og, out)
         def load_k(i):
             load_columns(k_raw[i], kT.rearrange("h (p j) c -> (h p) j c", j=PACK), *K_LOADS[i])
 
-        def load_mask(m):
-            a, b = MASK_LOADS[m]
-            load_columns(mask_raw[m], mask.rearrange("(s r) c -> s r c", r=PACK), a * QT, b * QT)
-
-        def load_mask_rows(n, rows):
-            nc.sync.dma_start(out=mask_raw[n][:, rows, :], in_=mask.rearrange("(s r) c -> s r c", r=PACK)[:, rows, n * QT:(n + 1) * QT])
+        def load_mask(m, rows=slice(0, PACK)):
+            a, b = MASK_PARTS[m]
+            nc.sync.dma_start(out=mask_raw[m][:, rows, :], in_=mask.rearrange("(s r) c -> s r c", r=PACK)[:, rows, a * QT:b * QT])
 
         def load_og(h):
             nc.sync.dma_start(out=og_sb[h][:], in_=og.rearrange("h (n p) e -> h p n e", p=QT)[h])
@@ -131,7 +129,7 @@ def tile_rows_a_tanh_mask_onorm_gate_kernel(tc, qT, kT, t, v, mask, gn, og, out)
             quantize(q_codes[n][:], q_scales[n][:], q_bf[n][:])
 
         def round_v(engine, h):
-            round_to_words(engine, v_bf[:, h, :], v_raw[h][:].rearrange("p (j e) -> p j e", j=PACK))
+            round_to_words(engine, v_bf[:, h, :], v_raw[:, h, :].rearrange("p (j e) -> p j e", j=PACK))
 
         def quantize_v():
             quantize(v_codes[:], v_scales[:], v_bf[:].rearrange("p h c -> p (h c)"))
@@ -169,8 +167,8 @@ def tile_rows_a_tanh_mask_onorm_gate_kernel(tc, qT, kT, t, v, mask, gn, og, out)
 
         def weigh(u):
             n, h = divmod(u, H)
-            m = [i for i, (a, b) in enumerate(MASK_LOADS) if a <= n < b][0]
-            first = (n - MASK_LOADS[m][0]) * QT
+            m = [i for i, (a, b) in enumerate(MASK_PARTS) if a <= n < b][0]
+            first = (n - MASK_PARTS[m][0]) * QT
             nc.vector.tensor_tensor(out=w_bf[n][:, h, :].rearrange("p (c i r) -> p c r i", i=2, r=PACK),
                                     in0=weights[u][:].rearrange("p (r c i) -> p c r i", i=2, r=PACK),
                                     in1=mask_t[m][:, :, first:first + QT].rearrange("p r (c i) -> p c r i", i=2),
@@ -202,12 +200,15 @@ def tile_rows_a_tanh_mask_onorm_gate_kernel(tc, qT, kT, t, v, mask, gn, og, out)
             nc.scalar.activation(out=inv_rms[:, cols], in_=sums[:, cols], func=ACT.Abs_reciprocal_sqrt,
                                  scale=1.0 / E, bias=256.0 * 1e-5)
 
-        def gate_tanh(h):
+        def gate_sigmoid(h):
             nc.scalar.activation(out=sigmoid[:, h::H, :], in_=og_sb[h][:], func=ACT.Sigmoid)
 
-        def gate_gain(first, last):
-            nc.vector.tensor_tensor(out=gate[:, first:last, :], in0=sigmoid[:, first:last, :],
-                                    in1=gn_sb[:].unsqueeze(1).broadcast_to([P, last - first, E]), op=ALU.mult)
+        def gate_gain(engine, dst, first, last):
+            engine.tensor_tensor(out=dst, in0=sigmoid[:, first:last, :],
+                                 in1=gn_sb[:].unsqueeze(1).broadcast_to([P, last - first, E]), op=ALU.mult)
+
+        def vector_gate(first, last):
+            gate_gain(nc.vector, gate[:, first:last, :], first, last)
 
         def finish(n):
             for h in range(H):
@@ -225,23 +226,22 @@ def tile_rows_a_tanh_mask_onorm_gate_kernel(tc, qT, kT, t, v, mask, gn, og, out)
             load_k(i)
         load_q(1)
         load_q(2)
-        load_mask_rows(0, slice(0, 2))
-        load_mask_rows(0, slice(2, PACK))
-        load_mask_rows(1, slice(0, 2))
-        load_mask_rows(1, slice(2, PACK))
+        for rows in ROW_HALVES:
+            load_mask(0, rows)
+        for rows in (slice(0, 2), slice(2, 3), slice(3, PACK)):
+            load_mask(1, rows)
         load_q(3)
-        for h in range(H):
-            nc.sync.dma_start(out=v_raw[h][:], in_=v.rearrange("h (s r) e -> h s (r e)", r=PACK)[h])
+        nc.sync.dma_start(out=v_raw[:], in_=v.rearrange("h (s r) e -> s h (r e)", r=PACK))
         load_mask(2)
         for h in range(H):
             load_og(h)
         nc.sync.dma_start(out=gn_sb[:], in_=gn)
 
-        table_probe = tile("table_probe", [P, 1], F32)
         nc.scalar.activation(out=table_probe[:], in_=t_sb[:, 0:1], func=ACT.Sigmoid)
+
         round_q(nc.vector, 0)
         quantize_q(0)
-        for i in range(12):
+        for i in range(WARM_UP_PASSES):
             nc.tensor.matmul_mx(out=y_bank[LAST][:, E:2 * E], lhsT=q_codes[0][:].bitcast(FP8X4), lhsT_scale=q_scales[0][:],
                                 rhs=q_codes[0][:].bitcast(FP8X4), rhs_scale=q_scales[0][:], start=True, stop=True)
         round_k(nc.vector, 0)
@@ -263,11 +263,10 @@ def tile_rows_a_tanh_mask_onorm_gate_kernel(tc, qT, kT, t, v, mask, gn, og, out)
         scale_mask(nc.scalar, 1, (3,))
         scale_mask(nc.vector, 0)
         quantize_q(2)
-        scale_mask(nc.vector, 1, (0, 1))
+        scale_mask(nc.vector, 1, (0, 1, 2))
         weigh(0)
         weigh(1)
         round_q(nc.vector, 3)
-        scale_mask(nc.vector, 1, (2,))
         quantize_w(0)
         quantize_q(3)
         scores(2)
@@ -277,11 +276,10 @@ def tile_rows_a_tanh_mask_onorm_gate_kernel(tc, qT, kT, t, v, mask, gn, og, out)
         weigh(2)
         weigh(3)
 
-        round_v(nc.scalar, 0)
         tanh(4)
-        tanh(5)
-        tanh(6)
-        tanh(7)
+        round_v(nc.scalar, 0)
+        for u in range(5, UNITS):
+            tanh(u)
         round_v(nc.vector, 1)
         scale_mask(nc.vector, 2)
         quantize_v()
@@ -292,7 +290,7 @@ def tile_rows_a_tanh_mask_onorm_gate_kernel(tc, qT, kT, t, v, mask, gn, og, out)
         values(1)
 
         for h in range(H):
-            gate_tanh(h)
+            gate_sigmoid(h)
         sum_squares(0, 4)
         inverse_rms(0, 4)
 
@@ -301,10 +299,10 @@ def tile_rows_a_tanh_mask_onorm_gate_kernel(tc, qT, kT, t, v, mask, gn, og, out)
         values(2)
         weigh(7)
         quantize_w(LAST, 0, 1)
-        gate_gain(0, 1)
+        vector_gate(0, 1)
         quantize_w(LAST, 1, H)
-        nc.gpsimd.tensor_tensor(out=last_gate, in0=sigmoid[:, H * LAST:, :], in1=gn_sb[:].unsqueeze(1).broadcast_to([P, H, E]), op=ALU.mult)
-        gate_gain(1, H)
+        gate_gain(nc.gpsimd, last_gate, H * LAST, UNITS)
+        vector_gate(1, H)
         values(LAST)
         sum_squares(4, 7)
         inverse_rms(4, 6)
@@ -312,6 +310,6 @@ def tile_rows_a_tanh_mask_onorm_gate_kernel(tc, qT, kT, t, v, mask, gn, og, out)
         inverse_rms(6, 7)
         inverse_rms(7, 8)
 
-        gate_gain(H, H * LAST)
+        vector_gate(H, H * LAST)
         for n in range(TILES):
             finish(n)

@@ -22,7 +22,7 @@ HALF = N // 2
 WINDOW = HALF // PACK
 K_LOADS = ((0, HALF), (HALF, 3 * N // 4), (3 * N // 4, N))
 MASK_PARTS = ((0, 1), (1, 2), (2, TILES))
-ROW_HALVES = (slice(0, PACK // 2), slice(PACK // 2, PACK))
+MASK_ROWS = (((0, 2), (2, PACK)), ((0, 2), (2, 3), (3, PACK)), ((0, PACK),))
 WARM_UP_PASSES = 12
 Y_PLACES = [divmod(u, H) for u in range(UNITS - 2)] + [(LAST - 1, H), (LAST, 0)]
 DMA_ALIGN = 256
@@ -73,11 +73,6 @@ def tile_rows_a_tanh_mask_onorm_gate_kernel(tc, qT, kT, t, v, mask, gn, og, out)
         score_bank = [ps.tile([P, PACK * QT], F32, name="score_bank" + str(i)) for i in range(2 * H)]
         y_bank = [ps.tile([P, PACK * QT], F32, name="y_bank" + str(i)) for i in range(TILES)]
 
-        last_gate = w_bf[LAST][:, H - 1, :].bitcast(F32).rearrange("p (h e) -> p h e", h=H)
-
-        def gate_of(u):
-            return last_gate[:, u % H, :] if u // H == LAST else gate[:, u, :]
-
         def load_columns(dst, src, first, last):
             nc.sync.dma_start(out=dst[:], in_=src[:, :, first:last])
 
@@ -87,9 +82,11 @@ def tile_rows_a_tanh_mask_onorm_gate_kernel(tc, qT, kT, t, v, mask, gn, og, out)
         def load_k(i):
             load_columns(k_raw[i], kT.rearrange("h (p j) c -> (h p) j c", j=PACK), *K_LOADS[i])
 
-        def load_mask(m, rows=slice(0, PACK)):
+        def load_mask(m):
             a, b = MASK_PARTS[m]
-            nc.sync.dma_start(out=mask_raw[m][:, rows, :], in_=mask.rearrange("(s r) c -> s r c", r=PACK)[:, rows, a * QT:b * QT])
+            for first, last in MASK_ROWS[m]:
+                nc.sync.dma_start(out=mask_raw[m][:, first:last, :],
+                                  in_=mask.rearrange("(s r) c -> s r c", r=PACK)[:, first:last, a * QT:b * QT])
 
         def load_og(h):
             nc.sync.dma_start(out=og_sb[h][:], in_=og.rearrange("h (n p) e -> h p n e", p=QT)[h])
@@ -214,7 +211,7 @@ def tile_rows_a_tanh_mask_onorm_gate_kernel(tc, qT, kT, t, v, mask, gn, og, out)
             for h in range(H):
                 u = H * n + h
                 nc.vector.scalar_tensor_tensor(out=result[n][:, h, :], in0=y_of(u), scalar=inv_rms[:, u:u + 1],
-                                               in1=gate_of(u), op0=ALU.mult, op1=ALU.mult)
+                                               in1=gate[:, u, :], op0=ALU.mult, op1=ALU.mult)
                 if n == LAST:
                     nc.sync.dma_start(out=out[h, n * QT:(n + 1) * QT, :], in_=result[n][:, h, :])
             if n < LAST:
@@ -226,10 +223,8 @@ def tile_rows_a_tanh_mask_onorm_gate_kernel(tc, qT, kT, t, v, mask, gn, og, out)
             load_k(i)
         load_q(1)
         load_q(2)
-        for rows in ROW_HALVES:
-            load_mask(0, rows)
-        for rows in (slice(0, 2), slice(2, 3), slice(3, PACK)):
-            load_mask(1, rows)
+        load_mask(0)
+        load_mask(1)
         load_q(3)
         nc.sync.dma_start(out=v_raw[:], in_=v.rearrange("h (s r) e -> s h (r e)", r=PACK))
         load_mask(2)
@@ -260,10 +255,10 @@ def tile_rows_a_tanh_mask_onorm_gate_kernel(tc, qT, kT, t, v, mask, gn, og, out)
         tanh(0, 2, PACK)
         scores(1)
         tanh(1)
-        scale_mask(nc.scalar, 1, (3,))
+        scale_mask(nc.scalar, 1, range(PACK - 1, PACK))
         scale_mask(nc.vector, 0)
         quantize_q(2)
-        scale_mask(nc.vector, 1, (0, 1, 2))
+        scale_mask(nc.vector, 1, range(PACK - 1))
         weigh(0)
         weigh(1)
         round_q(nc.vector, 3)
@@ -301,7 +296,7 @@ def tile_rows_a_tanh_mask_onorm_gate_kernel(tc, qT, kT, t, v, mask, gn, og, out)
         quantize_w(LAST, 0, 1)
         vector_gate(0, 1)
         quantize_w(LAST, 1, H)
-        gate_gain(nc.gpsimd, last_gate, H * LAST, UNITS)
+        gate_gain(nc.gpsimd, gate[:, H * LAST:, :], H * LAST, UNITS)
         vector_gate(1, H)
         values(LAST)
         sum_squares(4, 7)

@@ -154,9 +154,9 @@ def tile_rows_a_tanh_mask_onorm_gate_kernel(tc, qT, kT, t, v, mask, gn, og, out)
                                 start=True, stop=True)
 
         def scores(n):
-            for u in (H * n, H * n + 1):
-                for r in range(PACK):
-                    score_pass(u, r)
+            for r in range(PACK):
+                for h in range(H):
+                    score_pass(H * n + h, r)
 
         def tanh(u, first=0, last=PACK):
             cols = slice(first * QT, last * QT)
@@ -200,12 +200,9 @@ def tile_rows_a_tanh_mask_onorm_gate_kernel(tc, qT, kT, t, v, mask, gn, og, out)
         def gate_sigmoid(h):
             nc.scalar.activation(out=sigmoid[:, h::H, :], in_=og_sb[h][:], func=ACT.Sigmoid)
 
-        def gate_gain(engine, dst, first, last):
-            engine.tensor_tensor(out=dst, in0=sigmoid[:, first:last, :],
+        def gate_gain(engine, first, last):
+            engine.tensor_tensor(out=gate[:, first:last, :], in0=sigmoid[:, first:last, :],
                                  in1=gn_sb[:].unsqueeze(1).broadcast_to([P, last - first, E]), op=ALU.mult)
-
-        def vector_gate(first, last):
-            gate_gain(nc.vector, gate[:, first:last, :], first, last)
 
         def finish(n):
             for h in range(H):
@@ -244,9 +241,7 @@ def tile_rows_a_tanh_mask_onorm_gate_kernel(tc, qT, kT, t, v, mask, gn, og, out)
         round_k(nc.scalar, 1)
         round_k(nc.vector, 2)
         quantize_k(1)
-        for r in range(PACK):
-            for h in range(H):
-                score_pass(h, r)
+        scores(0)
 
         round_q(nc.scalar, 1)
         round_q(nc.vector, 2)
@@ -286,18 +281,18 @@ def tile_rows_a_tanh_mask_onorm_gate_kernel(tc, qT, kT, t, v, mask, gn, og, out)
 
         for h in range(H):
             gate_sigmoid(h)
-        sum_squares(0, 4)
-        inverse_rms(0, 4)
+        sum_squares(0, 2 * H)
+        inverse_rms(0, 2 * H)
 
         weigh(6)
         quantize_w(2)
         values(2)
         weigh(7)
         quantize_w(LAST, 0, 1)
-        vector_gate(0, 1)
+        gate_gain(nc.vector, 0, 1)
         quantize_w(LAST, 1, H)
-        gate_gain(nc.gpsimd, gate[:, H * LAST:, :], H * LAST, UNITS)
-        vector_gate(1, H)
+        gate_gain(nc.gpsimd, H * LAST, UNITS)
+        gate_gain(nc.vector, 1, H)
         values(LAST)
         sum_squares(4, 7)
         inverse_rms(4, 6)
@@ -305,6 +300,6 @@ def tile_rows_a_tanh_mask_onorm_gate_kernel(tc, qT, kT, t, v, mask, gn, og, out)
         inverse_rms(6, 7)
         inverse_rms(7, 8)
 
-        vector_gate(H, H * LAST)
+        gate_gain(nc.vector, H, H * LAST)
         for n in range(TILES):
             finish(n)

@@ -22,7 +22,7 @@ HALF = N // 2
 WINDOW = HALF // PACK
 K_LOADS = ((0, HALF), (HALF, 3 * N // 4), (3 * N // 4, N))
 MASK_PARTS = ((0, 1), (1, 2), (2, TILES))
-MASK_ROWS = (((0, 2), (2, PACK)), ((0, 2), (2, 3), (3, PACK)), ((0, PACK),))
+MASK_ROWS = (((0, 2), (2, PACK)), ((0, 2), (2, 3), (3, PACK)), ((0, 2), (2, PACK)))
 WARM_UP_PASSES = 12
 Y_PLACES = [divmod(u, H) for u in range(UNITS - 2)] + [(LAST - 1, H), (LAST, 0)]
 DMA_ALIGN = 256
@@ -209,10 +209,7 @@ def tile_rows_a_tanh_mask_onorm_gate_kernel(tc, qT, kT, t, v, mask, gn, og, out)
                 u = H * n + h
                 nc.vector.scalar_tensor_tensor(out=result[n][:, h, :], in0=y_of(u), scalar=inv_rms[:, u:u + 1],
                                                in1=gate[:, u, :], op0=ALU.mult, op1=ALU.mult)
-                if n == LAST:
-                    nc.sync.dma_start(out=out[h, n * QT:(n + 1) * QT, :], in_=result[n][:, h, :])
-            if n < LAST:
-                nc.sync.dma_start(out=out.rearrange("h (n p) e -> n p h e", p=QT)[n], in_=result[n][:])
+            nc.sync.dma_start(out=out.rearrange("h (n p) e -> n p h e", p=QT)[n], in_=result[n][:])
 
         nc.scalar.dma_start(out=t_sb[:], in_=t.rearrange("(s r) o -> s (r o)", r=PACK))
         load_q(0)

@@ -17,15 +17,11 @@ ROWS = D // PACK
 QT = 128
 TILES = NQ // QT
 UNITS = TILES * H
-LAST = TILES - 1
 HALF = N // 2
-WINDOW = HALF // PACK
 K_LOADS = ((0, HALF), (HALF, 3 * N // 4), (3 * N // 4, N))
 MASK_PARTS = ((0, 1), (1, 2), (2, TILES))
-MASK_ROWS = (((0, 2), (2, PACK)), ((0, 2), (2, 3), (3, PACK)), ((0, 2), (2, PACK)))
 WARM_UP_PASSES = 12
-Y_PLACES = [divmod(u, H) for u in range(UNITS - 2)] + [(LAST - 1, H), (LAST, 0)]
-DMA_ALIGN = 256
+ALIGN = 256
 FLOPS = 2 * H * N * NQ * D + 2 * H * NQ * N * E
 
 
@@ -36,60 +32,47 @@ def tile_rows_a_tanh_mask_onorm_gate_kernel(tc, qT, kT, t, v, mask, gn, og, out)
         ps = ctx.enter_context(tc.psum_pool(name="ps", bufs=1))
         ctx.enter_context(tc.manual_schedule())
 
-        def tiles(name, count, shape, dtype):
-            return [sb.tile(shape, dtype, name=name + str(i), align_bytes=DMA_ALIGN) for i in range(count)]
-
         def tile(name, shape, dtype):
-            return sb.tile(shape, dtype, name=name, align_bytes=DMA_ALIGN)
+            return sb.tile(shape, dtype, name=name, align_bytes=ALIGN)
+
+        def tiles(name, count, shape, dtype):
+            return [tile(name + str(i), shape, dtype) for i in range(count)]
 
         k_raw = [tile("k_raw" + str(a), [P, PACK, b - a], F32) for a, b in K_LOADS]
         k_bf = tiles("k_bf", 2, [P, PACK, HALF], BF16)
-        k_codes = tile("k_codes", [P, N], U32)
-        k_scales = tile("k_scales", [P, N], U8)
+        k_codes, k_scales = tile("k_codes", [P, N], U32), tile("k_scales", [P, N], U8)
         q_raw = tiles("q_raw", TILES, [P, PACK, QT], F32)
-        q_bf = tiles("q_bf", TILES, [P, QT * PACK], BF16)
-        q_codes = tiles("q_codes", TILES, [P, QT], U32)
-        q_scales = tiles("q_scales", TILES, [P, QT], U8)
+        q_bf = tiles("q_bf", TILES, [P, PACK * QT], BF16)
+        q_codes, q_scales = tiles("q_codes", TILES, [P, QT], U32), tiles("q_scales", TILES, [P, QT], U8)
         mask_raw = [tile("mask_raw" + str(a), [P, PACK, (b - a) * QT], F32) for a, b in MASK_PARTS]
-        mask_t = [tile("mask_t" + str(a), [P, PACK, (b - a) * QT], F32) for a, b in MASK_PARTS]
-        v_raw = tile("v_raw", [P, H, PACK * E], F32)
+        mask_t = [tile("mask_t" + str(a), [P, (b - a) * PACK * QT], F32) for a, b in MASK_PARTS]
+        v_raw = tile("v_raw", [P, H, PACK, E], F32)
         v_bf = tile("v_bf", [P, H, PACK * E], BF16)
-        v_codes = tile("v_codes", [P, H * E], U32)
-        v_scales = tile("v_scales", [P, H * E], U8)
-        t_sb = tile("t_sb", [P, PACK], F32)
-        gn_sb = tile("gn_sb", [P, E], F32)
+        v_codes, v_scales = tile("v_codes", [P, H * E], U32), tile("v_scales", [P, H * E], U8)
+        t_sb, gn_sb = tile("t_sb", [P, PACK], F32), tile("gn_sb", [P, E], F32)
         og_sb = tiles("og_sb", H, [P, TILES, E], F32)
-        sigmoid = tile("sigmoid", [P, UNITS, E], F32)
         gate = tile("gate", [P, UNITS, E], F32)
-        weights = tiles("weights", UNITS, [P, PACK * QT], F32)
-        w_bf = tiles("w_bf", TILES, [P, H, QT * PACK], BF16)
-        w_codes = tiles("w_codes", TILES, [P, H, QT], U32)
-        w_scales = tiles("w_scales", TILES, [P, H, QT], U8)
+        sigmoid = tile("sigmoid", [P, UNITS, E], F32)
+        weights = tiles("weights", TILES, [P, H, PACK * QT], F32)
+        w_bf = tiles("w_bf", TILES, [P, H, PACK * QT], BF16)
+        w_codes, w_scales = tiles("w_codes", TILES, [P, H, QT], U32), tiles("w_scales", TILES, [P, H, QT], U8)
         squares = tiles("squares", UNITS, [P, E], BF16)
-        sums = tile("sums", [P, UNITS], F32)
-        inv_rms = tile("inv_rms", [P, UNITS], F32)
+        sums, inv_rms = tile("sums", [P, UNITS], F32), tile("inv_rms", [P, UNITS], F32)
         result = tiles("result", TILES, [P, H, E], F32)
         table_probe = tile("table_probe", [P, 1], F32)
         score_bank = [ps.tile([P, PACK * QT], F32, name="score_bank" + str(i)) for i in range(2 * H)]
         y_bank = [ps.tile([P, PACK * QT], F32, name="y_bank" + str(i)) for i in range(TILES)]
 
-        def load_columns(dst, src, first, last):
-            nc.sync.dma_start(out=dst[:], in_=src[:, :, first:last])
+        features = "h (p j) c -> (h p) j c"
+
+        def load(dst, src):
+            nc.sync.dma_start(out=dst, in_=src)
 
         def load_q(n):
-            load_columns(q_raw[n], qT.rearrange("h (p j) c -> (h p) j c", j=PACK), n * QT, (n + 1) * QT)
+            load(q_raw[n][:], qT.rearrange(features, j=PACK)[:, :, n * QT:(n + 1) * QT])
 
-        def load_k(i):
-            load_columns(k_raw[i], kT.rearrange("h (p j) c -> (h p) j c", j=PACK), *K_LOADS[i])
-
-        def load_mask(m):
-            a, b = MASK_PARTS[m]
-            for first, last in MASK_ROWS[m]:
-                nc.sync.dma_start(out=mask_raw[m][:, first:last, :],
-                                  in_=mask.rearrange("(s r) c -> s r c", r=PACK)[:, first:last, a * QT:b * QT])
-
-        def load_og(h):
-            nc.sync.dma_start(out=og_sb[h][:], in_=og.rearrange("h (n p) e -> h p n e", p=QT)[h])
+        def load_mask(n, first=0, last=PACK):
+            load(mask_raw[n][:, first:last, :], mask.rearrange("(s r) c -> s r c", r=PACK)[:, first:last, MASK_PARTS[n][0] * QT:MASK_PARTS[n][1] * QT])
 
         def copy(engine, dst, src):
             if engine is nc.vector:
@@ -103,73 +86,58 @@ def tile_rows_a_tanh_mask_onorm_gate_kernel(tc, qT, kT, t, v, mask, gn, og, out)
         def quantize(codes, scales, src):
             nc.vector.quantize_mx(out=codes.bitcast(FP8X4), scales=scales, in_=src)
 
-        def round_k(engine, i):
+        def round_k(engine, i, groups):
             first, last = K_LOADS[i]
             half = first // HALF
             window = k_bf[half][:, :, first - half * HALF:last - half * HALF].rearrange("p (g r) (s j) -> p g s j r", r=2, j=PACK)
             source = k_raw[i][:].rearrange("p j (s g r) -> p g s j r", g=2, r=2)
-            if engine is nc.scalar:
-                copy(engine, window, source)
-            else:
-                for g in range(2):
-                    copy(engine, window[:, g], source[:, g])
+            copy(engine, window[:, groups], source[:, groups])
 
         def quantize_k(half):
             for r in range(PACK):
-                cols = slice(r * QT + half * WINDOW, r * QT + (half + 1) * WINDOW)
+                cols = slice(r * QT + half * QT // 2, r * QT + (half + 1) * QT // 2)
                 quantize(k_codes[:, cols], k_scales[:, cols], k_bf[half][:, r, :])
 
-        def round_q(engine, n):
-            round_to_words(engine, q_bf[n][:], q_raw[n][:])
+        def prepare_q(engine, n, first=0, last=QT):
+            round_to_words(engine, q_bf[n][:, first * PACK:last * PACK], q_raw[n][:, :, first:last])
 
         def quantize_q(n):
             quantize(q_codes[n][:], q_scales[n][:], q_bf[n][:])
 
-        def round_v(engine, h):
-            round_to_words(engine, v_bf[:, h, :], v_raw[:, h, :].rearrange("p (j e) -> p j e", j=PACK))
-
-        def quantize_v():
-            quantize(v_codes[:], v_scales[:], v_bf[:].rearrange("p h c -> p (h c)"))
-
-        def scale_mask(engine, m, rows=range(PACK)):
+        def scale_mask(engine, n, rows=range(PACK)):
             for r in rows:
-                dst, src, scale = mask_t[m][:, r, :], mask_raw[m][:, r, :], t_sb[:, r:r + 1]
+                dst = mask_t[n][:].rearrange("p (c r i) -> p r c i", r=PACK, i=4)[:, r]
+                src = mask_raw[n][:, r, :].rearrange("p (c i) -> p c i", i=4)
                 if engine is nc.vector:
-                    nc.vector.tensor_scalar(out=dst, in0=src, scalar1=scale, scalar2=None, op0=ALU.mult)
+                    nc.vector.tensor_scalar(out=dst, in0=src, scalar1=t_sb[:, r:r + 1], scalar2=None, op0=ALU.mult)
                 else:
-                    nc.scalar.activation(out=dst, in_=src, func=ACT.Copy, scale=scale)
+                    nc.scalar.activation(out=dst, in_=src, func=ACT.Copy, scale=t_sb[:, r:r + 1])
 
-        def score_bank_of(u, r):
-            n, h = divmod(u, H)
-            if u == 0:
+        def bank_of(n, h, r):
+            if n == 0 and h == 0:
                 return score_bank[r // 2]
             return score_bank[2 * h + (n + 1 - h) % 2]
 
-        def score_pass(u, r):
-            n, h = divmod(u, H)
-            rows, cols = slice(h * ROWS, (h + 1) * ROWS), slice(r * QT, (r + 1) * QT)
-            nc.tensor.matmul_mx(out=score_bank_of(u, r)[:, cols],
-                                lhsT=k_codes[rows, cols].bitcast(FP8X4), lhsT_scale=k_scales[rows, cols],
-                                rhs=q_codes[n][rows, :].bitcast(FP8X4), rhs_scale=q_scales[n][rows, :],
-                                start=True, stop=True)
-
-        def scores(n):
+        def scores(n, heads=range(H)):
             for r in range(PACK):
-                for h in range(H):
-                    score_pass(H * n + h, r)
+                for h in heads:
+                    rows, cols = slice(h * ROWS, (h + 1) * ROWS), slice(r * QT, (r + 1) * QT)
+                    nc.tensor.matmul_mx(out=bank_of(n, h, r)[:, cols],
+                                        lhsT=k_codes[rows, cols].bitcast(FP8X4), lhsT_scale=k_scales[rows, cols],
+                                        rhs=q_codes[n][rows, :].bitcast(FP8X4), rhs_scale=q_scales[n][rows, :],
+                                        start=True, stop=True)
 
-        def tanh(u, first=0, last=PACK):
-            cols = slice(first * QT, last * QT)
-            nc.scalar.activation(out=weights[u][:, cols], in_=score_bank_of(u, first)[:, cols], func=ACT.Tanh)
+        def tanh(n, h, first=0, last=PACK):
+            nc.scalar.activation(out=weights[n][:, h, :].rearrange("p (c r i) -> p c r i", r=PACK, i=4)[:, :, first:last],
+                                 in_=bank_of(n, h, first)[:].rearrange("p (r c i) -> p c r i", r=PACK, i=4)[:, :, first:last], func=ACT.Tanh)
 
-        def weigh(u):
-            n, h = divmod(u, H)
-            m = [i for i, (a, b) in enumerate(MASK_PARTS) if a <= n < b][0]
-            first = (n - MASK_PARTS[m][0]) * QT
-            nc.vector.tensor_tensor(out=w_bf[n][:, h, :].rearrange("p (c i r) -> p c r i", i=2, r=PACK),
-                                    in0=weights[u][:].rearrange("p (r c i) -> p c r i", i=2, r=PACK),
-                                    in1=mask_t[m][:, :, first:first + QT].rearrange("p r (c i) -> p c r i", i=2),
-                                    op=ALU.mult)
+        def weigh(n, first=0, last=H):
+            heads = last - first
+            nc.vector.tensor_tensor(
+                out=w_bf[n][:, first:last, :].rearrange("p h (c i r) -> p h c r i", i=4, r=PACK),
+                in0=weights[n][:, first:last, :].rearrange("p h (c r i) -> p h c r i", i=4, r=PACK),
+                in1=mask_t[min(n, 2)][:, max(n - 2, 0) * PACK * QT:(max(n - 2, 0) + 1) * PACK * QT].unsqueeze(1).broadcast_to([P, heads, PACK * QT]).rearrange("p h (c r i) -> p h c r i", i=4, r=PACK),
+                op=ALU.mult)
 
         def quantize_w(n, first=0, last=H):
             quantize(w_codes[n][:, first:last, :].rearrange("p h c -> p (h c)"),
@@ -177,7 +145,7 @@ def tile_rows_a_tanh_mask_onorm_gate_kernel(tc, qT, kT, t, v, mask, gn, og, out)
                      w_bf[n][:, first:last, :].rearrange("p h c -> p (h c)"))
 
         def y_of(u):
-            bank, place = Y_PLACES[u]
+            bank, place = divmod(u, H) if u != UNITS - 2 else (TILES - 2, H)
             return y_bank[bank][:, place * E:(place + 1) * E]
 
         def values(n):
@@ -185,118 +153,115 @@ def tile_rows_a_tanh_mask_onorm_gate_kernel(tc, qT, kT, t, v, mask, gn, og, out)
                 cols = slice(h * E, (h + 1) * E)
                 nc.tensor.matmul_mx(out=y_of(H * n + h),
                                     lhsT=w_codes[n][:, h, :].bitcast(FP8X4), lhsT_scale=w_scales[n][:, h, :],
-                                    rhs=v_codes[:, cols].bitcast(FP8X4), rhs_scale=v_scales[:, cols],
-                                    start=True, stop=True)
+                                    rhs=v_codes[:, cols].bitcast(FP8X4), rhs_scale=v_scales[:, cols], start=True, stop=True)
 
         def sum_squares(first, last):
             for u in range(first, last):
                 nc.scalar.activation(out=squares[u][:], in_=y_of(u), func=ACT.Square, accum_out=sums[:, u:u + 1])
 
         def inverse_rms(first, last):
-            cols = slice(first, last)
-            nc.scalar.activation(out=inv_rms[:, cols], in_=sums[:, cols], func=ACT.Abs_reciprocal_sqrt,
+            nc.scalar.activation(out=inv_rms[:, first:last], in_=sums[:, first:last], func=ACT.Abs_reciprocal_sqrt,
                                  scale=1.0 / E, bias=256.0 * 1e-5)
-
-        def gate_sigmoid(h):
-            nc.scalar.activation(out=sigmoid[:, h::H, :], in_=og_sb[h][:], func=ACT.Sigmoid)
 
         def gate_gain(engine, first, last):
             engine.tensor_tensor(out=gate[:, first:last, :], in0=sigmoid[:, first:last, :],
                                  in1=gn_sb[:].unsqueeze(1).broadcast_to([P, last - first, E]), op=ALU.mult)
 
-        def finish(n):
-            for h in range(H):
-                u = H * n + h
-                nc.vector.scalar_tensor_tensor(out=result[n][:, h, :], in0=y_of(u), scalar=inv_rms[:, u:u + 1],
-                                               in1=gate[:, u, :], op0=ALU.mult, op1=ALU.mult)
-            nc.sync.dma_start(out=out.rearrange("h (n p) e -> n p h e", p=QT)[n], in_=result[n][:])
+        def finish(u):
+            n, h = divmod(u, H)
+            nc.vector.scalar_tensor_tensor(out=result[n][:, h, :], in0=y_of(u), scalar=inv_rms[:, u:u + 1],
+                                           in1=gate[:, u, :], op0=ALU.mult, op1=ALU.mult)
+            if n == TILES - 1:
+                load(out[h, n * QT:(n + 1) * QT, :], result[n][:, h, :])
+            elif h == H - 1:
+                load(out.rearrange("h (n p) e -> n p h e", p=QT)[n], result[n][:])
 
         nc.scalar.dma_start(out=t_sb[:], in_=t.rearrange("(s r) o -> s (r o)", r=PACK))
         load_q(0)
         for i in range(len(K_LOADS)):
-            load_k(i)
+            load(k_raw[i][:], kT.rearrange(features, j=PACK)[:, :, K_LOADS[i][0]:K_LOADS[i][1]])
         load_q(1)
         load_q(2)
-        load_mask(0)
-        load_mask(1)
+        load_mask(0, 0, 2)
+        load_mask(0, 2, PACK)
+        load_mask(1, 0, 2)
+        load_mask(1, 2, 3)
+        load_mask(1, 3, PACK)
         load_q(3)
-        nc.sync.dma_start(out=v_raw[:], in_=v.rearrange("h (s r) e -> s h (r e)", r=PACK))
+        load(v_raw[:].rearrange("p h j e -> p h (j e)"), v.rearrange("h (s r) e -> s h (r e)", r=PACK))
         load_mask(2)
         for h in range(H):
-            load_og(h)
-        nc.sync.dma_start(out=gn_sb[:], in_=gn)
+            load(og_sb[h][:], og.rearrange("h (n p) e -> h p n e", p=QT)[h])
+        load(gn_sb[:], gn)
 
         nc.scalar.activation(out=table_probe[:], in_=t_sb[:, 0:1], func=ACT.Sigmoid)
-
-        round_q(nc.vector, 0)
+        prepare_q(nc.vector, 0)
         quantize_q(0)
         for i in range(WARM_UP_PASSES):
-            nc.tensor.matmul_mx(out=y_bank[LAST][:, E:2 * E], lhsT=q_codes[0][:].bitcast(FP8X4), lhsT_scale=q_scales[0][:],
+            nc.tensor.matmul_mx(out=y_bank[TILES - 1][:, 0:E], lhsT=q_codes[0][:].bitcast(FP8X4), lhsT_scale=q_scales[0][:],
                                 rhs=q_codes[0][:].bitcast(FP8X4), rhs_scale=q_scales[0][:], start=True, stop=True)
-        round_k(nc.vector, 0)
+        round_k(nc.vector, 0, slice(0, 1))
+        round_k(nc.vector, 0, slice(1, 2))
         quantize_k(0)
-        round_k(nc.scalar, 1)
-        round_k(nc.vector, 2)
+        round_k(nc.scalar, 1, slice(0, 2))
+        round_k(nc.vector, 2, slice(0, 1))
+        round_k(nc.vector, 2, slice(1, 2))
         quantize_k(1)
         scores(0)
-
-        round_q(nc.scalar, 1)
-        round_q(nc.vector, 2)
+        prepare_q(nc.scalar, 1, 0, QT // 2)
+        prepare_q(nc.vector, 1, QT // 2, QT)
         quantize_q(1)
-        tanh(0, 0, 2)
-        tanh(0, 2, PACK)
-        scores(1)
-        tanh(1)
-        scale_mask(nc.scalar, 1, range(PACK - 1, PACK))
+        prepare_q(nc.vector, 2)
+        scores(1, range(1, H))
+        tanh(0, 0, 0, 2)
+        tanh(0, 0, 2, PACK)
+        scores(1, range(1))
+        tanh(0, 1)
+        scale_mask(nc.scalar, 1, range(3, PACK))
         scale_mask(nc.vector, 0)
         quantize_q(2)
-        scale_mask(nc.vector, 1, range(PACK - 1))
-        weigh(0)
-        weigh(1)
-        round_q(nc.vector, 3)
+        scale_mask(nc.vector, 1, range(3))
+        weigh(0, 0, 1)
+        weigh(0, 1, H)
+        prepare_q(nc.vector, 3)
         quantize_w(0)
         quantize_q(3)
         scores(2)
-        tanh(2)
-        tanh(3)
+        tanh(1, 1)
+        tanh(1, 0)
         scores(3)
-        weigh(2)
-        weigh(3)
-
-        tanh(4)
-        round_v(nc.scalar, 0)
-        for u in range(5, UNITS):
-            tanh(u)
-        round_v(nc.vector, 1)
+        weigh(1)
+        tanh(2, 0)
+        round_to_words(nc.scalar, v_bf[:, 0, :], v_raw[:, 0])
+        tanh(2, 1)
+        tanh(3, 0)
+        tanh(3, 1)
+        round_to_words(nc.vector, v_bf[:, 1, :], v_raw[:, 1])
         scale_mask(nc.vector, 2)
-        quantize_v()
+        quantize(v_codes[:], v_scales[:], v_bf[:].rearrange("p h c -> p (h c)"))
         quantize_w(1)
-        weigh(4)
-        weigh(5)
+        weigh(2)
         values(0)
         values(1)
-
         for h in range(H):
-            gate_sigmoid(h)
-        sum_squares(0, 2 * H)
-        inverse_rms(0, 2 * H)
-
-        weigh(6)
+            nc.scalar.activation(out=sigmoid[:, h::H, :], in_=og_sb[h][:], func=ACT.Sigmoid)
+        sum_squares(0, 4)
+        inverse_rms(0, 4)
+        weigh(3, 0, 1)
         quantize_w(2)
         values(2)
-        weigh(7)
-        quantize_w(LAST, 0, 1)
+        weigh(3, 1, H)
+        quantize_w(3, 0, 1)
         gate_gain(nc.vector, 0, 1)
-        quantize_w(LAST, 1, H)
-        gate_gain(nc.gpsimd, H * LAST, UNITS)
-        gate_gain(nc.vector, 1, H)
-        values(LAST)
+        quantize_w(3, 1, H)
+        gate_gain(nc.gpsimd, 6, 8)
+        gate_gain(nc.vector, 1, 2)
+        gate_gain(nc.vector, 2, 6)
+        values(3)
         sum_squares(4, 7)
         inverse_rms(4, 6)
         sum_squares(7, 8)
         inverse_rms(6, 7)
         inverse_rms(7, 8)
-
-        gate_gain(nc.vector, H, H * LAST)
-        for n in range(TILES):
-            finish(n)
+        for u in range(UNITS):
+            finish(u)

@@ -208,10 +208,10 @@ def tile_rows_a_tanh_mask_onorm_gate_kernel(tc, qT, kT, t, v, mask, gn, og, out)
         round_k(nc.vector, 2, slice(1, 2))
         quantize_k(1)
         scores(0)
-        prepare_q(nc.scalar, 1, 0, QT // 2)
-        prepare_q(nc.vector, 1, QT // 2, QT)
+        prepare_q(nc.vector, 1)
+        prepare_q(nc.scalar, 2, 0, QT // 4)
+        prepare_q(nc.vector, 2, QT // 4, QT)
         quantize_q(1)
-        prepare_q(nc.vector, 2)
         scores(1, range(1, H))
         tanh(0, 0, 0, 2)
         tanh(0, 0, 2, PACK)

@@ -20,6 +20,7 @@ UNITS = TILES * H
 HALF = N // 2
 K_LOADS = ((0, HALF), (HALF, 3 * N // 4), (3 * N // 4, N))
 MASK_PARTS = ((0, 1), (1, 2), (2, TILES))
+V_SPLIT = 72
 WARM_UP_PASSES = 12
 ALIGN = 256
 FLOPS = 2 * H * N * NQ * D + 2 * H * NQ * N * E
@@ -83,15 +84,19 @@ def tile_rows_a_tanh_mask_onorm_gate_kernel(tc, qT, kT, t, v, mask, gn, og, out)
         def round_to_words(engine, dst, src):
             copy(engine, dst.rearrange("p (c i j) -> p c j i", i=4, j=PACK), src.rearrange("p j (c i) -> p c j i", i=4))
 
+        def round_v(engine, first, last):
+            copy(engine, v_bf[:, :, first * PACK:last * PACK].rearrange("p h (c i j) -> p h c j i", i=4, j=PACK),
+                 v_raw[:, :, :, first:last].rearrange("p h j (c i) -> p h c j i", i=4))
+
         def quantize(codes, scales, src):
             nc.vector.quantize_mx(out=codes.bitcast(FP8X4), scales=scales, in_=src)
 
-        def round_k(engine, i, groups):
+        def round_k(engine, i, groups, part=slice(None)):
             first, last = K_LOADS[i]
             half = first // HALF
             window = k_bf[half][:, :, first - half * HALF:last - half * HALF].rearrange("p (g r) (s j) -> p g s j r", r=2, j=PACK)
             source = k_raw[i][:].rearrange("p j (s g r) -> p g s j r", g=2, r=2)
-            copy(engine, window[:, groups], source[:, groups])
+            copy(engine, window[:, groups, part], source[:, groups, part])
 
         def quantize_k(half):
             for r in range(PACK):
@@ -114,9 +119,9 @@ def tile_rows_a_tanh_mask_onorm_gate_kernel(tc, qT, kT, t, v, mask, gn, og, out)
                     nc.scalar.activation(out=dst, in_=src, func=ACT.Copy, scale=t_sb[:, r:r + 1])
 
         def bank_of(n, h, r):
-            if n == 0 and h == 0:
-                return score_bank[r // 2]
-            return score_bank[2 * h + (n + 1 - h) % 2]
+            if n == 0:
+                return score_bank[2 * h + min(r, 1)]
+            return score_bank[2 * h + (n + 1) % 2]
 
         def scores(n, heads=range(H)):
             for r in range(PACK):
@@ -204,7 +209,8 @@ def tile_rows_a_tanh_mask_onorm_gate_kernel(tc, qT, kT, t, v, mask, gn, og, out)
         round_k(nc.vector, 0, slice(1, 2))
         quantize_k(0)
         round_k(nc.scalar, 1, slice(0, 2))
-        round_k(nc.vector, 2, slice(0, 1))
+        round_k(nc.scalar, 2, slice(0, 1), slice(0, 16))
+        round_k(nc.vector, 2, slice(0, 1), slice(16, 32))
         round_k(nc.vector, 2, slice(1, 2))
         quantize_k(1)
         scores(0)
@@ -212,11 +218,11 @@ def tile_rows_a_tanh_mask_onorm_gate_kernel(tc, qT, kT, t, v, mask, gn, og, out)
         prepare_q(nc.scalar, 2, 0, QT // 4)
         prepare_q(nc.vector, 2, QT // 4, QT)
         quantize_q(1)
-        scores(1, range(1, H))
-        tanh(0, 0, 0, 2)
-        tanh(0, 0, 2, PACK)
-        scores(1, range(1))
-        tanh(0, 1)
+        tanh(0, 0, 0, 1)
+        tanh(0, 1, 0, 1)
+        scores(1)
+        tanh(0, 0, 1, PACK)
+        tanh(0, 1, 1, PACK)
         scale_mask(nc.scalar, 1, range(3, PACK))
         scale_mask(nc.vector, 0)
         quantize_q(2)
@@ -227,16 +233,16 @@ def tile_rows_a_tanh_mask_onorm_gate_kernel(tc, qT, kT, t, v, mask, gn, og, out)
         quantize_w(0)
         quantize_q(3)
         scores(2)
-        tanh(1, 1)
         tanh(1, 0)
+        tanh(1, 1)
         scores(3)
         weigh(1)
         tanh(2, 0)
-        round_to_words(nc.scalar, v_bf[:, 0, :], v_raw[:, 0])
+        round_v(nc.scalar, 0, V_SPLIT)
         tanh(2, 1)
         tanh(3, 0)
         tanh(3, 1)
-        round_to_words(nc.vector, v_bf[:, 1, :], v_raw[:, 1])
+        round_v(nc.vector, V_SPLIT, E)
         scale_mask(nc.vector, 2)
         quantize(v_codes[:], v_scales[:], v_bf[:].rearrange("p h c -> p (h c)"))
         quantize_w(1)

@@ -20,7 +20,7 @@ UNITS = TILES * H
 HALF = N // 2
 K_LOADS = ((0, HALF), (HALF, 3 * N // 4), (3 * N // 4, N))
 MASK_PARTS = ((0, 1), (1, 2), (2, TILES))
-V_SPLIT = 72
+V_SPLIT = 60
 WARM_UP_PASSES = 12
 ALIGN = 256
 FLOPS = 2 * H * N * NQ * D + 2 * H * NQ * N * E

@@ -55,8 +55,8 @@ def tile_rows_a_tanh_mask_onorm_gate_kernel(tc, qT, kT, t, v, mask, gn, og, out)
         gate = tile("gate", [P, UNITS, E], F32)
         sigmoid = tile("sigmoid", [P, UNITS, E], F32)
         weights = tiles("weights", TILES, [P, H, PACK * QT], F32)
-        w_bf = tiles("w_bf", TILES, [P, H, PACK * QT], BF16)
-        w_codes, w_scales = tiles("w_codes", TILES, [P, H, QT], U32), tiles("w_scales", TILES, [P, H, QT], U8)
+        w_bf = tiles("w_bf", 2, [P, 2 * H, PACK * QT], BF16)
+        w_codes, w_scales = tiles("w_codes", 2, [P, 2 * H, QT], U32), tiles("w_scales", 2, [P, 2 * H, QT], U8)
         squares = tiles("squares", UNITS, [P, E], BF16)
         sums, inv_rms = tile("sums", [P, UNITS], F32), tile("inv_rms", [P, UNITS], F32)
         result = tiles("result", TILES, [P, H, E], F32)
@@ -139,25 +139,26 @@ def tile_rows_a_tanh_mask_onorm_gate_kernel(tc, qT, kT, t, v, mask, gn, og, out)
         def weigh(n, first=0, last=H):
             heads = last - first
             nc.vector.tensor_tensor(
-                out=w_bf[n][:, first:last, :].rearrange("p h (c i r) -> p h c r i", i=4, r=PACK),
+                out=w_bf[n // 2][:, n % 2 * H + first:n % 2 * H + last, :].rearrange("p h (c i r) -> p h c r i", i=4, r=PACK),
                 in0=weights[n][:, first:last, :].rearrange("p h (c r i) -> p h c r i", i=4, r=PACK),
                 in1=mask_t[min(n, 2)][:, max(n - 2, 0) * PACK * QT:(max(n - 2, 0) + 1) * PACK * QT].unsqueeze(1).broadcast_to([P, heads, PACK * QT]).rearrange("p h (c r i) -> p h c r i", i=4, r=PACK),
                 op=ALU.mult)
 
-        def quantize_w(n, first=0, last=H):
+        def quantize_w(first, last):
+            n, first, last = first // 4, first % 4, (last - 1) % 4 + 1
             quantize(w_codes[n][:, first:last, :].rearrange("p h c -> p (h c)"),
                      w_scales[n][:, first:last, :].rearrange("p h c -> p (h c)"),
                      w_bf[n][:, first:last, :].rearrange("p h c -> p (h c)"))
 
         def y_of(u):
-            bank, place = divmod(u, H) if u != UNITS - 2 else (TILES - 2, H)
+            bank, place = ((0, 0), (0, 1), (1, 0), (1, 1), (1, 2), (2, 0), (2, 1), (3, 0))[u]
             return y_bank[bank][:, place * E:(place + 1) * E]
 
-        def values(n):
-            for h in range(H):
-                cols = slice(h * E, (h + 1) * E)
-                nc.tensor.matmul_mx(out=y_of(H * n + h),
-                                    lhsT=w_codes[n][:, h, :].bitcast(FP8X4), lhsT_scale=w_scales[n][:, h, :],
+        def values(first, last):
+            for u in range(first, last):
+                cols = slice(u % H * E, (u % H + 1) * E)
+                nc.tensor.matmul_mx(out=y_of(u),
+                                    lhsT=w_codes[u // 4][:, u % 4, :].bitcast(FP8X4), lhsT_scale=w_scales[u // 4][:, u % 4, :],
                                     rhs=v_codes[:, cols].bitcast(FP8X4), rhs_scale=v_scales[:, cols], start=True, stop=True)
 
         def sum_squares(first, last):
@@ -230,7 +231,7 @@ def tile_rows_a_tanh_mask_onorm_gate_kernel(tc, qT, kT, t, v, mask, gn, og, out)
         weigh(0, 0, 1)
         weigh(0, 1, H)
         prepare_q(nc.vector, 3)
-        quantize_w(0)
+        quantize_w(0, 2)
         quantize_q(3)
         scores(2)
         tanh(1, 0)
@@ -245,25 +246,23 @@ def tile_rows_a_tanh_mask_onorm_gate_kernel(tc, qT, kT, t, v, mask, gn, og, out)
         round_v(nc.vector, V_SPLIT, E)
         scale_mask(nc.vector, 2)
         quantize(v_codes[:], v_scales[:], v_bf[:].rearrange("p h c -> p (h c)"))
-        quantize_w(1)
+        quantize_w(2, 4)
         weigh(2)
-        values(0)
-        values(1)
+        values(0, 4)
         for h in range(H):
             nc.scalar.activation(out=sigmoid[:, h::H, :], in_=og_sb[h][:], func=ACT.Sigmoid)
         sum_squares(0, 4)
         inverse_rms(0, 4)
         weigh(3, 0, 1)
-        quantize_w(2)
-        values(2)
+        quantize_w(4, 5)
+        values(4, 5)
         weigh(3, 1, H)
-        quantize_w(3, 0, 1)
-        gate_gain(nc.vector, 0, 1)
-        quantize_w(3, 1, H)
+        quantize_w(5, 7)
+        quantize_w(7, 8)
         gate_gain(nc.gpsimd, 6, 8)
-        gate_gain(nc.vector, 1, 2)
+        gate_gain(nc.vector, 0, 2)
         gate_gain(nc.vector, 2, 6)
-        values(3)
+        values(5, 8)
         sum_squares(4, 7)
         inverse_rms(4, 6)
         sum_squares(7, 8)

@@ -20,7 +20,7 @@ UNITS = TILES * H
 HALF = N // 2
 K_LOADS = ((0, HALF), (HALF, 3 * N // 4), (3 * N // 4, N))
 MASK_PARTS = ((0, 1), (1, 2), (2, TILES))
-V_SPLIT = 60
+V_SPLIT = 56
 WARM_UP_PASSES = 12
 ALIGN = 256
 FLOPS = 2 * H * N * NQ * D + 2 * H * NQ * N * E
@@ -151,7 +151,7 @@ def tile_rows_a_tanh_mask_onorm_gate_kernel(tc, qT, kT, t, v, mask, gn, og, out)
                      w_bf[n][:, first:last, :].rearrange("p h c -> p (h c)"))
 
         def y_of(u):
-            bank, place = ((0, 0), (0, 1), (1, 0), (1, 1), (1, 2), (2, 0), (2, 1), (3, 0))[u]
+            bank, place = ((0, 0), (0, 1), (1, 0), (1, 1), (2, 0), (2, 1), (3, 0), (3, 1))[u]
             return y_bank[bank][:, place * E:(place + 1) * E]
 
         def values(first, last):
@@ -201,7 +201,8 @@ def tile_rows_a_tanh_mask_onorm_gate_kernel(tc, qT, kT, t, v, mask, gn, og, out)
         load(gn_sb[:], gn)
 
         nc.scalar.activation(out=table_probe[:], in_=t_sb[:, 0:1], func=ACT.Sigmoid)
-        prepare_q(nc.vector, 0)
+        for first in range(0, QT, QT // 8):
+            prepare_q(nc.vector, 0, first, first + QT // 8)
         quantize_q(0)
         for i in range(WARM_UP_PASSES):
             nc.tensor.matmul_mx(out=y_bank[TILES - 1][:, 0:E], lhsT=q_codes[0][:].bitcast(FP8X4), lhsT_scale=q_scales[0][:],
@@ -254,19 +255,20 @@ def tile_rows_a_tanh_mask_onorm_gate_kernel(tc, qT, kT, t, v, mask, gn, og, out)
         sum_squares(0, 4)
         inverse_rms(0, 4)
         weigh(3, 0, 1)
-        quantize_w(4, 5)
-        values(4, 5)
+        quantize_w(4, 6)
+        values(4, 6)
         weigh(3, 1, H)
-        quantize_w(5, 7)
+        quantize_w(6, 7)
+        gate_gain(nc.vector, 0, 1)
         quantize_w(7, 8)
-        gate_gain(nc.gpsimd, 6, 8)
-        gate_gain(nc.vector, 0, 2)
-        gate_gain(nc.vector, 2, 6)
-        values(5, 8)
-        sum_squares(4, 7)
+        gate_gain(nc.gpsimd, 5, 7)
+        gate_gain(nc.gpsimd, 7, 8)
+        gate_gain(nc.vector, 1, 2)
+        gate_gain(nc.vector, 2, 5)
+        values(6, 8)
+        sum_squares(4, 6)
         inverse_rms(4, 6)
-        sum_squares(7, 8)
+        sum_squares(6, 8)
         inverse_rms(6, 7)
         inverse_rms(7, 8)
-        for u in range(UNITS):
-            finish(u)
+        for u in range(UNITS): finish(u)

@@ -207,8 +207,9 @@ def tile_rows_a_tanh_mask_onorm_gate_kernel(tc, qT, kT, t, v, mask, gn, og, out)
         for i in range(WARM_UP_PASSES):
             nc.tensor.matmul_mx(out=y_bank[TILES - 1][:, 0:E], lhsT=q_codes[0][:].bitcast(FP8X4), lhsT_scale=q_scales[0][:],
                                 rhs=q_codes[0][:].bitcast(FP8X4), rhs_scale=q_scales[0][:], start=True, stop=True)
-        round_k(nc.vector, 0, slice(0, 1))
-        round_k(nc.vector, 0, slice(1, 2))
+        for group in range(2):
+            for first in range(0, 64, 32):
+                round_k(nc.vector, 0, slice(group, group + 1), slice(first, first + 32))
         quantize_k(0)
         round_k(nc.scalar, 1, slice(0, 2))
         round_k(nc.scalar, 2, slice(0, 1), slice(0, 16))
@@ -254,21 +255,20 @@ def tile_rows_a_tanh_mask_onorm_gate_kernel(tc, qT, kT, t, v, mask, gn, og, out)
             nc.scalar.activation(out=sigmoid[:, h::H, :], in_=og_sb[h][:], func=ACT.Sigmoid)
         sum_squares(0, 4)
         inverse_rms(0, 4)
-        weigh(3, 0, 1)
+        weigh(3)
         quantize_w(4, 6)
         values(4, 6)
-        weigh(3, 1, H)
-        quantize_w(6, 7)
-        gate_gain(nc.vector, 0, 1)
-        quantize_w(7, 8)
+        quantize_w(6, 8)
         gate_gain(nc.gpsimd, 5, 7)
         gate_gain(nc.gpsimd, 7, 8)
-        gate_gain(nc.vector, 1, 2)
+        gate_gain(nc.vector, 0, 2)
         gate_gain(nc.vector, 2, 5)
         values(6, 8)
         sum_squares(4, 6)
-        inverse_rms(4, 6)
-        sum_squares(6, 8)
+        inverse_rms(4, 5)
+        sum_squares(6, 7)
+        inverse_rms(5, 6)
+        sum_squares(7, 8)
         inverse_rms(6, 7)
         inverse_rms(7, 8)
         for u in range(UNITS): finish(u)

@@ -20,7 +20,7 @@ UNITS = TILES * H
 HALF = N // 2
 K_LOADS = ((0, HALF), (HALF, 3 * N // 4), (3 * N // 4, N))
 MASK_PARTS = ((0, 1), (1, 2), (2, TILES))
-V_SPLIT = 56
+V_SPLIT = 52
 WARM_UP_PASSES = 12
 ALIGN = 256
 FLOPS = 2 * H * N * NQ * D + 2 * H * NQ * N * E
@@ -255,13 +255,16 @@ def tile_rows_a_tanh_mask_onorm_gate_kernel(tc, qT, kT, t, v, mask, gn, og, out)
             nc.scalar.activation(out=sigmoid[:, h::H, :], in_=og_sb[h][:], func=ACT.Sigmoid)
         sum_squares(0, 4)
         inverse_rms(0, 4)
-        weigh(3)
+        weigh(3, 0, 1)
         quantize_w(4, 6)
         values(4, 6)
-        quantize_w(6, 8)
+        weigh(3, 1, H)
+        quantize_w(6, 7)
+        gate_gain(nc.vector, 0, 1)
+        quantize_w(7, 8)
         gate_gain(nc.gpsimd, 5, 7)
         gate_gain(nc.gpsimd, 7, 8)
-        gate_gain(nc.vector, 0, 2)
+        gate_gain(nc.vector, 1, 2)
         gate_gain(nc.vector, 2, 5)
         values(6, 8)
         sum_squares(4, 6)

@@ -161,6 +161,11 @@ def tile_rows_a_tanh_mask_onorm_gate_kernel(tc, qT, kT, t, v, mask, gn, og, out)
                                     lhsT=w_codes[u // 4][:, u % 4, :].bitcast(FP8X4), lhsT_scale=w_scales[u // 4][:, u % 4, :],
                                     rhs=v_codes[:, cols].bitcast(FP8X4), rhs_scale=v_scales[:, cols], start=True, stop=True)
 
+        def warm_up(passes):
+            for i in range(passes):
+                nc.tensor.matmul_mx(out=y_bank[TILES - 1][:, 0:E], lhsT=q_codes[0][:].bitcast(FP8X4), lhsT_scale=q_scales[0][:],
+                                    rhs=q_codes[0][:].bitcast(FP8X4), rhs_scale=q_scales[0][:], start=True, stop=True)
+
         def sum_squares(first, last):
             for u in range(first, last):
                 nc.scalar.activation(out=squares[u][:], in_=y_of(u), func=ACT.Square, accum_out=sums[:, u:u + 1])
@@ -204,9 +209,7 @@ def tile_rows_a_tanh_mask_onorm_gate_kernel(tc, qT, kT, t, v, mask, gn, og, out)
         for first in range(0, QT, QT // 8):
             prepare_q(nc.vector, 0, first, first + QT // 8)
         quantize_q(0)
-        for i in range(WARM_UP_PASSES):
-            nc.tensor.matmul_mx(out=y_bank[TILES - 1][:, 0:E], lhsT=q_codes[0][:].bitcast(FP8X4), lhsT_scale=q_scales[0][:],
-                                rhs=q_codes[0][:].bitcast(FP8X4), rhs_scale=q_scales[0][:], start=True, stop=True)
+        warm_up(WARM_UP_PASSES)
         for group in range(2):
             for first in range(0, 64, 32):
                 round_k(nc.vector, 0, slice(group, group + 1), slice(first, first + 32))
@@ -236,6 +239,7 @@ def tile_rows_a_tanh_mask_onorm_gate_kernel(tc, qT, kT, t, v, mask, gn, og, out)
         quantize_w(0, 2)
         quantize_q(3)
         scores(2)
+        warm_up(11)
         tanh(1, 0)
         tanh(1, 1)
         scores(3)

@@ -174,14 +174,19 @@ def tile_rows_a_tanh_mask_onorm_gate_kernel(tc, qT, kT, t, v, mask, gn, og, out)
             nc.scalar.activation(out=inv_rms[:, first:last], in_=sums[:, first:last], func=ACT.Abs_reciprocal_sqrt,
                                  scale=1.0 / E, bias=256.0 * 1e-5)
 
+        late_gate = w_bf[1][:, H:, :].rearrange("p h c -> p (h c)").bitcast(F32).rearrange("p (u e) -> p u e", e=E)
+
+        def gate_of(first, last):
+            return gate[:, first:last, :] if first < 5 else late_gate[:, first - 5:last - 5, :]
+
         def gate_gain(engine, first, last):
-            engine.tensor_tensor(out=gate[:, first:last, :], in0=sigmoid[:, first:last, :],
+            engine.tensor_tensor(out=gate_of(first, last), in0=sigmoid[:, first:last, :],
                                  in1=gn_sb[:].unsqueeze(1).broadcast_to([P, last - first, E]), op=ALU.mult)
 
         def finish(u):
             n, h = divmod(u, H)
             nc.vector.scalar_tensor_tensor(out=result[n][:, h, :], in0=y_of(u), scalar=inv_rms[:, u:u + 1],
-                                           in1=gate[:, u, :], op0=ALU.mult, op1=ALU.mult)
+                                           in1=gate_of(u, u + 1)[:, 0, :], op0=ALU.mult, op1=ALU.mult)
             if n == TILES - 1:
                 load(out[h, n * QT:(n + 1) * QT, :], result[n][:, h, :])
             elif h == H - 1:

@@ -13,16 +13,24 @@ ALU = mybir.AluOpType
 H, D, NQ, N, E = 2, 256, 512, 512, 128
 P = 128
 PACK = 4
+RUN = 4
 ROWS = D // PACK
 QT = 128
 TILES = NQ // QT
 UNITS = TILES * H
+LAST = TILES - 1
 HALF = N // 2
+WINDOW = HALF // PACK
 K_LOADS = ((0, HALF), (HALF, 3 * N // 4), (3 * N // 4, N))
 MASK_PARTS = ((0, 1), (1, 2), (2, TILES))
-V_SPLIT = 52
-WARM_UP_PASSES = 12
-ALIGN = 256
+MASK_ROWS = (((0, 2), (2, PACK)), ((0, 2), (2, 3), (3, PACK)), ((0, PACK),))
+W_UNITS = 2 * H
+V_ON_SCALAR = 52
+GATES_ON_VECTOR = 5
+Q_PIECES, K_PIECES = 8, 2
+FIRST_WARM_UP = 12
+SECOND_WARM_UP = 11
+DMA_ALIGN = 256
 FLOPS = 2 * H * N * NQ * D + 2 * H * NQ * N * E
 
 
@@ -34,7 +42,7 @@ def tile_rows_a_tanh_mask_onorm_gate_kernel(tc, qT, kT, t, v, mask, gn, og, out)
         ctx.enter_context(tc.manual_schedule())
 
         def tile(name, shape, dtype):
-            return sb.tile(shape, dtype, name=name, align_bytes=ALIGN)
+            return sb.tile(shape, dtype, name=name, align_bytes=DMA_ALIGN)
 
         def tiles(name, count, shape, dtype):
             return [tile(name + str(i), shape, dtype) for i in range(count)]
@@ -52,28 +60,35 @@ def tile_rows_a_tanh_mask_onorm_gate_kernel(tc, qT, kT, t, v, mask, gn, og, out)
         v_codes, v_scales = tile("v_codes", [P, H * E], U32), tile("v_scales", [P, H * E], U8)
         t_sb, gn_sb = tile("t_sb", [P, PACK], F32), tile("gn_sb", [P, E], F32)
         og_sb = tiles("og_sb", H, [P, TILES, E], F32)
-        gate = tile("gate", [P, UNITS, E], F32)
+        gate = tile("gate", [P, GATES_ON_VECTOR, E], F32)
         sigmoid = tile("sigmoid", [P, UNITS, E], F32)
         weights = tiles("weights", TILES, [P, H, PACK * QT], F32)
-        w_bf = tiles("w_bf", 2, [P, 2 * H, PACK * QT], BF16)
-        w_codes, w_scales = tiles("w_codes", 2, [P, 2 * H, QT], U32), tiles("w_scales", 2, [P, 2 * H, QT], U8)
+        w_bf = tiles("w_bf", UNITS // W_UNITS, [P, W_UNITS, PACK * QT], BF16)
+        w_codes = tiles("w_codes", UNITS // W_UNITS, [P, W_UNITS, QT], U32)
+        w_scales = tiles("w_scales", UNITS // W_UNITS, [P, W_UNITS, QT], U8)
         squares = tiles("squares", UNITS, [P, E], BF16)
         sums, inv_rms = tile("sums", [P, UNITS], F32), tile("inv_rms", [P, UNITS], F32)
         result = tiles("result", TILES, [P, H, E], F32)
         table_probe = tile("table_probe", [P, 1], F32)
         score_bank = [ps.tile([P, PACK * QT], F32, name="score_bank" + str(i)) for i in range(2 * H)]
         y_bank = [ps.tile([P, PACK * QT], F32, name="y_bank" + str(i)) for i in range(TILES)]
+        late_gate = w_bf[-1][:, W_UNITS - H:, :].rearrange("p h c -> p (h c)").bitcast(F32).rearrange("p (u e) -> p u e", e=E)
 
-        features = "h (p j) c -> (h p) j c"
-
-        def load(dst, src):
-            nc.sync.dma_start(out=dst, in_=src)
+        def by_features(x):
+            return x.rearrange("h (p j) c -> (h p) j c", j=PACK)
 
         def load_q(n):
-            load(q_raw[n][:], qT.rearrange(features, j=PACK)[:, :, n * QT:(n + 1) * QT])
+            nc.sync.dma_start(out=q_raw[n][:], in_=by_features(qT)[:, :, n * QT:(n + 1) * QT])
 
-        def load_mask(n, first=0, last=PACK):
-            load(mask_raw[n][:, first:last, :], mask.rearrange("(s r) c -> s r c", r=PACK)[:, first:last, MASK_PARTS[n][0] * QT:MASK_PARTS[n][1] * QT])
+        def load_k(i):
+            first, last = K_LOADS[i]
+            nc.sync.dma_start(out=k_raw[i][:], in_=by_features(kT)[:, :, first:last])
+
+        def load_mask(m):
+            a, b = MASK_PARTS[m]
+            for first, last in MASK_ROWS[m]:
+                nc.sync.dma_start(out=mask_raw[m][:, first:last, :],
+                                  in_=mask.rearrange("(s r) c -> s r c", r=PACK)[:, first:last, a * QT:b * QT])
 
         def copy(engine, dst, src):
             if engine is nc.vector:
@@ -81,89 +96,90 @@ def tile_rows_a_tanh_mask_onorm_gate_kernel(tc, qT, kT, t, v, mask, gn, og, out)
             else:
                 nc.scalar.copy(out=dst, in_=src)
 
-        def round_to_words(engine, dst, src):
-            copy(engine, dst.rearrange("p (c i j) -> p c j i", i=4, j=PACK), src.rearrange("p j (c i) -> p c j i", i=4))
-
-        def round_v(engine, first, last):
-            copy(engine, v_bf[:, :, first * PACK:last * PACK].rearrange("p h (c i j) -> p h c j i", i=4, j=PACK),
-                 v_raw[:, :, :, first:last].rearrange("p h j (c i) -> p h c j i", i=4))
-
         def quantize(codes, scales, src):
             nc.vector.quantize_mx(out=codes.bitcast(FP8X4), scales=scales, in_=src)
 
-        def round_k(engine, i, groups, part=slice(None)):
+        def round_k(engine, i, pairs, columns=slice(None)):
             first, last = K_LOADS[i]
             half = first // HALF
             window = k_bf[half][:, :, first - half * HALF:last - half * HALF].rearrange("p (g r) (s j) -> p g s j r", r=2, j=PACK)
             source = k_raw[i][:].rearrange("p j (s g r) -> p g s j r", g=2, r=2)
-            copy(engine, window[:, groups, part], source[:, groups, part])
+            copy(engine, window[:, pairs, columns], source[:, pairs, columns])
 
         def quantize_k(half):
             for r in range(PACK):
-                cols = slice(r * QT + half * QT // 2, r * QT + (half + 1) * QT // 2)
+                cols = slice(r * QT + half * WINDOW, r * QT + (half + 1) * WINDOW)
                 quantize(k_codes[:, cols], k_scales[:, cols], k_bf[half][:, r, :])
 
-        def prepare_q(engine, n, first=0, last=QT):
-            round_to_words(engine, q_bf[n][:, first * PACK:last * PACK], q_raw[n][:, :, first:last])
+        def round_q(engine, n, first=0, last=QT):
+            copy(engine, q_bf[n][:, first * PACK:last * PACK].rearrange("p (c i j) -> p c j i", i=RUN, j=PACK),
+                 q_raw[n][:, :, first:last].rearrange("p j (c i) -> p c j i", i=RUN))
 
         def quantize_q(n):
             quantize(q_codes[n][:], q_scales[n][:], q_bf[n][:])
 
-        def scale_mask(engine, n, rows=range(PACK)):
+        def round_v(engine, first, last):
+            copy(engine, v_bf[:, :, first * PACK:last * PACK].rearrange("p h (c i r) -> p h c r i", i=RUN, r=PACK),
+                 v_raw[:, :, :, first:last].rearrange("p h r (c i) -> p h c r i", i=RUN))
+
+        def scale_mask(engine, m, rows=range(PACK)):
             for r in rows:
-                dst = mask_t[n][:].rearrange("p (c r i) -> p r c i", r=PACK, i=4)[:, r]
-                src = mask_raw[n][:, r, :].rearrange("p (c i) -> p c i", i=4)
+                dst = mask_t[m][:].rearrange("p (c r i) -> p r c i", r=PACK, i=RUN)[:, r]
+                src = mask_raw[m][:, r, :].rearrange("p (c i) -> p c i", i=RUN)
                 if engine is nc.vector:
                     nc.vector.tensor_scalar(out=dst, in0=src, scalar1=t_sb[:, r:r + 1], scalar2=None, op0=ALU.mult)
                 else:
                     nc.scalar.activation(out=dst, in_=src, func=ACT.Copy, scale=t_sb[:, r:r + 1])
 
-        def bank_of(n, h, r):
+        def score_bank_of(n, h, r):
             if n == 0:
                 return score_bank[2 * h + min(r, 1)]
             return score_bank[2 * h + (n + 1) % 2]
 
-        def scores(n, heads=range(H)):
+        def scores(n):
             for r in range(PACK):
-                for h in heads:
+                for h in range(H):
                     rows, cols = slice(h * ROWS, (h + 1) * ROWS), slice(r * QT, (r + 1) * QT)
-                    nc.tensor.matmul_mx(out=bank_of(n, h, r)[:, cols],
+                    nc.tensor.matmul_mx(out=score_bank_of(n, h, r)[:, cols],
                                         lhsT=k_codes[rows, cols].bitcast(FP8X4), lhsT_scale=k_scales[rows, cols],
                                         rhs=q_codes[n][rows, :].bitcast(FP8X4), rhs_scale=q_scales[n][rows, :],
                                         start=True, stop=True)
 
         def tanh(n, h, first=0, last=PACK):
-            nc.scalar.activation(out=weights[n][:, h, :].rearrange("p (c r i) -> p c r i", r=PACK, i=4)[:, :, first:last],
-                                 in_=bank_of(n, h, first)[:].rearrange("p (r c i) -> p c r i", r=PACK, i=4)[:, :, first:last], func=ACT.Tanh)
+            dst = weights[n][:, h, :].rearrange("p (c r i) -> p c r i", r=PACK, i=RUN)
+            src = score_bank_of(n, h, first)[:].rearrange("p (r c i) -> p c r i", r=PACK, i=RUN)
+            nc.scalar.activation(out=dst[:, :, first:last], in_=src[:, :, first:last], func=ACT.Tanh)
+
+        def w_place(buffers, first, last):
+            offset = first % W_UNITS
+            return buffers[first // W_UNITS][:, offset:offset + last - first, :]
 
         def weigh(n, first=0, last=H):
-            heads = last - first
+            m = [i for i, (a, b) in enumerate(MASK_PARTS) if a <= n < b][0]
+            offset = (n - MASK_PARTS[m][0]) * PACK * QT
+            scaled_mask = mask_t[m][:, offset:offset + PACK * QT].unsqueeze(1).broadcast_to([P, last - first, PACK * QT])
             nc.vector.tensor_tensor(
-                out=w_bf[n // 2][:, n % 2 * H + first:n % 2 * H + last, :].rearrange("p h (c i r) -> p h c r i", i=4, r=PACK),
-                in0=weights[n][:, first:last, :].rearrange("p h (c r i) -> p h c r i", i=4, r=PACK),
-                in1=mask_t[min(n, 2)][:, max(n - 2, 0) * PACK * QT:(max(n - 2, 0) + 1) * PACK * QT].unsqueeze(1).broadcast_to([P, heads, PACK * QT]).rearrange("p h (c r i) -> p h c r i", i=4, r=PACK),
-                op=ALU.mult)
+                out=w_place(w_bf, H * n + first, H * n + last).rearrange("p h (c i r) -> p h c r i", i=RUN, r=PACK),
+                in0=weights[n][:, first:last, :].rearrange("p h (c r i) -> p h c r i", i=RUN, r=PACK),
+                in1=scaled_mask.rearrange("p h (c r i) -> p h c r i", i=RUN, r=PACK), op=ALU.mult)
 
         def quantize_w(first, last):
-            n, first, last = first // 4, first % 4, (last - 1) % 4 + 1
-            quantize(w_codes[n][:, first:last, :].rearrange("p h c -> p (h c)"),
-                     w_scales[n][:, first:last, :].rearrange("p h c -> p (h c)"),
-                     w_bf[n][:, first:last, :].rearrange("p h c -> p (h c)"))
+            quantize(*[w_place(x, first, last).rearrange("p u c -> p (u c)") for x in (w_codes, w_scales, w_bf)])
 
         def y_of(u):
-            bank, place = ((0, 0), (0, 1), (1, 0), (1, 1), (2, 0), (2, 1), (3, 0), (3, 1))[u]
-            return y_bank[bank][:, place * E:(place + 1) * E]
+            n, h = divmod(u, H)
+            return y_bank[n][:, h * E:(h + 1) * E]
 
         def values(first, last):
             for u in range(first, last):
                 cols = slice(u % H * E, (u % H + 1) * E)
-                nc.tensor.matmul_mx(out=y_of(u),
-                                    lhsT=w_codes[u // 4][:, u % 4, :].bitcast(FP8X4), lhsT_scale=w_scales[u // 4][:, u % 4, :],
+                nc.tensor.matmul_mx(out=y_of(u), lhsT=w_place(w_codes, u, u + 1)[:, 0, :].bitcast(FP8X4),
+                                    lhsT_scale=w_place(w_scales, u, u + 1)[:, 0, :],
                                     rhs=v_codes[:, cols].bitcast(FP8X4), rhs_scale=v_scales[:, cols], start=True, stop=True)
 
         def warm_up(passes):
             for i in range(passes):
-                nc.tensor.matmul_mx(out=y_bank[TILES - 1][:, 0:E], lhsT=q_codes[0][:].bitcast(FP8X4), lhsT_scale=q_scales[0][:],
+                nc.tensor.matmul_mx(out=y_bank[LAST][:, 0:E], lhsT=q_codes[0][:].bitcast(FP8X4), lhsT_scale=q_scales[0][:],
                                     rhs=q_codes[0][:].bitcast(FP8X4), rhs_scale=q_scales[0][:], start=True, stop=True)
 
         def sum_squares(first, last):
@@ -174,10 +190,10 @@ def tile_rows_a_tanh_mask_onorm_gate_kernel(tc, qT, kT, t, v, mask, gn, og, out)
             nc.scalar.activation(out=inv_rms[:, first:last], in_=sums[:, first:last], func=ACT.Abs_reciprocal_sqrt,
                                  scale=1.0 / E, bias=256.0 * 1e-5)
 
-        late_gate = w_bf[1][:, H:, :].rearrange("p h c -> p (h c)").bitcast(F32).rearrange("p (u e) -> p u e", e=E)
-
         def gate_of(first, last):
-            return gate[:, first:last, :] if first < 5 else late_gate[:, first - 5:last - 5, :]
+            if first < GATES_ON_VECTOR:
+                return gate[:, first:last, :]
+            return late_gate[:, first - GATES_ON_VECTOR:last - GATES_ON_VECTOR, :]
 
         def gate_gain(engine, first, last):
             engine.tensor_tensor(out=gate_of(first, last), in0=sigmoid[:, first:last, :],
@@ -187,100 +203,102 @@ def tile_rows_a_tanh_mask_onorm_gate_kernel(tc, qT, kT, t, v, mask, gn, og, out)
             n, h = divmod(u, H)
             nc.vector.scalar_tensor_tensor(out=result[n][:, h, :], in0=y_of(u), scalar=inv_rms[:, u:u + 1],
                                            in1=gate_of(u, u + 1)[:, 0, :], op0=ALU.mult, op1=ALU.mult)
-            if n == TILES - 1:
-                load(out[h, n * QT:(n + 1) * QT, :], result[n][:, h, :])
+            if n == LAST:
+                nc.sync.dma_start(out=out[h, n * QT:(n + 1) * QT, :], in_=result[n][:, h, :])
             elif h == H - 1:
-                load(out.rearrange("h (n p) e -> n p h e", p=QT)[n], result[n][:])
+                nc.sync.dma_start(out=out.rearrange("h (n p) e -> n p h e", p=QT)[n], in_=result[n][:])
 
         nc.scalar.dma_start(out=t_sb[:], in_=t.rearrange("(s r) o -> s (r o)", r=PACK))
         load_q(0)
         for i in range(len(K_LOADS)):
-            load(k_raw[i][:], kT.rearrange(features, j=PACK)[:, :, K_LOADS[i][0]:K_LOADS[i][1]])
+            load_k(i)
         load_q(1)
         load_q(2)
-        load_mask(0, 0, 2)
-        load_mask(0, 2, PACK)
-        load_mask(1, 0, 2)
-        load_mask(1, 2, 3)
-        load_mask(1, 3, PACK)
+        load_mask(0)
+        load_mask(1)
         load_q(3)
-        load(v_raw[:].rearrange("p h j e -> p h (j e)"), v.rearrange("h (s r) e -> s h (r e)", r=PACK))
+        nc.sync.dma_start(out=v_raw[:].rearrange("p h r e -> p h (r e)"), in_=v.rearrange("h (s r) e -> s h (r e)", r=PACK))
         load_mask(2)
         for h in range(H):
-            load(og_sb[h][:], og.rearrange("h (n p) e -> h p n e", p=QT)[h])
-        load(gn_sb[:], gn)
+            nc.sync.dma_start(out=og_sb[h][:], in_=og.rearrange("h (n p) e -> h p n e", p=QT)[h])
+        nc.sync.dma_start(out=gn_sb[:], in_=gn)
 
         nc.scalar.activation(out=table_probe[:], in_=t_sb[:, 0:1], func=ACT.Sigmoid)
-        for first in range(0, QT, QT // 8):
-            prepare_q(nc.vector, 0, first, first + QT // 8)
+
+        for first in range(0, QT, QT // Q_PIECES):
+            round_q(nc.vector, 0, first, first + QT // Q_PIECES)
         quantize_q(0)
-        warm_up(WARM_UP_PASSES)
-        for group in range(2):
-            for first in range(0, 64, 32):
-                round_k(nc.vector, 0, slice(group, group + 1), slice(first, first + 32))
+        warm_up(FIRST_WARM_UP)
+        for pair in range(2):
+            for first in range(0, WINDOW, WINDOW // K_PIECES):
+                round_k(nc.vector, 0, slice(pair, pair + 1), slice(first, first + WINDOW // K_PIECES))
         quantize_k(0)
         round_k(nc.scalar, 1, slice(0, 2))
-        round_k(nc.scalar, 2, slice(0, 1), slice(0, 16))
-        round_k(nc.vector, 2, slice(0, 1), slice(16, 32))
+        round_k(nc.scalar, 2, slice(0, 1), slice(0, WINDOW // 4))
+        round_k(nc.vector, 2, slice(0, 1), slice(WINDOW // 4, WINDOW // 2))
         round_k(nc.vector, 2, slice(1, 2))
         quantize_k(1)
         scores(0)
-        prepare_q(nc.vector, 1)
-        prepare_q(nc.scalar, 2, 0, QT // 4)
-        prepare_q(nc.vector, 2, QT // 4, QT)
+
+        round_q(nc.vector, 1)
+        round_q(nc.scalar, 2, 0, QT // 4)
+        round_q(nc.vector, 2, QT // 4, QT)
         quantize_q(1)
-        tanh(0, 0, 0, 1)
-        tanh(0, 1, 0, 1)
+        for h in range(H):
+            tanh(0, h, 0, 1)
         scores(1)
-        tanh(0, 0, 1, PACK)
-        tanh(0, 1, 1, PACK)
-        scale_mask(nc.scalar, 1, range(3, PACK))
+        for h in range(H):
+            tanh(0, h, 1, PACK)
+        scale_mask(nc.scalar, 1, range(PACK - 1, PACK))
         scale_mask(nc.vector, 0)
         quantize_q(2)
-        scale_mask(nc.vector, 1, range(3))
-        weigh(0, 0, 1)
-        weigh(0, 1, H)
-        prepare_q(nc.vector, 3)
-        quantize_w(0, 2)
+        scale_mask(nc.vector, 1, range(PACK - 1))
+        for h in range(H):
+            weigh(0, h, h + 1)
+        round_q(nc.vector, 3)
+        quantize_w(0, H)
         quantize_q(3)
         scores(2)
-        warm_up(11)
-        tanh(1, 0)
-        tanh(1, 1)
+        warm_up(SECOND_WARM_UP)
+        for h in range(H):
+            tanh(1, h)
         scores(3)
         weigh(1)
+
         tanh(2, 0)
-        round_v(nc.scalar, 0, V_SPLIT)
+        round_v(nc.scalar, 0, V_ON_SCALAR)
         tanh(2, 1)
-        tanh(3, 0)
-        tanh(3, 1)
-        round_v(nc.vector, V_SPLIT, E)
+        for h in range(H):
+            tanh(LAST, h)
+        round_v(nc.vector, V_ON_SCALAR, E)
         scale_mask(nc.vector, 2)
         quantize(v_codes[:], v_scales[:], v_bf[:].rearrange("p h c -> p (h c)"))
-        quantize_w(2, 4)
+        quantize_w(H, 2 * H)
         weigh(2)
-        values(0, 4)
+        values(0, 2 * H)
+
         for h in range(H):
             nc.scalar.activation(out=sigmoid[:, h::H, :], in_=og_sb[h][:], func=ACT.Sigmoid)
-        sum_squares(0, 4)
-        inverse_rms(0, 4)
-        weigh(3, 0, 1)
-        quantize_w(4, 6)
-        values(4, 6)
-        weigh(3, 1, H)
-        quantize_w(6, 7)
+        sum_squares(0, 2 * H)
+        inverse_rms(0, 2 * H)
+
+        weigh(LAST, 0, 1)
+        quantize_w(2 * H, LAST * H)
+        values(2 * H, LAST * H)
+        weigh(LAST, 1, H)
+        quantize_w(UNITS - 2, UNITS - 1)
         gate_gain(nc.vector, 0, 1)
-        quantize_w(7, 8)
-        gate_gain(nc.gpsimd, 5, 7)
-        gate_gain(nc.gpsimd, 7, 8)
-        gate_gain(nc.vector, 1, 2)
-        gate_gain(nc.vector, 2, 5)
-        values(6, 8)
-        sum_squares(4, 6)
-        inverse_rms(4, 5)
-        sum_squares(6, 7)
-        inverse_rms(5, 6)
-        sum_squares(7, 8)
-        inverse_rms(6, 7)
-        inverse_rms(7, 8)
-        for u in range(UNITS): finish(u)
+        quantize_w(UNITS - 1, UNITS)
+        gate_gain(nc.gpsimd, GATES_ON_VECTOR, UNITS - 1)
+        gate_gain(nc.gpsimd, UNITS - 1, UNITS)
+        gate_gain(nc.vector, 1, H)
+        gate_gain(nc.vector, H, GATES_ON_VECTOR)
+        values(LAST * H, UNITS)
+
+        sum_squares(2 * H, 2 * H + 1)
+        for u in range(2 * H + 1, UNITS):
+            sum_squares(u, u + 1)
+            inverse_rms(u - 1, u)
+        inverse_rms(UNITS - 1, UNITS)
+        for u in range(UNITS):
+            finish(u)

@@ -27,7 +27,7 @@ MASK_ROWS = (((0, 2), (2, PACK)), ((0, 2), (2, 3), (3, PACK)), ((0, PACK),))
 W_UNITS = 2 * H
 V_ON_SCALAR = 52
 GATES_ON_VECTOR = 5
-Q_PIECES, K_PIECES = 8, 2
+Q_PIECES, K_PIECES = 4, 2
 FIRST_WARM_UP = 12
 SECOND_WARM_UP = 11
 DMA_ALIGN = 256
@@ -58,7 +58,9 @@ def tile_rows_a_tanh_mask_onorm_gate_kernel(tc, qT, kT, t, v, mask, gn, og, out)
         v_raw = tile("v_raw", [P, H, PACK, E], F32)
         v_bf = tile("v_bf", [P, H, PACK * E], BF16)
         v_codes, v_scales = tile("v_codes", [P, H * E], U32), tile("v_scales", [P, H * E], U8)
-        t_sb, gn_sb = tile("t_sb", [P, PACK], F32), tile("gn_sb", [P, E], F32)
+        t_rows, t_dealt, t_turned = tiles("t_", 3, [P, P], F32)
+        t_sb = t_turned[:, 0:P:32]
+        gn_sb = tile("gn_sb", [P, E], F32)
         og_sb = tiles("og_sb", H, [P, TILES, E], F32)
         gate = tile("gate", [P, GATES_ON_VECTOR, E], F32)
         sigmoid = tile("sigmoid", [P, UNITS, E], F32)
@@ -208,7 +210,8 @@ def tile_rows_a_tanh_mask_onorm_gate_kernel(tc, qT, kT, t, v, mask, gn, og, out)
             elif h == H - 1:
                 nc.sync.dma_start(out=out.rearrange("h (n p) e -> n p h e", p=QT)[n], in_=result[n][:])
 
-        nc.scalar.dma_start(out=t_sb[:], in_=t.rearrange("(s r) o -> s (r o)", r=PACK))
+        nc.vector.memset(t_rows[:], 0.0)
+        nc.scalar.dma_start(out=t_rows[0:P:32, :], in_=t.rearrange("(g c) o -> g (c o)", c=P))
         load_q(0)
         for i in range(len(K_LOADS)):
             load_k(i)
@@ -223,7 +226,7 @@ def tile_rows_a_tanh_mask_onorm_gate_kernel(tc, qT, kT, t, v, mask, gn, og, out)
             nc.sync.dma_start(out=og_sb[h][:], in_=og.rearrange("h (n p) e -> h p n e", p=QT)[h])
         nc.sync.dma_start(out=gn_sb[:], in_=gn)
 
-        nc.scalar.activation(out=table_probe[:], in_=t_sb[:, 0:1], func=ACT.Sigmoid)
+        nc.scalar.activation(out=table_probe[:], in_=q_raw[0][:, 0, 0:1], func=ACT.Sigmoid)
 
         for first in range(0, QT, QT // Q_PIECES):
             round_q(nc.vector, 0, first, first + QT // Q_PIECES)
@@ -237,10 +240,12 @@ def tile_rows_a_tanh_mask_onorm_gate_kernel(tc, qT, kT, t, v, mask, gn, og, out)
         round_k(nc.scalar, 2, slice(0, 1), slice(0, WINDOW // 4))
         round_k(nc.vector, 2, slice(0, 1), slice(WINDOW // 4, WINDOW // 2))
         round_k(nc.vector, 2, slice(1, 2))
+        nc.vector.tensor_copy(out=t_dealt[:].rearrange("p (r b) -> p r b", r=PACK), in_=t_rows[:].rearrange("p (b r) -> p r b", r=PACK))
         quantize_k(1)
         scores(0)
 
         round_q(nc.vector, 1)
+        nc.vector.transpose(out=t_turned[:], in_=t_dealt[:])
         round_q(nc.scalar, 2, 0, QT // 4)
         round_q(nc.vector, 2, QT // 4, QT)
         quantize_q(1)

@@ -211,10 +211,11 @@ def tile_rows_a_tanh_mask_onorm_gate_kernel(tc, qT, kT, t, v, mask, gn, og, out)
                 nc.sync.dma_start(out=out.rearrange("h (n p) e -> n p h e", p=QT)[n], in_=result[n][:])
 
         nc.vector.memset(t_rows[:], 0.0)
-        nc.scalar.dma_start(out=t_rows[0:P:32, :], in_=t.rearrange("(g c) o -> g (c o)", c=P))
         load_q(0)
-        for i in range(len(K_LOADS)):
-            load_k(i)
+        load_k(0)
+        nc.sync.dma_start(out=t_rows[0:P:32, :], in_=t.rearrange("(g c) o -> g (c o)", c=P))
+        load_k(1)
+        load_k(2)
         load_q(1)
         load_q(2)
         load_mask(0)

@@ -13,6 +13,7 @@ ALU = mybir.AluOpType
 H, D, NQ, N, E = 2, 256, 512, 512, 128
 P = 128
 PACK = 4
+BLOCK = 32
 RUN = 4
 ROWS = D // PACK
 QT = 128
@@ -59,7 +60,7 @@ def tile_rows_a_tanh_mask_onorm_gate_kernel(tc, qT, kT, t, v, mask, gn, og, out)
         v_bf = tile("v_bf", [P, H, PACK * E], BF16)
         v_codes, v_scales = tile("v_codes", [P, H * E], U32), tile("v_scales", [P, H * E], U8)
         t_rows, t_dealt, t_turned = tiles("t_", 3, [P, P], F32)
-        t_sb = t_turned[:, 0:P:32]
+        t_sb = t_turned[:, 0:P:BLOCK]
         gn_sb = tile("gn_sb", [P, E], F32)
         og_sb = tiles("og_sb", H, [P, TILES, E], F32)
         gate = tile("gate", [P, GATES_ON_VECTOR, E], F32)
@@ -82,9 +83,9 @@ def tile_rows_a_tanh_mask_onorm_gate_kernel(tc, qT, kT, t, v, mask, gn, og, out)
         def load_q(n):
             nc.sync.dma_start(out=q_raw[n][:], in_=by_features(qT)[:, :, n * QT:(n + 1) * QT])
 
-        def load_k(i):
-            first, last = K_LOADS[i]
-            nc.sync.dma_start(out=k_raw[i][:], in_=by_features(kT)[:, :, first:last])
+        def load_k(piece):
+            first, last = K_LOADS[piece]
+            nc.sync.dma_start(out=k_raw[piece][:], in_=by_features(kT)[:, :, first:last])
 
         def load_mask(m):
             a, b = MASK_PARTS[m]
@@ -101,11 +102,11 @@ def tile_rows_a_tanh_mask_onorm_gate_kernel(tc, qT, kT, t, v, mask, gn, og, out)
         def quantize(codes, scales, src):
             nc.vector.quantize_mx(out=codes.bitcast(FP8X4), scales=scales, in_=src)
 
-        def round_k(engine, i, pairs, columns=slice(None)):
-            first, last = K_LOADS[i]
+        def round_k(engine, piece, pairs, columns=slice(None)):
+            first, last = K_LOADS[piece]
             half = first // HALF
             window = k_bf[half][:, :, first - half * HALF:last - half * HALF].rearrange("p (g r) (s j) -> p g s j r", r=2, j=PACK)
-            source = k_raw[i][:].rearrange("p j (s g r) -> p g s j r", g=2, r=2)
+            source = k_raw[piece][:].rearrange("p j (s g r) -> p g s j r", g=2, r=2)
             copy(engine, window[:, pairs, columns], source[:, pairs, columns])
 
         def quantize_k(half):
@@ -157,7 +158,7 @@ def tile_rows_a_tanh_mask_onorm_gate_kernel(tc, qT, kT, t, v, mask, gn, og, out)
             return buffers[first // W_UNITS][:, offset:offset + last - first, :]
 
         def weigh(n, first=0, last=H):
-            m = [i for i, (a, b) in enumerate(MASK_PARTS) if a <= n < b][0]
+            m = [part for part, (a, b) in enumerate(MASK_PARTS) if a <= n < b][0]
             offset = (n - MASK_PARTS[m][0]) * PACK * QT
             scaled_mask = mask_t[m][:, offset:offset + PACK * QT].unsqueeze(1).broadcast_to([P, last - first, PACK * QT])
             nc.vector.tensor_tensor(
@@ -180,7 +181,7 @@ def tile_rows_a_tanh_mask_onorm_gate_kernel(tc, qT, kT, t, v, mask, gn, og, out)
                                     rhs=v_codes[:, cols].bitcast(FP8X4), rhs_scale=v_scales[:, cols], start=True, stop=True)
 
         def warm_up(passes):
-            for i in range(passes):
+            for number in range(passes):
                 nc.tensor.matmul_mx(out=y_bank[LAST][:, 0:E], lhsT=q_codes[0][:].bitcast(FP8X4), lhsT_scale=q_scales[0][:],
                                     rhs=q_codes[0][:].bitcast(FP8X4), rhs_scale=q_scales[0][:], start=True, stop=True)
 
@@ -212,10 +213,9 @@ def tile_rows_a_tanh_mask_onorm_gate_kernel(tc, qT, kT, t, v, mask, gn, og, out)
 
         nc.vector.memset(t_rows[:], 0.0)
         load_q(0)
-        load_k(0)
-        nc.sync.dma_start(out=t_rows[0:P:32, :], in_=t.rearrange("(g c) o -> g (c o)", c=P))
-        load_k(1)
-        load_k(2)
+        nc.sync.dma_start(out=t_rows[0:P:BLOCK, :], in_=t.rearrange("(g c) o -> g (c o)", c=P))
+        for piece in range(len(K_LOADS)):
+            load_k(piece)
         load_q(1)
         load_q(2)
         load_mask(0)
@@ -231,7 +231,10 @@ def tile_rows_a_tanh_mask_onorm_gate_kernel(tc, qT, kT, t, v, mask, gn, og, out)
 
         for first in range(0, QT, QT // Q_PIECES):
             round_q(nc.vector, 0, first, first + QT // Q_PIECES)
+        nc.vector.tensor_copy(out=t_dealt[:].rearrange("p (r b) -> p r b", r=PACK),
+                              in_=t_rows[:].rearrange("p (b r) -> p r b", r=PACK))
         quantize_q(0)
+        nc.vector.transpose(out=t_turned[:], in_=t_dealt[:])
         warm_up(FIRST_WARM_UP)
         for pair in range(2):
             for first in range(0, WINDOW, WINDOW // K_PIECES):
@@ -241,12 +244,10 @@ def tile_rows_a_tanh_mask_onorm_gate_kernel(tc, qT, kT, t, v, mask, gn, og, out)
         round_k(nc.scalar, 2, slice(0, 1), slice(0, WINDOW // 4))
         round_k(nc.vector, 2, slice(0, 1), slice(WINDOW // 4, WINDOW // 2))
         round_k(nc.vector, 2, slice(1, 2))
-        nc.vector.tensor_copy(out=t_dealt[:].rearrange("p (r b) -> p r b", r=PACK), in_=t_rows[:].rearrange("p (b r) -> p r b", r=PACK))
         quantize_k(1)
         scores(0)
 
         round_q(nc.vector, 1)
-        nc.vector.transpose(out=t_turned[:], in_=t_dealt[:])
         round_q(nc.scalar, 2, 0, QT // 4)
         round_q(nc.vector, 2, QT // 4, QT)
         quantize_q(1)

@@ -26,11 +26,11 @@ K_LOADS = ((0, HALF), (HALF, 3 * N // 4), (3 * N // 4, N))
 MASK_PARTS = ((0, 1), (1, 2), (2, TILES))
 MASK_ROWS = (((0, 2), (2, PACK)), ((0, 2), (2, 3), (3, PACK)), ((0, PACK),))
 W_UNITS = 2 * H
-V_ON_SCALAR = 52
+V_ON_SCALAR = 36
 GATES_ON_VECTOR = 5
 Q_PIECES, K_PIECES = 4, 2
-FIRST_WARM_UP = 12
-SECOND_WARM_UP = 11
+Q1_ON_SCALAR, Q2_ON_SCALAR = 96, 84
+FREE_BANK_LEAD = 2
 DMA_ALIGN = 256
 FLOPS = 2 * H * N * NQ * D + 2 * H * NQ * N * E
 
@@ -136,17 +136,24 @@ def tile_rows_a_tanh_mask_onorm_gate_kernel(tc, qT, kT, t, v, mask, gn, og, out)
 
         def score_bank_of(n, h, r):
             if n == 0:
-                return score_bank[2 * h + min(r, 1)]
-            return score_bank[2 * h + (n + 1) % 2]
+                return score_bank[r // 2] if h == 0 else score_bank[2]
+            return score_bank[2 * h + (n + h + 1) % 2]
 
-        def scores(n):
-            for r in range(PACK):
-                for h in range(H):
-                    rows, cols = slice(h * ROWS, (h + 1) * ROWS), slice(r * QT, (r + 1) * QT)
-                    nc.tensor.matmul_mx(out=score_bank_of(n, h, r)[:, cols],
-                                        lhsT=k_codes[rows, cols].bitcast(FP8X4), lhsT_scale=k_scales[rows, cols],
-                                        rhs=q_codes[n][rows, :].bitcast(FP8X4), rhs_scale=q_scales[n][rows, :],
-                                        start=True, stop=True)
+        def score_pass(n, h, r):
+            rows, cols = slice(h * ROWS, (h + 1) * ROWS), slice(r * QT, (r + 1) * QT)
+            nc.tensor.matmul_mx(out=score_bank_of(n, h, r)[:, cols],
+                                lhsT=k_codes[rows, cols].bitcast(FP8X4), lhsT_scale=k_scales[rows, cols],
+                                rhs=q_codes[n][rows, :].bitcast(FP8X4), rhs_scale=q_scales[n][rows, :],
+                                start=True, stop=True)
+
+        def scores(n, lead=0):
+            for step in range(PACK + lead):
+                if lead and step < PACK:
+                    score_pass(n, 1, step)
+                if step >= lead:
+                    score_pass(n, 0, step - lead)
+                if not lead:
+                    score_pass(n, 1, step)
 
         def tanh(n, h, first=0, last=PACK):
             dst = weights[n][:, h, :].rearrange("p (c r i) -> p c r i", r=PACK, i=RUN)
@@ -179,11 +186,6 @@ def tile_rows_a_tanh_mask_onorm_gate_kernel(tc, qT, kT, t, v, mask, gn, og, out)
                 nc.tensor.matmul_mx(out=y_of(u), lhsT=w_place(w_codes, u, u + 1)[:, 0, :].bitcast(FP8X4),
                                     lhsT_scale=w_place(w_scales, u, u + 1)[:, 0, :],
                                     rhs=v_codes[:, cols].bitcast(FP8X4), rhs_scale=v_scales[:, cols], start=True, stop=True)
-
-        def warm_up(passes):
-            for number in range(passes):
-                nc.tensor.matmul_mx(out=y_bank[LAST][:, 0:E], lhsT=q_codes[0][:].bitcast(FP8X4), lhsT_scale=q_scales[0][:],
-                                    rhs=q_codes[0][:].bitcast(FP8X4), rhs_scale=q_scales[0][:], start=True, stop=True)
 
         def sum_squares(first, last):
             for u in range(first, last):
@@ -235,7 +237,6 @@ def tile_rows_a_tanh_mask_onorm_gate_kernel(tc, qT, kT, t, v, mask, gn, og, out)
                               in_=t_rows[:].rearrange("p (b r) -> p r b", r=PACK))
         quantize_q(0)
         nc.vector.transpose(out=t_turned[:], in_=t_dealt[:])
-        warm_up(FIRST_WARM_UP)
         for pair in range(2):
             for first in range(0, WINDOW, WINDOW // K_PIECES):
                 round_k(nc.vector, 0, slice(pair, pair + 1), slice(first, first + WINDOW // K_PIECES))
@@ -247,27 +248,26 @@ def tile_rows_a_tanh_mask_onorm_gate_kernel(tc, qT, kT, t, v, mask, gn, og, out)
         quantize_k(1)
         scores(0)
 
-        round_q(nc.vector, 1)
-        round_q(nc.scalar, 2, 0, QT // 4)
-        round_q(nc.vector, 2, QT // 4, QT)
+        round_q(nc.scalar, 1, 0, Q1_ON_SCALAR)
+        round_q(nc.vector, 1, Q1_ON_SCALAR, QT)
+        round_q(nc.scalar, 2, 0, Q2_ON_SCALAR)
+        round_q(nc.vector, 2, Q2_ON_SCALAR, QT)
         quantize_q(1)
-        for h in range(H):
-            tanh(0, h, 0, 1)
-        scores(1)
-        for h in range(H):
-            tanh(0, h, 1, PACK)
+        tanh(0, 0, 0, 2)
+        scores(1, FREE_BANK_LEAD)
+        tanh(0, 0, 2, PACK)
+        tanh(0, 1)
         scale_mask(nc.scalar, 1, range(PACK - 1, PACK))
         scale_mask(nc.vector, 0)
         quantize_q(2)
         scale_mask(nc.vector, 1, range(PACK - 1))
-        for h in range(H):
-            weigh(0, h, h + 1)
+        weigh(0, 0, 1)
+        weigh(0, 1, 2)
         round_q(nc.vector, 3)
         quantize_w(0, H)
         quantize_q(3)
         scores(2)
-        warm_up(SECOND_WARM_UP)
-        for h in range(H):
+        for h in reversed(range(H)):
             tanh(1, h)
         scores(3)
         weigh(1)

@@ -26,7 +26,7 @@ K_LOADS = ((0, HALF), (HALF, 3 * N // 4), (3 * N // 4, N))
 MASK_PARTS = ((0, 1), (1, 2), (2, TILES))
 MASK_ROWS = (((0, 2), (2, PACK)), ((0, 2), (2, 3), (3, PACK)), ((0, PACK),))
 W_UNITS = 2 * H
-V_ON_SCALAR = 36
+V_ON_SCALAR = 44
 GATES_ON_VECTOR = 5
 Q_PIECES, K_PIECES = 4, 2
 Q1_ON_SCALAR, Q2_ON_SCALAR = 96, 84
@@ -146,14 +146,12 @@ def tile_rows_a_tanh_mask_onorm_gate_kernel(tc, qT, kT, t, v, mask, gn, og, out)
                                 rhs=q_codes[n][rows, :].bitcast(FP8X4), rhs_scale=q_scales[n][rows, :],
                                 start=True, stop=True)
 
-        def scores(n, lead=0):
+        def scores(n, leader=0, lead=0):
             for step in range(PACK + lead):
-                if lead and step < PACK:
-                    score_pass(n, 1, step)
+                if step < PACK:
+                    score_pass(n, leader, step)
                 if step >= lead:
-                    score_pass(n, 0, step - lead)
-                if not lead:
-                    score_pass(n, 1, step)
+                    score_pass(n, 1 - leader, step - lead)
 
         def tanh(n, h, first=0, last=PACK):
             dst = weights[n][:, h, :].rearrange("p (c r i) -> p c r i", r=PACK, i=RUN)
@@ -254,15 +252,15 @@ def tile_rows_a_tanh_mask_onorm_gate_kernel(tc, qT, kT, t, v, mask, gn, og, out)
         round_q(nc.vector, 2, Q2_ON_SCALAR, QT)
         quantize_q(1)
         tanh(0, 0, 0, 2)
-        scores(1, FREE_BANK_LEAD)
+        scores(1, 1, FREE_BANK_LEAD)
         tanh(0, 0, 2, PACK)
         tanh(0, 1)
         scale_mask(nc.scalar, 1, range(PACK - 1, PACK))
         scale_mask(nc.vector, 0)
         quantize_q(2)
         scale_mask(nc.vector, 1, range(PACK - 1))
-        weigh(0, 0, 1)
-        weigh(0, 1, 2)
+        for h in range(H):
+            weigh(0, h, h + 1)
         round_q(nc.vector, 3)
         quantize_w(0, H)
         quantize_q(3)

@@ -26,11 +26,11 @@ K_LOADS = ((0, HALF), (HALF, 3 * N // 4), (3 * N // 4, N))
 MASK_PARTS = ((0, 1), (1, 2), (2, TILES))
 MASK_ROWS = (((0, 2), (2, PACK)), ((0, 2), (2, 3), (3, PACK)), ((0, PACK),))
 W_UNITS = 2 * H
-V_ON_SCALAR = 44
+V_ON_SCALAR = 40
 GATES_ON_VECTOR = 5
 Q_PIECES, K_PIECES = 4, 2
 Q1_ON_SCALAR, Q2_ON_SCALAR = 96, 84
-FREE_BANK_LEAD = 2
+LEAD = 2
 DMA_ALIGN = 256
 FLOPS = 2 * H * N * NQ * D + 2 * H * NQ * N * E
 
@@ -252,7 +252,7 @@ def tile_rows_a_tanh_mask_onorm_gate_kernel(tc, qT, kT, t, v, mask, gn, og, out)
         round_q(nc.vector, 2, Q2_ON_SCALAR, QT)
         quantize_q(1)
         tanh(0, 0, 0, 2)
-        scores(1, 1, FREE_BANK_LEAD)
+        scores(1, 1, LEAD)
         tanh(0, 0, 2, PACK)
         tanh(0, 1)
         scale_mask(nc.scalar, 1, range(PACK - 1, PACK))
@@ -264,10 +264,10 @@ def tile_rows_a_tanh_mask_onorm_gate_kernel(tc, qT, kT, t, v, mask, gn, og, out)
         round_q(nc.vector, 3)
         quantize_w(0, H)
         quantize_q(3)
-        scores(2)
+        scores(2, 0, LEAD)
         for h in reversed(range(H)):
             tanh(1, h)
-        scores(3)
+        scores(LAST, 0, LEAD)
         weigh(1)
 
         tanh(2, 0)

@@ -29,8 +29,9 @@ W_UNITS = 2 * H
 V_ON_SCALAR = 40
 GATES_ON_VECTOR = 5
 Q_PIECES, K_PIECES = 4, 2
-Q1_ON_SCALAR, Q2_ON_SCALAR = 96, 84
+Q1_ON_SCALAR, Q2_ON_SCALAR = 96, 64
 LEAD = 2
+FIRST_LEAD = 1
 DMA_ALIGN = 256
 FLOPS = 2 * H * N * NQ * D + 2 * H * NQ * N * E
 
@@ -244,7 +245,7 @@ def tile_rows_a_tanh_mask_onorm_gate_kernel(tc, qT, kT, t, v, mask, gn, og, out)
         round_k(nc.vector, 2, slice(0, 1), slice(WINDOW // 4, WINDOW // 2))
         round_k(nc.vector, 2, slice(1, 2))
         quantize_k(1)
-        scores(0)
+        scores(0, 0, FIRST_LEAD)
 
         round_q(nc.scalar, 1, 0, Q1_ON_SCALAR)
         round_q(nc.vector, 1, Q1_ON_SCALAR, QT)

@@ -26,10 +26,10 @@ K_LOADS = ((0, HALF), (HALF, 3 * N // 4), (3 * N // 4, N))
 MASK_PARTS = ((0, 1), (1, 2), (2, TILES))
 MASK_ROWS = (((0, 2), (2, PACK)), ((0, 2), (2, 3), (3, PACK)), ((0, PACK),))
 W_UNITS = 2 * H
-V_ON_SCALAR = 40
+V_ON_SCALAR = 60
 GATES_ON_VECTOR = 5
-Q_PIECES, K_PIECES = 4, 2
-Q1_ON_SCALAR, Q2_ON_SCALAR = 96, 64
+Q_PIECES, K_PIECES = 4, 4
+Q1_ON_SCALAR, Q2_ON_SCALAR = 96, 48
 LEAD = 2
 FIRST_LEAD = 1
 DMA_ALIGN = 256
@@ -110,8 +110,8 @@ def tile_rows_a_tanh_mask_onorm_gate_kernel(tc, qT, kT, t, v, mask, gn, og, out)
             source = k_raw[piece][:].rearrange("p j (s g r) -> p g s j r", g=2, r=2)
             copy(engine, window[:, pairs, columns], source[:, pairs, columns])
 
-        def quantize_k(half):
-            for r in range(PACK):
+        def quantize_k(half, groups=range(PACK)):
+            for r in groups:
                 cols = slice(r * QT + half * WINDOW, r * QT + (half + 1) * WINDOW)
                 quantize(k_codes[:, cols], k_scales[:, cols], k_bf[half][:, r, :])
 
@@ -236,14 +236,14 @@ def tile_rows_a_tanh_mask_onorm_gate_kernel(tc, qT, kT, t, v, mask, gn, og, out)
                               in_=t_rows[:].rearrange("p (b r) -> p r b", r=PACK))
         quantize_q(0)
         nc.vector.transpose(out=t_turned[:], in_=t_dealt[:])
-        for pair in range(2):
-            for first in range(0, WINDOW, WINDOW // K_PIECES):
-                round_k(nc.vector, 0, slice(pair, pair + 1), slice(first, first + WINDOW // K_PIECES))
-        quantize_k(0)
-        round_k(nc.scalar, 1, slice(0, 2))
-        round_k(nc.scalar, 2, slice(0, 1), slice(0, WINDOW // 4))
-        round_k(nc.vector, 2, slice(0, 1), slice(WINDOW // 4, WINDOW // 2))
-        round_k(nc.vector, 2, slice(1, 2))
+        for first in range(0, WINDOW, WINDOW // K_PIECES):
+            round_k(nc.vector, 0, slice(0, 1), slice(first, first + WINDOW // K_PIECES))
+        for piece in range(len(K_LOADS)):
+            round_k(nc.scalar, piece, slice(1, 2))
+        quantize_k(0, range(0, 2))
+        round_k(nc.vector, 1, slice(0, 1))
+        quantize_k(0, range(2, PACK))
+        round_k(nc.vector, 2, slice(0, 1))
         quantize_k(1)
         scores(0, 0, FIRST_LEAD)
 

@@ -26,7 +26,7 @@ K_LOADS = ((0, HALF), (HALF, 3 * N // 4), (3 * N // 4, N))
 MASK_PARTS = ((0, 1), (1, 2), (2, TILES))
 MASK_ROWS = (((0, 2), (2, PACK)), ((0, 2), (2, 3), (3, PACK)), ((0, PACK),))
 W_UNITS = 2 * H
-V_ON_SCALAR = 60
+V_ON_SCALAR = 44
 GATES_ON_VECTOR = 5
 Q_PIECES, K_PIECES = 4, 4
 Q1_ON_SCALAR, Q2_ON_SCALAR = 96, 48

@@ -26,7 +26,7 @@ K_LOADS = ((0, HALF), (HALF, 3 * N // 4), (3 * N // 4, N))
 MASK_PARTS = ((0, 1), (1, 2), (2, TILES))
 MASK_ROWS = (((0, 2), (2, PACK)), ((0, 2), (2, 3), (3, PACK)), ((0, PACK),))
 W_UNITS = 2 * H
-V_ON_SCALAR = 44
+V_ON_SCALAR = 52
 GATES_ON_VECTOR = 5
 Q_PIECES, K_PIECES = 4, 4
 Q1_ON_SCALAR, Q2_ON_SCALAR = 96, 48
@@ -268,7 +268,7 @@ def tile_rows_a_tanh_mask_onorm_gate_kernel(tc, qT, kT, t, v, mask, gn, og, out)
         scores(2, 0, LEAD)
         for h in reversed(range(H)):
             tanh(1, h)
-        scores(LAST, 0, LEAD)
+        scores(LAST, 0, PACK)
         weigh(1)
 
         tanh(2, 0)

@@ -27,6 +27,7 @@ MASK_PARTS = ((0, 1), (1, 2), (2, TILES))
 MASK_ROWS = (((0, 2), (2, PACK)), ((0, 2), (2, 3), (3, PACK)), ((0, PACK),))
 W_UNITS = 2 * H
 V_ON_SCALAR = 52
+EARLY = 3
 GATES_ON_VECTOR = 5
 Q_PIECES, K_PIECES = 4, 4
 Q1_ON_SCALAR, Q2_ON_SCALAR = 96, 48
@@ -285,8 +286,8 @@ def tile_rows_a_tanh_mask_onorm_gate_kernel(tc, qT, kT, t, v, mask, gn, og, out)
 
         for h in range(H):
             nc.scalar.activation(out=sigmoid[:, h::H, :], in_=og_sb[h][:], func=ACT.Sigmoid)
-        sum_squares(0, 2 * H)
-        inverse_rms(0, 2 * H)
+        sum_squares(0, EARLY)
+        inverse_rms(0, EARLY)
 
         weigh(LAST, 0, 1)
         quantize_w(2 * H, LAST * H)
@@ -301,10 +302,12 @@ def tile_rows_a_tanh_mask_onorm_gate_kernel(tc, qT, kT, t, v, mask, gn, og, out)
         gate_gain(nc.vector, H, GATES_ON_VECTOR)
         values(LAST * H, UNITS)
 
-        sum_squares(2 * H, 2 * H + 1)
-        for u in range(2 * H + 1, UNITS):
-            sum_squares(u, u + 1)
-            inverse_rms(u - 1, u)
-        inverse_rms(UNITS - 1, UNITS)
+        sum_squares(EARLY, LAST * H)
+        inverse_rms(EARLY, 2 * H)
+        sum_squares(UNITS - 2, UNITS - 1)
+        inverse_rms(2 * H, LAST * H)
+        sum_squares(UNITS - 1, UNITS)
+        for u in range(LAST * H, UNITS):
+            inverse_rms(u, u + 1)
         for u in range(UNITS):
             finish(u)

from contextlib import ExitStack

import concourse.mybir as mybir

F32 = mybir.dt.float32
BF16 = mybir.dt.bfloat16
U32 = mybir.dt.uint32
U8 = mybir.dt.uint8
FP8X4 = mybir.dt.float8_e4m3fn_x4
ACT = mybir.ActivationFunctionType
ALU = mybir.AluOpType

H, D, NQ, N, E = 2, 256, 512, 512, 128
P = 128
PACK = 4
BLOCK = 32
RUN = 4
ROWS = D // PACK
QT = 128
TILES = NQ // QT
UNITS = TILES * H
LAST = TILES - 1
HALF = N // 2
WINDOW = HALF // PACK
K_LOADS = ((0, HALF), (HALF, 3 * N // 4), (3 * N // 4, N))
MASK_PARTS = ((0, 1), (1, 2), (2, TILES))
MASK_ROWS = (((0, 2), (2, PACK)), ((0, 2), (2, 3), (3, PACK)), ((0, PACK),))
W_UNITS = 2 * H
V_ON_SCALAR = 52
EARLY = 3
GATES_ON_VECTOR = 5
Q_PIECES, K_PIECES = 4, 4
Q1_ON_SCALAR, Q2_ON_SCALAR = 96, 48
LEAD = 2
FIRST_LEAD = 1
DMA_ALIGN = 256
FLOPS = 2 * H * N * NQ * D + 2 * H * NQ * N * E


def tile_rows_a_tanh_mask_onorm_gate_kernel(tc, qT, kT, t, v, mask, gn, og, out):
    nc = tc.nc
    with ExitStack() as ctx:
        sb = ctx.enter_context(tc.tile_pool(name="sb", bufs=1))
        ps = ctx.enter_context(tc.psum_pool(name="ps", bufs=1))
        ctx.enter_context(tc.manual_schedule())

        def tile(name, shape, dtype):
            return sb.tile(shape, dtype, name=name, align_bytes=DMA_ALIGN)

        def tiles(name, count, shape, dtype):
            return [tile(name + str(i), shape, dtype) for i in range(count)]

        k_raw = [tile("k_raw" + str(a), [P, PACK, b - a], F32) for a, b in K_LOADS]
        k_bf = tiles("k_bf", 2, [P, PACK, HALF], BF16)
        k_codes, k_scales = tile("k_codes", [P, N], U32), tile("k_scales", [P, N], U8)
        q_raw = tiles("q_raw", TILES, [P, PACK, QT], F32)
        q_bf = tiles("q_bf", TILES, [P, PACK * QT], BF16)
        q_codes, q_scales = tiles("q_codes", TILES, [P, QT], U32), tiles("q_scales", TILES, [P, QT], U8)
        mask_raw = [tile("mask_raw" + str(a), [P, PACK, (b - a) * QT], F32) for a, b in MASK_PARTS]
        mask_t = [tile("mask_t" + str(a), [P, (b - a) * PACK * QT], F32) for a, b in MASK_PARTS]
        v_raw = tile("v_raw", [P, H, PACK, E], F32)
        v_bf = tile("v_bf", [P, H, PACK * E], BF16)
        v_codes, v_scales = tile("v_codes", [P, H * E], U32), tile("v_scales", [P, H * E], U8)
        t_rows, t_dealt, t_turned = tiles("t_", 3, [P, P], F32)
        t_sb = t_turned[:, 0:P:BLOCK]
        gn_sb = tile("gn_sb", [P, E], F32)
        og_sb = tiles("og_sb", H, [P, TILES, E], F32)
        gate = tile("gate", [P, GATES_ON_VECTOR, E], F32)
        sigmoid = tile("sigmoid", [P, UNITS, E], F32)
        weights = tiles("weights", TILES, [P, H, PACK * QT], F32)
        w_bf = tiles("w_bf", UNITS // W_UNITS, [P, W_UNITS, PACK * QT], BF16)
        w_codes = tiles("w_codes", UNITS // W_UNITS, [P, W_UNITS, QT], U32)
        w_scales = tiles("w_scales", UNITS // W_UNITS, [P, W_UNITS, QT], U8)
        squares = tiles("squares", UNITS, [P, E], BF16)
        sums, inv_rms = tile("sums", [P, UNITS], F32), tile("inv_rms", [P, UNITS], F32)
        result = tiles("result", TILES, [P, H, E], F32)
        table_probe = tile("table_probe", [P, 1], F32)
        score_bank = [ps.tile([P, PACK * QT], F32, name="score_bank" + str(i)) for i in range(2 * H)]
        y_bank = [ps.tile([P, PACK * QT], F32, name="y_bank" + str(i)) for i in range(TILES)]
        late_gate = w_bf[-1][:, W_UNITS - H:, :].rearrange("p h c -> p (h c)").bitcast(F32).rearrange("p (u e) -> p u e", e=E)

        def by_features(x):
            return x.rearrange("h (p j) c -> (h p) j c", j=PACK)

        def load_q(n):
            nc.sync.dma_start(out=q_raw[n][:], in_=by_features(qT)[:, :, n * QT:(n + 1) * QT])

        def load_k(piece):
            first, last = K_LOADS[piece]
            nc.sync.dma_start(out=k_raw[piece][:], in_=by_features(kT)[:, :, first:last])

        def load_mask(m):
            a, b = MASK_PARTS[m]
            for first, last in MASK_ROWS[m]:
                nc.sync.dma_start(out=mask_raw[m][:, first:last, :],
                                  in_=mask.rearrange("(s r) c -> s r c", r=PACK)[:, first:last, a * QT:b * QT])

        def copy(engine, dst, src):
            if engine is nc.vector:
                nc.vector.tensor_copy(out=dst, in_=src)
            else:
                nc.scalar.copy(out=dst, in_=src)

        def quantize(codes, scales, src):
            nc.vector.quantize_mx(out=codes.bitcast(FP8X4), scales=scales, in_=src)

        def round_k(engine, piece, pairs, columns=slice(None)):
            first, last = K_LOADS[piece]
            half = first // HALF
            window = k_bf[half][:, :, first - half * HALF:last - half * HALF].rearrange("p (g r) (s j) -> p g s j r", r=2, j=PACK)
            source = k_raw[piece][:].rearrange("p j (s g r) -> p g s j r", g=2, r=2)
            copy(engine, window[:, pairs, columns], source[:, pairs, columns])

        def quantize_k(half, groups=range(PACK)):
            for r in groups:
                cols = slice(r * QT + half * WINDOW, r * QT + (half + 1) * WINDOW)
                quantize(k_codes[:, cols], k_scales[:, cols], k_bf[half][:, r, :])

        def round_q(engine, n, first=0, last=QT):
            copy(engine, q_bf[n][:, first * PACK:last * PACK].rearrange("p (c i j) -> p c j i", i=RUN, j=PACK),
                 q_raw[n][:, :, first:last].rearrange("p j (c i) -> p c j i", i=RUN))

        def quantize_q(n):
            quantize(q_codes[n][:], q_scales[n][:], q_bf[n][:])

        def round_v(engine, first, last):
            copy(engine, v_bf[:, :, first * PACK:last * PACK].rearrange("p h (c i r) -> p h c r i", i=RUN, r=PACK),
                 v_raw[:, :, :, first:last].rearrange("p h r (c i) -> p h c r i", i=RUN))

        def scale_mask(engine, m, rows=range(PACK)):
            for r in rows:
                dst = mask_t[m][:].rearrange("p (c r i) -> p r c i", r=PACK, i=RUN)[:, r]
                src = mask_raw[m][:, r, :].rearrange("p (c i) -> p c i", i=RUN)
                if engine is nc.vector:
                    nc.vector.tensor_scalar(out=dst, in0=src, scalar1=t_sb[:, r:r + 1], scalar2=None, op0=ALU.mult)
                else:
                    nc.scalar.activation(out=dst, in_=src, func=ACT.Copy, scale=t_sb[:, r:r + 1])

        def score_bank_of(n, h, r):
            if n == 0:
                return score_bank[r // 2] if h == 0 else score_bank[2]
            return score_bank[2 * h + (n + h + 1) % 2]

        def score_pass(n, h, r):
            rows, cols = slice(h * ROWS, (h + 1) * ROWS), slice(r * QT, (r + 1) * QT)
            nc.tensor.matmul_mx(out=score_bank_of(n, h, r)[:, cols],
                                lhsT=k_codes[rows, cols].bitcast(FP8X4), lhsT_scale=k_scales[rows, cols],
                                rhs=q_codes[n][rows, :].bitcast(FP8X4), rhs_scale=q_scales[n][rows, :],
                                start=True, stop=True)

        def scores(n, leader=0, lead=0):
            for step in range(PACK + lead):
                if step < PACK:
                    score_pass(n, leader, step)
                if step >= lead:
                    score_pass(n, 1 - leader, step - lead)

        def tanh(n, h, first=0, last=PACK):
            dst = weights[n][:, h, :].rearrange("p (c r i) -> p c r i", r=PACK, i=RUN)
            src = score_bank_of(n, h, first)[:].rearrange("p (r c i) -> p c r i", r=PACK, i=RUN)
            nc.scalar.activation(out=dst[:, :, first:last], in_=src[:, :, first:last], func=ACT.Tanh)

        def w_place(buffers, first, last):
            offset = first % W_UNITS
            return buffers[first // W_UNITS][:, offset:offset + last - first, :]

        def weigh(n, first=0, last=H):
            m = [part for part, (a, b) in enumerate(MASK_PARTS) if a <= n < b][0]
            offset = (n - MASK_PARTS[m][0]) * PACK * QT
            scaled_mask = mask_t[m][:, offset:offset + PACK * QT].unsqueeze(1).broadcast_to([P, last - first, PACK * QT])
            nc.vector.tensor_tensor(
                out=w_place(w_bf, H * n + first, H * n + last).rearrange("p h (c i r) -> p h c r i", i=RUN, r=PACK),
                in0=weights[n][:, first:last, :].rearrange("p h (c r i) -> p h c r i", i=RUN, r=PACK),
                in1=scaled_mask.rearrange("p h (c r i) -> p h c r i", i=RUN, r=PACK), op=ALU.mult)

        def quantize_w(first, last):
            quantize(*[w_place(x, first, last).rearrange("p u c -> p (u c)") for x in (w_codes, w_scales, w_bf)])

        def y_of(u):
            n, h = divmod(u, H)
            return y_bank[n][:, h * E:(h + 1) * E]

        def values(first, last):
            for u in range(first, last):
                cols = slice(u % H * E, (u % H + 1) * E)
                nc.tensor.matmul_mx(out=y_of(u), lhsT=w_place(w_codes, u, u + 1)[:, 0, :].bitcast(FP8X4),
                                    lhsT_scale=w_place(w_scales, u, u + 1)[:, 0, :],
                                    rhs=v_codes[:, cols].bitcast(FP8X4), rhs_scale=v_scales[:, cols], start=True, stop=True)

        def sum_squares(first, last):
            for u in range(first, last):
                nc.scalar.activation(out=squares[u][:], in_=y_of(u), func=ACT.Square, accum_out=sums[:, u:u + 1])

        def inverse_rms(first, last):
            nc.scalar.activation(out=inv_rms[:, first:last], in_=sums[:, first:last], func=ACT.Abs_reciprocal_sqrt,
                                 scale=1.0 / E, bias=256.0 * 1e-5)

        def gate_of(first, last):
            if first < GATES_ON_VECTOR:
                return gate[:, first:last, :]
            return late_gate[:, first - GATES_ON_VECTOR:last - GATES_ON_VECTOR, :]

        def gate_gain(engine, first, last):
            engine.tensor_tensor(out=gate_of(first, last), in0=sigmoid[:, first:last, :],
                                 in1=gn_sb[:].unsqueeze(1).broadcast_to([P, last - first, E]), op=ALU.mult)

        def finish(u):
            n, h = divmod(u, H)
            nc.vector.scalar_tensor_tensor(out=result[n][:, h, :], in0=y_of(u), scalar=inv_rms[:, u:u + 1],
                                           in1=gate_of(u, u + 1)[:, 0, :], op0=ALU.mult, op1=ALU.mult)
            if n == LAST:
                nc.sync.dma_start(out=out[h, n * QT:(n + 1) * QT, :], in_=result[n][:, h, :])
            elif h == H - 1:
                nc.sync.dma_start(out=out.rearrange("h (n p) e -> n p h e", p=QT)[n], in_=result[n][:])

        nc.vector.memset(t_rows[:], 0.0)
        load_q(0)
        nc.sync.dma_start(out=t_rows[0:P:BLOCK, :], in_=t.rearrange("(g c) o -> g (c o)", c=P))
        for piece in range(len(K_LOADS)):
            load_k(piece)
        load_q(1)
        load_q(2)
        load_mask(0)
        load_mask(1)
        load_q(3)
        nc.sync.dma_start(out=v_raw[:].rearrange("p h r e -> p h (r e)"), in_=v.rearrange("h (s r) e -> s h (r e)", r=PACK))
        load_mask(2)
        for h in range(H):
            nc.sync.dma_start(out=og_sb[h][:], in_=og.rearrange("h (n p) e -> h p n e", p=QT)[h])
        nc.sync.dma_start(out=gn_sb[:], in_=gn)

        nc.scalar.activation(out=table_probe[:], in_=q_raw[0][:, 0, 0:1], func=ACT.Sigmoid)

        for first in range(0, QT, QT // Q_PIECES):
            round_q(nc.vector, 0, first, first + QT // Q_PIECES)
        nc.vector.tensor_copy(out=t_dealt[:].rearrange("p (r b) -> p r b", r=PACK),
                              in_=t_rows[:].rearrange("p (b r) -> p r b", r=PACK))
        quantize_q(0)
        nc.vector.transpose(out=t_turned[:], in_=t_dealt[:])
        for first in range(0, WINDOW, WINDOW // K_PIECES):
            round_k(nc.vector, 0, slice(0, 1), slice(first, first + WINDOW // K_PIECES))
        for piece in range(len(K_LOADS)):
            round_k(nc.scalar, piece, slice(1, 2))
        quantize_k(0, range(0, 2))
        round_k(nc.vector, 1, slice(0, 1))
        quantize_k(0, range(2, PACK))
        round_k(nc.vector, 2, slice(0, 1))
        quantize_k(1)
        scores(0, 0, FIRST_LEAD)

        round_q(nc.scalar, 1, 0, Q1_ON_SCALAR)
        round_q(nc.vector, 1, Q1_ON_SCALAR, QT)
        round_q(nc.scalar, 2, 0, Q2_ON_SCALAR)
        round_q(nc.vector, 2, Q2_ON_SCALAR, QT)
        quantize_q(1)
        tanh(0, 0, 0, 2)
        scores(1, 1, LEAD)
        tanh(0, 0, 2, PACK)
        tanh(0, 1)
        scale_mask(nc.scalar, 1, range(PACK - 1, PACK))
        scale_mask(nc.vector, 0)
        quantize_q(2)
        scale_mask(nc.vector, 1, range(PACK - 1))
        for h in range(H):
            weigh(0, h, h + 1)
        round_q(nc.vector, 3)
        quantize_w(0, H)
        quantize_q(3)
        scores(2, 0, LEAD)
        for h in reversed(range(H)):
            tanh(1, h)
        scores(LAST, 0, PACK)
        weigh(1)

        tanh(2, 0)
        round_v(nc.scalar, 0, V_ON_SCALAR)
        tanh(2, 1)
        for h in range(H):
            tanh(LAST, h)
        round_v(nc.vector, V_ON_SCALAR, E)
        scale_mask(nc.vector, 2)
        quantize(v_codes[:], v_scales[:], v_bf[:].rearrange("p h c -> p (h c)"))
        quantize_w(H, 2 * H)
        weigh(2)
        values(0, 2 * H)

        for h in range(H):
            nc.scalar.activation(out=sigmoid[:, h::H, :], in_=og_sb[h][:], func=ACT.Sigmoid)
        sum_squares(0, EARLY)
        inverse_rms(0, EARLY)

        weigh(LAST, 0, 1)
        quantize_w(2 * H, LAST * H)
        values(2 * H, LAST * H)
        weigh(LAST, 1, H)
        quantize_w(UNITS - 2, UNITS - 1)
        gate_gain(nc.vector, 0, 1)
        quantize_w(UNITS - 1, UNITS)
        gate_gain(nc.gpsimd, GATES_ON_VECTOR, UNITS - 1)
        gate_gain(nc.gpsimd, UNITS - 1, UNITS)
        gate_gain(nc.vector, 1, H)
        gate_gain(nc.vector, H, GATES_ON_VECTOR)
        values(LAST * H, UNITS)

        sum_squares(EARLY, LAST * H)
        inverse_rms(EARLY, 2 * H)
        sum_squares(UNITS - 2, UNITS - 1)
        inverse_rms(2 * H, LAST * H)
        sum_squares(UNITS - 1, UNITS)
        for u in range(LAST * H, UNITS):
            inverse_rms(u, u + 1)
        for u in range(UNITS):
            finish(u)
